import numpy as np, ml_dtypes
CORES = [6,15,38,47]
N = 4
BF = ml_dtypes.bfloat16
V, M, S, CAP, P, RO, STEP, LN = 2048, 4096, 256, 64, 8, 3, 650, 2
W1 = 13 * np.arange(16) + 5; W2 = 255 - 14 * np.arange(16); A = N * CAP
def mix(d):
    u = np.add.reduce(W1[:, None] * d, axis=2) & 4095; w = np.add.reduce(W2[:, None] * d, axis=2) & 4095
    return u, (u * w) >> 5
def kid(d, c, hm, t):
    R, n = d.shape[0], d.shape[3]
    hv = np.take_along_axis(hm, d.reshape(R, 8, 1, 16 * n), 3).reshape(R, 8, 16, 16, n)
    e = np.add.reduce(np.minimum(hv, np.abs(c)[:, :, :, None]), axis=2)
    k = np.argmax(e, axis=2); u, h = mix(d); v = (h + 37 * np.max(e, axis=2) + t) & 4095
    void = np.any(d == v[:, :, None], axis=2) | (v >= M)
    new = np.where(np.arange(16)[:, None] == k[:, :, None], v[:, :, None], d)
    q = np.add.reduce((new < v[:, :, None]).astype(np.int64), axis=2)
    return ~void, np.sort(new, axis=2), np.where((((q - k) & 1) == 1)[:, :, None], -(c >> 2), c >> 2)
def spawn(D, C, hm, t):
    start = STEP * (t + 1); a = np.roll(np.any(C != 0, axis=2), -start, axis=2)
    o = np.argsort(~a, axis=2, kind="stable")[:, :, :S]; on = np.take_along_axis(a, o, 2); pl = (o + start) & (V - 1)
    good, ch, c = kid(np.take_along_axis(D, pl[:, :, None], 3), np.take_along_axis(C, pl[:, :, None], 3), hm, t)
    return pl, on, on & good, ch, c
def recs(rng, shape):
    return np.sort(rng.integers(0, M - 15, shape), axis=-2) + np.arange(16)[:, None]
def base(rng, share=None):
    lim = rng.choice(np.array([1, 3, 20, 127]), (N, 8, 1, V), p=[0.15, 0.15, 0.2, 0.5]); C = rng.integers(-lim, lim + 1, (N, 8, 16, V))
    if share is None: share = rng.choice(np.array([0.4, 0.55, 0.75, 0.92]), (N, 8, 1, 1))
    C = C * (rng.random((N, 8, 1, V)) < share)
    return recs(rng, (N, 8, 16, V)), C, rng.integers(0, 128, (N, 8, 16, M))
def plant(rng, D, C, hm, part, twin=False, t=0, own=False):
    live = np.any(C != 0, axis=2); pl, on, good, ch, c = spawn(D, C, hm, t); u, h = mix(ch)
    busy = np.zeros((N, 8, V), bool); np.put_along_axis(busy, pl, on, 2)
    q, g, s = np.nonzero(good & (rng.random(good.shape) < part)); r = h[q, g, s] & (N - 1)
    p = ((h[q, g, s] >> LN) + rng.integers(0, P, q.size) * (2 * u[q, g, s] + 1)) & (V - 1)
    one = np.unique((r * 8 + g) * V + p, return_index=True)[1]
    if not own: one = one[~busy[r[one], g[one], p[one]]]
    q, g, s, r, p = q[one], g[one], s[one], r[one], p[one]
    rec = ch[q, g, :, s]; w = c[q, g, :, s]; lv = live[r, g, p][:, None]; bs = busy[r, g, p][:, None]; n = one.size
    if twin:
        nxt = np.concatenate([rec[:, 1:], np.full((n, 1), M)], axis=1); way = rng.random(n)
        fit = (rec[:, :14] + 1 < rec[:, 1:15] - 2) & (rec[:, 2:] + 1 < nxt[:, 2:]); i = np.argmax(fit * (0.01 + rng.random(fit.shape)), axis=1)
        z = np.nonzero(np.any(fit, axis=1) & (way < 0.4))[0]
        rec[z, i[z]] += 1; rec[z, i[z] + 1] -= 2; rec[z, i[z] + 2] += 1
        i = np.where(rng.random(n) < 0.3, 15, rng.integers(0, 16, n))
        z = np.nonzero((way > 0.6) & (rec[np.arange(n), i] + 1 < nxt[np.arange(n), i]))[0]
        rec[z, i[z]] += 1
    D[r, g, :, p] = rec
    mode = rng.integers(0, 4, (n, 1)); old = C[r, g, :, p]; some = np.any(w != 0, axis=1)[:, None]
    new = np.where(lv & (mode == 0) & some, -w, np.where(lv & (mode == 1), np.where(w < 0, -127, 127), old))
    C[r, g, :, p] = np.where(bs & (mode == 3), rng.choice(np.array([-1, 1]), (n, 16)), new)
def pack(D, C, hm):
    return {"det": np.ascontiguousarray((256 * D + C + 128).reshape(N, 128, V)).astype(np.int32), "ham": np.ascontiguousarray(hm.reshape(N, 128, M)).astype(np.float32).astype(BF)}
def setup_inputs(rng):
    D, C, hm = base(rng)
    for t in range(RO - 1, -1, -1): plant(rng, D, C, hm, 0.35, False, t, True)
    return pack(D, C, hm)
def setup_inputs_slots(rng):
    D, C, hm = base(rng, 2.0); C[:, :, 0] = np.where(np.any(C != 0, axis=2), C[:, :, 0], 1)
    for q in range(N):
        good, ch, c = kid(D[q:q + 1], C[q:q + 1], hm[q:q + 1], 0); mine = good[0] & ((mix(ch)[1][0] & (N - 1)) == ((q + 1) & (N - 1)))
        for g in range(8):
            hit = rng.permutation(np.nonzero(mine[g])[0]); rest = rng.permutation(np.nonzero(~mine[g])[0])
            n = min((CAP, CAP + 1, CAP - 1, S, 0, 1, CAP, CAP + 1)[g], len(hit))
            seq = np.concatenate([rng.permutation(np.concatenate([hit[:n], rest[:S - n]])), rng.permutation(np.concatenate([hit[n:], rest[S - n:]]))])
            k = int(rng.integers(S, V - 63)); o = rng.permutation(V); at = (np.concatenate([np.sort(o[:k]), o[k:]]) + STEP) & (V - 1)
            d2 = np.zeros_like(D[q, g]); c2 = np.zeros_like(C[q, g])
            d2[:, at] = D[q, g][:, seq]; c2[:, at[:k]] = C[q, g][:, seq[:k]]; D[q, g] = d2; C[q, g] = c2
    return pack(D, C, hm)
def setup_inputs_ties(rng):
    D, C, hm = base(rng); ev = np.ascontiguousarray(D[:, ::2]); u, h = mix(ev)
    x = np.take_along_axis(ev, rng.integers(0, 16, (N, 4, 1, V)), 2); y = np.take_along_axis(ev, rng.integers(0, 16, (N, 4, 1, V)), 2)
    goal = rng.permuted(np.concatenate([x, x + 1, x - 1, y, y + 1, ev[:, :, :1], ev[:, :, 15:], 0 * x, 0 * x + M - 1, 0 * x + 4095], axis=2), axis=2)
    e = ((goal - h[:, :, None]) * pow(37, -1, 4096)) & 4095; ok = (e >= 1) & (e <= 2032)
    e = np.take_along_axis(e, np.argmax(ok, axis=2)[:, :, None], 2); ok = np.any(ok, axis=2)[:, :, None]
    z = (np.arange(16)[:, None] + rng.integers(0, 16, (N, 4, 1, V))) & 15
    new = ((e >> 4) + (z < (e & 15))) * rng.choice(np.array([-1, 1]), (N, 4, 16, V)); live = np.any(C[:, ::2] != 0, axis=2)[:, :, None]
    C[:, ::2] = np.where(ok & live, new, C[:, ::2])
    hm[:, ::2] = 127; hm[:, 1::2] = rng.choice(np.array([0, 9, 60]), (N, 4, 1, M))
    hm[np.arange(N), 2 * rng.integers(0, 4, N) + 1] = 0
    plant(rng, D, C, hm, 0.2)
    return pack(D, C, hm)
def setup_inputs_twins(rng):
    D, C, hm = base(rng); hm = np.repeat(hm[:1], N, axis=0); ix = rng.integers(0, 40, (N, 8, 1, V))
    pd = np.repeat(recs(rng, (1, 8, 16, 40)), N, axis=0)
    pc = np.repeat(np.where(np.arange(40) < 12, rng.integers(0, 4, (1, 8, 16, 40)), rng.integers(4, 128, (1, 8, 16, 40))), N, axis=0)
    use = rng.random((N, 8, 1, V)) < 0.6; live = np.any(C != 0, axis=2)[:, :, None]
    sign = np.where(rng.random((N, 8, 1, V)) < 0.4, 1, rng.choice(np.array([-1, 1]), (N, 8, 16, V)))
    D = np.where(use, np.take_along_axis(pd, ix, 3), D)
    C = np.where(use & live, np.take_along_axis(pc, ix, 3) * sign, C)
    plant(rng, D, C, hm, 0.5); plant(rng, D, C, hm, 0.4); plant(rng, D, C, hm, 0.4, True)
    return pack(D, C, hm)
def setup_inputs_thin(rng):
    D, C, hm = base(rng, 2.0); lone = np.arange(16)[:, None] == rng.integers(0, 16, (N, 8, 1, V))
    C[:, 1::2] = np.where(lone, np.where(C == 0, -1, C), 0)[:, 1::2]
    C[:, :, 0] = np.where(np.any(C != 0, axis=2), C[:, :, 0], 1); sizes = np.array([0, 1, 5, S - 1, S, S + 1, V - 1, V])
    for q in range(N):
        for g in range(8):
            n = int(sizes[g]) if q == 0 else int(rng.choice(sizes)); o = rng.permutation(V)
            if n == 5: o = np.array([0, V - 1, STEP - 1, STEP, STEP + 1])
            keep = np.zeros(V, np.int64); keep[o[:n]] = 1; C[q, g] = C[q, g] * keep
    plant(rng, D, C, hm, 0.3)
    return pack(D, C, hm)
def setup_inputs_spread(rng):
    D, C, hm = base(rng)
    D = np.sort(((M - 15) * rng.random((N, 8, 16, V)) ** rng.choice(np.array([1.0, 4.0]), (N, 8, 1, V))).astype(np.int64), axis=2) + np.arange(16)[:, None]
    size = np.exp2(7 * rng.random((N, 8, 1, V))); live = np.any(C != 0, axis=2)[:, :, None]
    C = np.minimum((size * rng.random((N, 8, 16, V))).astype(np.int64), 127) * rng.choice(np.array([-1, 1]), (N, 8, 16, V)) * live
    hm = np.minimum((np.exp2(7 * rng.random((N, 8, 1, M))) * rng.random((N, 8, 16, M))).astype(np.int64), 127)
    plant(rng, D, C, hm, 0.3)
    return pack(D, C, hm)
def check_inputs(d):
    bad = []
    x = d["det"].astype(np.int64).reshape(N, 8, 16, V); o = x >> 8
    if np.min(o) < 0 or np.max(o) > M - 1: bad.append("orbitals of det")
    if np.min(x & 255) < 1: bad.append("counts of det")
    if not np.all(o[:, :, 1:] > o[:, :, :-1]): bad.append("rising orbitals of det")
    h = d["ham"].astype(np.float32)
    if not np.all((h >= 0) & (h <= 127) & (h == np.floor(h))): bad.append("numbers of ham")
    return bad
def reference(det, ham):
    x = det.astype(np.int64).reshape(N, 8, 16, V); D = x >> 8; C = (x & 255) - 128
    hm = ham.astype(np.float32).astype(np.int64).reshape(N, 8, 16, M); num = np.arange(P)[:, None]
    for t in range(RO):
        pl, on, good, ch, c = spawn(D, C, hm, t)
        sel = np.zeros((N, 8, V), bool); np.put_along_axis(sel, pl, on, 2)
        C = C - np.sign(C) * sel[:, :, None]
        f = good[:, :, None] & ((mix(ch)[1] & (N - 1))[:, :, None] == np.arange(N)[:, None])
        before = np.add.accumulate(f.astype(np.int64), axis=3) - f.astype(np.int64)
        q, g, r, s = np.nonzero(f & (before < CAP)); a = q * CAP + before[q, g, r, s]
        ad = np.zeros((N, 8, 16, A), np.int64); ac = np.zeros((N, 8, 16, A), np.int64); there = np.zeros((N, 8, A), bool)
        ad[r, g, :, a] = ch[q, g, :, s]; ac[r, g, :, a] = c[q, g, :, s]; there[r, g, a] = True
        u, h = mix(ad)
        p = ((h >> LN)[:, :, None] + num * (2 * u + 1)[:, :, None]) & (V - 1)
        live = np.any(C != 0, axis=2); lp = np.take_along_axis(live, p.reshape(N, 8, P * A), 2).reshape(N, 8, P, A)
        dp = np.take_along_axis(D, p.reshape(N, 8, 1, P * A), 3).reshape(N, 8, 16, P, A)
        same = np.all(dp == ad[:, :, :, None], axis=2) & lp
        score = np.where(same, num, np.where(lp, 2 * P, P + num))
        ok = there & (np.min(score, axis=2) < 2 * P); place = np.take_along_axis(p, np.argmin(score, axis=2)[:, :, None], 2)[:, :, 0]
        r, g, a = np.nonzero(ok); low = np.full((N, 8, V), A); np.minimum.at(low, (r, g, place[r, g, a]), a)
        r, g, a = np.nonzero(ok & (np.take_along_axis(low, place, 2) == np.arange(A))); b = place[r, g, a]
        D[r, g, :, b] = ad[r, g, :, a]; C[r, g, :, b] = np.clip(C[r, g, :, b] + ac[r, g, :, a], -127, 127)
    return {"y": (256 * D + C + 128).reshape(N, 128, V).astype(np.float32)}

@@ -1,0 +1,583 @@
+from concourse.bass import DstId, RemoteDMATransfer
+from concourse.mybir import AluOpType as O, ActivationFunctionType as F
+
+RO, STEP, N, CAP = 3, 650, 4, 64
+CH = ((0, 64), (64, 128), (128, 192), (192, 224))
+TW = 2576
+DUMMY, DUMP = 2064, 2320
+K = 1 << 22
+F32, B16, H16, I32, U16 = "float32", "bfloat16", "float16", "int32", "uint16"
+
+WIDE = {
+    "detb": (2048, I32), "big": (2048, I32), "tab": (TW, F32), "cab": (TW, B16), "hamb": (4096, B16), "ones": (2048, B16),
+    "em": (2048, B16), "ep": (2048, B16), "e1": (2048, B16), "e2": (2048, B16), "bc": (2048, B16), "rexp": (2048, B16),
+    "lb0": (1024, B16), "lb1": (1024, B16), "lb2": (1024, B16), "rvk": (512, B16), "cmp": (2048, B16), "lg": (4096, B16),
+    "mn": (4096, B16), "sb0": (1280, I32), "sb1": (1280, I32), "sb2": (1280, I32), "ar0": (256, I32), "ar1": (256, I32),
+    "ar2": (256, I32), "df": (2048, F32), "ab": (2048, F32), "rl": (2048, B16), "eq": (4096, B16),
+}
+SMALL = {
+    F32: "pcol 1 cols 16 rr0 128 rr1 128 rr2 128 cw0 8 cw1 8 cw2 8 kscan 256 m64 64 sel15 128 iow 16 iow1 16 iow4 16 xio 16 tm 16 "
+         "kr 256 mc 128 dumpc 16 cneg 8 totu 1 bad4 16 cc 256 sgc 256 ff 256 km 256 ma 256 mb 256 lo 256 t1 256 tt 256 own2 16 "
+         "inc 64 rk 64 chp 256 pk 256 fs 256 fg 256 ft 256 aa 256 aam 256 st1 16 st2 32 st4 64 mz 128 k1 128 k2 128 k3 128 k4 64 "
+         "k5 32 inv 16 keyw 16 cs 256 cn 256 tg 256 tn 256 es 256 ls 16 ls2 16 fo 16",
+    B16: "blk 128 blk592 8 idb 128 shu 128 shd 128 cor 128 tmpb 128 mid 128 gum 128 gdm 128 ns0 128 ns1 128 ns2 128 ni0 128 "
+         "ni1 128 ni2 128 t10 128 t11 128 t12 128 t20 128 t21 128 t22 128 r00 256 r01 256 r02 256 negb 256 io0 256 io1 256 "
+         "a1 128 m128 128 trb 128 orow 64 zb 256 w12 16 live 128 w 128 wz 128 val 256 abc 256 ct 256 sd 256 st_ 256 oh 64 fa 256 "
+         "ent 256 dm 256 lsb 256",
+    H16: "nx 16 nt 16 d16 256 vk16 32 t32 128 ch16 256 mk 64 bo 16 a16 256 key16 16 kb16 256",
+    I32: "icol 1 icol2 1 ti 256 ci 256 fi 256 ui 32 ui2 32 pi 16 h16 16 h16t 16 si 16 vk 32 vo 16 vo2 16 own 16 npi 256 "
+         "npa 256 ai 256 ac 256 z 128 zi2 128 kmi 16 plc 16 oi 256 oc 256",
+    U16: "pl 16 du 256 sl 16 zu 128 plu 16 fou 16",
+}
+
+
+def _layout():
+    scratch, place = {}, {}
+    for i in range(8):
+        scratch["p%d" % i] = ("psum", [128, 512], F32)
+        place["p%d" % i] = ("p%d" % i, 0, 512)
+    for name in WIDE:
+        scratch[name] = ("sbuf", [128, WIDE[name][0]], WIDE[name][1])
+        place[name] = (name, 0, WIDE[name][0])
+    for dtype in SMALL:
+        words = SMALL[dtype].split()
+        at = 0
+        for j in range(0, len(words), 2):
+            w = int(words[j + 1])
+            place[words[j]] = ("w_" + dtype, at, w)
+            at += (w + 15) // 16 * 16
+        scratch["w_" + dtype] = ("sbuf", [128, at], dtype)
+    return scratch, place
+
+
+SCRATCH, PLACE = _layout()
+SEMAPHORES = ["sv", "ss", "st", "sg", "sent", "ldh"] + ["ld%d" % i for i in range(4)] + ["out%d" % i for i in range(4)] + ["arr%d" % i for i in range(RO)]
+SEMOF = {"v": "sv", "s": "ss", "t": "st", "g": "sg"}
+
+
+def plan(topo, cores, rank):
+    a = topo.chip(cores[rank])
+
+    def far(o):
+        b = topo.chip(cores[o])
+        return 0 if topo.mates(a, b) or topo.same_plane(a, b) else 1
+    out, used = [], 0
+    others = sorted([o for o in range(N) if o != rank], key=far)
+    for o in others:
+        n = 4 if o == others[-1] else 2
+        out.append((o, topo.engines(cores[rank], cores[o])[used:used + n]))
+        used += n
+    return out
+
+
+def rank_program(g, core, T, topo):
+    rank = T.rank_of(core)
+    if rank is None:
+        return
+    queues = {"v": g.vector, "s": g.scalar, "t": g.tensor, "g": g, "y": g.sync}
+    count = {"v": 0, "s": 0, "t": 0, "g": 0}
+    known = {q: {} for q in queues}
+    clock, hist, srcq = {}, {}, {}
+
+    def A(name, c0=0, c1=None, step=1, p0=0, p1=128):
+        buf, base, w = PLACE[name]
+        lo, hi = base + c0, base + (w if c1 is None else c1)
+        t = T[buf]
+        ap = t[p0:p1, lo:hi] if step == 1 else t[p0:p1, lo:hi:step]
+        return (ap, buf, lo, hi)
+
+    def P(b, c0, c1, step=1, p0=0, p1=128):
+        return A("p%d" % b, c0, c1, step, p0, p1)
+
+    def ind(win, off):
+        return (win[0].indirect(off[0]), win, off)
+
+    def flat(x):
+        return [x[1], x[2]] if len(x) == 3 else [x]
+
+    def ispsum(buf):
+        return buf[0] == "p" and buf[1:].isdigit()
+
+    def need(q, outs, ins, extra=()):
+        want = dict(extra)
+        acc = [(a, "w") for o in outs for a in flat(o)] + [(a, "r") for i in ins for a in flat(i)]
+        for (_, buf, lo, hi), kind in acc:
+            ps = ispsum(buf)
+            for (sq, idx, k2, l2, h2) in hist.get(buf, ()):
+                if sq == q == "t":
+                    continue
+                if (ps and sq != q) or ((kind == "w" or k2 == "w") and lo < h2 and l2 < hi):
+                    want[sq] = max(want.get(sq, 0), idx)
+        for s in sorted(want):
+            if known[q].get(s, 0) < want[s]:
+                queues[q].wait_ge(T.sem[SEMOF.get(s, s)], want[s])
+                known[q][s] = want[s]
+                for k, v in clock.get((s, want[s]), {}).items():
+                    known[q][k] = max(known[q].get(k, 0), v)
+        return acc
+
+    def note(q, idx, acc):
+        clock[(q, idx)] = dict(known[srcq.get(q, q)])
+        for (_, buf, lo, hi), kind in acc:
+            old = hist.get(buf, [])
+            if ispsum(buf):
+                keep = [e for e in old if e[0] == q and q != "t" and not (kind == "w" and lo <= e[3] and e[4] <= hi)]
+            else:
+                keep = [e for e in old if not (lo <= e[3] and e[4] <= hi and (kind == "w" or (e[2] == "r" and e[0] == q)))]
+            hist[buf] = keep + [(q, idx, kind, lo, hi)]
+
+    def emit(q, outs, ins, call, extra=()):
+        acc = need(q, outs, ins, extra)
+        r = call()
+        count[q] += 1
+        r.then_inc(T.sem[SEMOF[q]], 1)
+        note(q, count[q], acc)
+
+    def load(q, sem, out, src):
+        acc = need(q, [out], [])
+        queues[q].dma_start(out[0], src).then_inc(T.sem[sem], 16)
+        srcq[sem] = q
+        note(sem, 16, acc)
+
+    def store(q, sem, dst, i):
+        acc = need(q, [], [i])
+        queues[q].dma_start(dst, i[0]).then_inc(T.sem[sem], 16)
+        srcq[sem] = q
+        note(sem, 16, acc)
+
+    def mm(out, l, r, start=True, stop=True):
+        emit("t", [out], [l, r], lambda: g.tensor.matmul(out[0], l[0], r[0], start, stop))
+
+    def cp(out, i):
+        emit("v", [out], [i], lambda: g.vector.tensor_copy(out[0], i[0]))
+
+    def tt(out, a, b, op):
+        emit("v", [out], [a, b], lambda: g.vector.tensor_tensor(out[0], a[0], b[0], op))
+
+    def ts(out, i, s1, op0, s2=None, op1=None, extra=()):
+        ins = [i] + [s for s in (s1, s2) if isinstance(s, tuple)]
+        x1 = s1[0] if isinstance(s1, tuple) else s1
+        x2 = s2[0] if isinstance(s2, tuple) else s2
+        if op1 is None:
+            emit("v", [out], ins, lambda: g.vector.tensor_scalar(out[0], i[0], x1, None, op0), extra)
+        else:
+            emit("v", [out], ins, lambda: g.vector.tensor_scalar(out[0], i[0], x1, x2, op0, op1), extra)
+
+    def scan(out, a, b, op0, op1):
+        emit("v", [out], [a, b], lambda: g.vector.tensor_tensor_scan(out[0], a[0], b[0], 0.0, op0, op1))
+
+    def fill(out, c):
+        emit("v", [out], [], lambda: g.vector.memset(out[0], c))
+
+    def act(out, i, func, bias=0.0, scale=1.0):
+        ins = [i] + [s for s in (bias, scale) if isinstance(s, tuple)]
+        b = bias[0] if isinstance(bias, tuple) else bias
+        c = scale[0] if isinstance(scale, tuple) else scale
+        if func == F.Copy:
+            emit("s", [out], ins, lambda: g.scalar.activation(out[0], i[0], func))
+        else:
+            emit("s", [out], ins, lambda: g.scalar.activation(out[0], i[0], func, bias=b, scale=c))
+
+    def iota(out, pat, base, cm):
+        emit("g", [out], [], lambda: g.iota(out[0], pat, base, cm, allow_small_or_imprecise_dtypes=True))
+
+    def sel(out, i, pat, op, fillv, base, cm):
+        emit("g", [out], [i], lambda: g.affine_select(out[0], i[0], pat, op, fillv, base, cm))
+
+    one = lambda w: A("ones", 0, w)
+    col = lambda j: A("cols", j, j + 1)
+
+    for c in range(4):
+        load("y", "ld%d" % c, A("detb", 512 * c, 512 * c + 512), T.det[:, 512 * c:512 * c + 512])
+    load("s", "ldh", A("hamb"), T.ham[:, :])
+
+    fill(A("ones", 0, 256), 1.0)
+    fill(A("em"), 0.0)
+    iota(A("icol"), [[0, 1]], 0, 1)
+    sel(A("tmpb"), one(128), [[-16, 8], [0, 16]], O.is_ge, 0.0, 0, 1)
+    sel(A("blk"), A("tmpb"), [[16, 8], [0, 16]], O.is_ge, 0.0, 15, -1)
+    ts(A("icol2"), A("icol"), 15, O.bitwise_and)
+    cp(A("pcol"), A("icol"))
+    cp(col(0), A("icol2"))
+    ts(col(1), col(0), 15.0, O.is_equal)
+    ts(col(2), col(1), 15.0, O.mult, 1.0, O.add)
+    ts(col(3), col(1), -1000.0, O.mult)
+    ts(col(4), col(1), 999.0, O.mult, 1.0, O.add)
+    ts(col(5), col(0), 13.0, O.mult, 5.0, O.add)
+    ts(col(6), col(0), -14.0, O.mult, 255.0, O.add)
+    fill(A("negb"), -1.0)
+    ts(col(7), col(0), -1.0, O.mult, -2033.0, O.add)
+    ts(col(8), col(7), 8192.0, O.mult, 8192.0, O.add)
+    ts(col(9), col(1), -8192.0, O.mult)
+    ts(col(10), col(0), 0.0, O.is_equal, 8192.0, O.mult)
+    for r in range(16):
+        act(A("em", 128 * r + r, 128 * r + 128, 16), A("blk", 0, 128, 16), F.Copy)
+    act(A("ep"), A("em"), F.Identity, scale=col(2))
+    sel(A("idb"), one(128), [[-1, 128]], O.is_equal, 0.0, 0, 1)
+    sel(A("shu"), one(128), [[-1, 128]], O.is_equal, 0.0, -1, 1)
+    sel(A("cor"), one(128), [[-1, 128]], O.is_equal, 0.0, 127, 1)
+    sel(A("m128"), one(128), [[0, 8], [1, 16]], O.not_equal, 0.0, 0, 0)
+    sel(A("a1"), one(128), [[0, 8], [1, 16]], O.not_equal, 0.0, -15, 0)
+    iota(A("io0"), [[1, 256]], 0, 0)
+    iota(A("io1"), [[1, 256]], 1, 0)
+    for c in range(4):
+        s = 512 * c
+        ts(A("big", s, s + 512), A("detb", s, s + 512), 255, O.bitwise_and)
+        ts(A("df", s, s + 512), A("big", s, s + 512), 128.0, O.subtract)
+        act(A("cab", s, s + 512), A("df", s, s + 512), F.Abs)
+        if c == 0:
+            tt(A("tmpb"), A("idb"), A("shu"), O.subtract)
+            tt(A("tmpb"), A("tmpb"), A("cor"), O.subtract)
+            ts(A("mid"), A("idb"), -1.0, O.mult)
+    act(A("cab", 2048, 2064), A("cab", 0, 16), F.Copy)
+    act(A("e1"), A("em"), F.Identity, scale=col(5))
+    act(A("e2"), A("em"), F.Identity, scale=col(6))
+
+    def chunk(t):
+        m0 = STEP * (t + 1) // 16
+        return m0, m0 - 1
+
+    def round_g(t):
+        m0, ml = chunk(t)
+        rr = "rr%d" % t
+        iota(A(rr, 0, ml), [[1, ml]], 128, 0)
+        iota(A(rr, m0, 128), [[1, 128 - m0]], m0, 0)
+        iota(A(rr, ml, m0), [[0, 1]], 126, 0)
+        sel(A("cw%d" % t), one(8), [[0, 8]], O.not_equal, -128.0, -ml, 1)
+        sel(A("t2%d" % t), one(128), [[200, 128]], O.is_equal, 0.0, -127 - 200 * ml, 1)
+        sel(A("ns%d" % t), A("tmpb"), [[1, 128]], O.not_equal, 0.0, -ml, 0)
+        sel(A("ni%d" % t), A("mid"), [[1, 128]], O.not_equal, 0.0, -ml, 0)
+        sel(A("r0%d" % t), A("negb"), [[0, 256]], O.is_equal, 0.0, -m0, 1)
+        if t:
+            iota(A("lb%d" % t), [[0, 1024]], 0, 0)
+
+    def round_v(t):
+        m0, ml = chunk(t)
+        ts(col(11), A("pcol"), float(m0), O.is_lt, 128.0, O.mult)
+        tt(col(12), col(11), A("pcol"), O.add)
+        ts(A("t1%d" % t), A("rr%d" % t), col(12), O.is_ge)
+        if t == 0:
+            fill(A("lb%d" % t), 0.0)
+        cp(A("lb%d" % t, 15, 1024, 144), A("cw%d" % t))
+
+    round_g(0)
+    iota(A("iow"), [[16, 16]], 0, 0)
+    round_v(0)
+    fill(A("ones", 256, 2048), 1.0)
+
+    def rest_g():
+        sel(A("rexp"), one(2048), [[-1, 128], [0, 16]], O.is_equal, 0.0, 0, 1)
+        sel(A("shd"), one(128), [[-1, 128]], O.is_equal, 0.0, 1, 1)
+        sel(A("trb"), A("blk"), [[-1, 128]], O.is_ge, 0.0, 0, 1)
+        sel(A("kscan"), one(256), [[0, 16], [1, 16]], O.not_equal, -4.0e6, 0, 0)
+        sel(A("rvk"), one(512), [[-8, 4], [-1, 8], [0, 16]], O.is_equal, 0.0, 0, 1)
+        iota(A("orow"), [[256, 4], [0, 16]], 0, 0)
+        sel(A("m64"), one(64), [[0, 4], [1, 16]], O.not_equal, 0.0, 0, 0)
+
+    def rest_v():
+        ts(A("blk592"), A("blk", 0, 128, 16), 592.0, O.mult)
+        ts(A("w12", 0, 8), A("blk", 0, 128, 16), col(5), O.mult)
+        ts(A("w12", 8, 16), A("blk", 0, 128, 16), col(6), O.mult)
+        fill(A("zb"), 0.0)
+        ts(A("iow4"), A("iow"), 0.25, O.mult, 256.0, O.add)
+        ts(A("dumpc"), A("iow"), float(DUMP), O.add)
+
+    def rest_v2():
+        tt(A("gum"), A("idb"), A("shu"), O.subtract)
+        tt(A("gdm"), A("idb"), A("shd"), O.subtract)
+        tt(A("gum"), A("gum"), A("a1"), O.mult)
+        tt(A("gdm"), A("gdm"), A("m128"), O.mult)
+
+    def whash(src):
+        for e in range(2):
+            for r in range(16):
+                mm(P(6, 16 * e, 16 * e + 16), A("e%d" % (e + 1), 128 * r, 128 * r + 128), A(src, r, 256, 16), r == 0, r == 15)
+
+    def mix(steps=False):
+        cp(A("ui"), P(6, 0, 32))
+        ts(A("ui2"), A("ui"), 4095, O.bitwise_and)
+        if steps:
+            ts(A("st1"), A("ui2", 0, 16), 2.0, O.mult, 1.0, O.add)
+            for j in range(2):
+                act(A("st2", 16 * j, 16 * j + 16), A("st1"), F.Identity, scale=2.0)
+            for j in range(2):
+                act(A("st4", 32 * j, 32 * j + 32), A("st2"), F.Identity, scale=2.0)
+        tt(A("pi"), A("ui2", 0, 16), A("ui2", 16, 32), O.mult)
+
+    def wsum(out, weights, src, c0, c1, start=True):
+        for r in range(16):
+            mm(out, A(weights, 128 * r, 128 * r + 128), A(src, c0 + r, c1, 16), start and r == 0, r == 15)
+
+    for t in range(RO):
+        start = STEP * (t + 1)
+        m0, off = start // 16, start % 16
+        last = t == RO - 1
+        for u in range(16):
+            mm(P(0, u, 128, 16), A("cab", off + u, off + u + 2033, 16), A("blk", 0, 128, 16))
+        mm(P(3, 0, 256), A("a1", 0, 128, 1, 0, 1), A("io1", 0, 256, 1, 0, 1), True, False)
+        ts(A("live"), P(0, 0, 128), 0.5, O.is_gt)
+        scan(A("w"), A("m128"), A("live"), O.mult, O.add)
+        if t == 0:
+            ts(A("sel15"), A("blk"), col(1), O.mult)
+            ts(A("iow"), A("iow"), col(0), O.add)
+            ts(A("iow1"), A("iow"), 1.0, O.add)
+            for c in range(4):
+                ts(A("tab", 512 * c, 512 * c + 512), A("detb", 512 * c, 512 * c + 512), float(K), O.subtract)
+        mm(P(1, 0, 8), A("t1%d" % t), A("w", 15, 128, 16), True, False)
+        mm(P(1, 0, 8), A("t2%d" % t), A("w", 15 - off, 128, 16), False, True)
+        mm(P(5, 0, 1), A("w"), A("ones", 0, 1))
+        mm(P(2, 128, 136), A("ni%d" % t), A("w", 15, 128, 16))
+        mm(P(2, 0, 128), A("ns%d" % t), A("w"))
+        sel(A("wz"), A("w"), [[0, 8], [1, 16]], O.not_equal, 0.0, -15, 0)
+        if t == 0:
+            rest_g()
+        iota(A("sb%d" % t, 0, 1024), [[0, 1024]], K + 128, 0)
+        act(A("cneg"), P(2, 128, 136), F.Copy)
+        lb = "lb%d" % t
+        for h in range(8):
+            ts(A("cmp", 256 * h, 256 * h + 256), A("io0"), P(1, h, h + 1), O.is_ge)
+            act(A(lb, 144 * h, 144 * h + 15), P(2, 16 * h, 16 * h + 15), F.Identity, bias=A("cneg", h, h + 1))
+            if h == 3:
+                mm(P(3, 0, 256), A("wz"), A("r0%d" % t), False, False)
+            if h == 4:
+                act(A("totu"), P(5, 0, 1), F.Copy)
+                mm(P(5, 1, 2), A("sel15"), A("totu"))
+            mm(P(3, 0, 256), A(lb, 128 * h, 128 * h + 128), A("cmp", 256 * h, 256 * h + 256), False, h == 7)
+        ts(A("nx"), A("iow1"), P(5, 1, 2), O.subtract, 0.0, O.max)
+        ts(A("nt"), A("iow"), P(5, 1, 2), O.is_ge, float(DUMMY - start), O.mult)
+        mm(P(4, 0, 16), A("idb"), A("nx"), True, False)
+        mm(P(4, 0, 16), A("idb"), A("nt"), False, False)
+        ts(A("val"), P(3, 0, 256), col(3), O.max, col(4), O.min)
+        wsum(P(4, 0, 16), "ep", "val", 0, 256, False)
+        if t == 0:
+            rest_v()
+            act(A("tab", 2048, TW), A("ones", 0, TW - 2048), F.Identity, bias=128.0 - K, scale=0.0)
+            act(A("cab", 2064, TW), A("ones", 0, TW - 2064), F.Identity, scale=0.0)
+        ts(A("pl"), P(4, 0, 16), float(16 * m0 + off), O.add)
+        ts(A("du"), ind(A("tab"), A("pl")), 1.0 / 256, O.mult, K / 256 - 0.5, O.add)
+        act(A("abc"), ind(A("cab"), A("pl")), F.Copy)
+        for h in range(2):
+            mm(P(7, 128 * h, 128 * h + 128), A("abc", 128 * h, 128 * h + 128), A("idb"))
+        for a, b in CH:
+            act(A("lg", 16 * a, 16 * b), ind(A("hamb"), A("du", a, b)), F.Copy)
+        ts(A("d16"), A("du"), 2048.0, O.subtract)
+        cp(A("ct"), P(7, 0, 256))
+        if t == 0:
+            rest_v2()
+        for h in range(2):
+            for e in range(2):
+                mm(P(4, 16 * e + 8 * h, 16 * e + 8 * h + 8), A("d16", 128 * h, 128 * h + 128), A("w12", 8 * e, 8 * e + 8))
+
+        def rep(b):
+            mm(P(b % 4, 0, 512), A("ct", 128 * (b // 4), 128 * (b // 4) + 128), A("rexp", 512 * (b % 4), 512 * (b % 4) + 512))
+
+        for b in range(4):
+            rep(b)
+        mm(P(7, 0, 256), A("gum"), A("d16"))
+        mm(P(7, 256, 512), A("gdm"), A("d16"))
+        cp(A("ui"), P(4, 0, 32))
+        ts(A("ui2"), A("ui"), 4095, O.bitwise_and)
+        tt(A("pi"), A("ui2", 0, 16), A("ui2", 16, 32), O.mult)
+        ts(A("h16"), A("pi"), 1, O.arith_shift_right, 0x7FFFFFF0, O.bitwise_and)
+        ts(A("h16t"), A("h16"), float(16 * t), O.add)
+        cp(A("lg", 3584, 4096), ind(A("hamb"), A("du", 224, 256)))
+        for b in range(8):
+            s = 512 * b
+            tt(A("mn", s, s + 512), A("lg", s, s + 512), P(b % 4, 0, 512), O.min)
+            if b < 4:
+                rep(b + 4)
+            if b % 4 == 3:
+                h = b // 4
+                for k in range(16):
+                    mm(P(6, 128 * h + k, 128 * h + 128, 16), A("mn", 2048 * h + k, 2048 * h + 2048, 16), A("blk592"))
+        if t == 0:
+            ts(A("rvk", 0, 256), A("rvk", 0, 256), -1.0, O.mult)
+            ts(A("trb"), A("trb"), -1.0, O.mult)
+        cp(A("ti"), ind(A("tab"), A("pl")))
+        ts(A("fi"), A("ti"), 255, O.bitwise_and, 2, O.arith_shift_right)
+        ts(A("ff"), A("fi"), 32.0, O.subtract)
+        act(P(7, 0, 256), P(7, 0, 256), F.Identity, bias=col(9))
+        act(P(7, 256, 512), P(7, 256, 512), F.Identity, bias=col(10))
+        mm(P(5, 0, 256), A("idb"), A("d16"))
+        scan(A("km"), A("kscan"), P(6, 0, 256), O.add, O.max)
+        tt(A("si"), A("km", 15, 256, 16), A("h16t"), O.add)
+        ts(A("vk", 0, 16), A("si"), 4, O.arith_shift_right, 4095, O.bitwise_and)
+        ts(A("vk", 16, 32), A("si"), 15, O.bitwise_and)
+        ts(A("vk16"), A("vk"), 2048.0, O.subtract)
+        mm(P(4, 0, 128, 1, 0, 32), A("vk16"), A("idb"))
+        cp(A("t32", 0, 128, 1, 0, 32), P(4, 0, 128, 1, 0, 32))
+        for h in range(2):
+            s = 128 * h
+            mm(P(1, s, s + 128), A("rvk", 256 + s, 256 + s + 128, 1, 0, 32), A("t32", 0, 128, 1, 0, 32))
+        for h in range(2):
+            s = 128 * h
+            mm(P(0, s, s + 128), A("idb"), A("d16", s, s + 128), True, False)
+            mm(P(0, s, s + 128), A("rvk", s, s + 128, 1, 0, 32), A("t32", 0, 128, 1, 0, 32), False, True)
+        ts(A("ma"), P(1, 0, 256), col(7), O.is_ge)
+        act(A("sd"), P(0, 0, 256), F.Sign)
+        act(A("mb"), P(1, 0, 256), F.Relu, bias=col(8), scale=-8192.0)
+        wsum(P(3, 0, 16), "em", "sd", 0, 256)
+        tt(P(2, 0, 256), P(7, 0, 256), A("ma"), O.mult)
+        tt(A("lo"), P(7, 256, 512), A("mb"), O.min)
+        tt(A("t1"), A("lo"), P(0, 0, 256), O.min)
+        tt(A("tt"), A("t1"), P(2, 0, 256), O.max)
+        tt(A("ch16"), P(5, 0, 256), A("tt"), O.subtract)
+        act(A("st_"), A("tt"), F.Sign)
+        mm(P(5, 256, 512), A("blk"), A("st_"))
+        whash("ch16")
+        act(A("fa"), A("abc"), F.Relu, bias=-1.0)
+        mm(P(2, 0, 256), A("blk"), A("fa"))
+        act(A("fs"), P(2, 0, 256), F.Sign, bias=-0.5)
+        cp(A("vo"), P(3, 0, 16))
+        ts(A("vo2"), A("vo"), 1, O.bitwise_and)
+        tt(A("bad4"), A("vo2"), A("nt"), O.max)
+        ts(A("bad4"), A("bad4"), 0.0, O.is_gt, 4.0, O.mult)
+        tt(A("bo"), A("bad4"), A("iow4"), O.mult)
+        ts(A("chp"), A("ch16"), 256.0, O.mult, 2048.0 * 256 + 128, O.add)
+        cp(A("npi"), P(5, 256, 512))
+        ts(A("npa"), A("npi"), 1, O.bitwise_and)
+        ts(P(1, 0, 256), A("npa"), 2.0, O.mult, -1.0, O.add)
+        tt(P(1, 0, 256), P(1, 0, 256), A("ff"), O.mult)
+        tt(A("pk"), P(1, 0, 256), A("chp"), O.add)
+        mix()
+        ts(A("own"), A("pi"), 5, O.arith_shift_right, 3, O.bitwise_and)
+        tt(A("own2"), A("own"), A("bad4"), O.max)
+        for o in range(4):
+            ts(A("oh", 16 * o, 16 * o + 16), A("own2"), float(o), O.is_equal)
+        mm(P(7, 64, 128), A("blk"), A("oh"))
+        mm(P(4, 0, 64), A("ones", 0, 128, 1, 0, 1), A("orow", 0, 64, 1, 0, 1), True, False)
+        mm(P(4, 0, 64), A("trb"), A("oh"), False, True)
+        scan(A("inc"), A("m64"), P(7, 64, 128), O.mult, O.add)
+        tt(A("rk"), A("inc"), P(4, 0, 64), O.add)
+        tt(A("mk"), A("rk"), A("oh"), O.mult)
+        mm(P(3, 0, 16), A("idb"), A("bo"), True, False)
+        for o in range(4):
+            mm(P(3, 0, 16), A("idb"), A("mk", 16 * o, 16 * o + 16), False, o == 3)
+        cp(A("sl"), P(3, 0, 16))
+        sb, ar, arr = "sb%d" % t, "ar%d" % t, "arr%d" % t
+        cp(ind(A(sb), A("sl")), A("pk"))
+        trs = []
+        for o, es in plan(topo, T.cores, rank):
+            rid, pid = topo.addr(T.cores[o])[:2]
+            trs.append(RemoteDMATransfer(dst_ids=[DstId(rid=rid, pnc=pid)], dma_engine_mask=sum(1 << e for e in es), remote_sem=T.sem[arr],
+                                         src=A(sb, 256 * o, 256 * o + 64)[0], dst=A(ar, 64 * rank, 64 * rank + 64)[0]))
+        need("g", [], [A(sb)])
+        g.remote_dma_fused(trs, local_sem=T.sem.sent)
+        got = sum(len(es) for q in range(N) if q != rank for o, es in plan(topo, T.cores, q) if o == rank)
+        if t == 0:
+            sel(A("bc"), one(2048), [[-1, 16], [-16, 8], [0, 16]], O.is_equal, 0.0, 0, 1)
+            iota(A("mc"), [[2048, 8], [0, 16]], 0, 0)
+            iota(A("xio"), [[1, 16]], 0, 0)
+        if not last:
+            round_g(t + 1)
+        cp(A(ar, 64 * rank, 64 * rank + 64), A(sb, 256 * rank, 256 * rank + 64))
+        ts(A("ci"), A("ti"), 255, O.bitwise_and)
+        ts(A("cc"), A("ci"), 128.0, O.subtract)
+        act(A("sgc"), A("cc"), F.Sign)
+        if t == 0:
+            for c in range(4):
+                s = 512 * c
+                mm(P(c % 3, 0, 512), A("blk"), A("cab", s, s + 512))
+                act(P(c % 3, 0, 512), P(c % 3, 0, 512), F.Sign, bias=-0.5)
+                tt(A("tab", s, s + 512), A("tab", s, s + 512), P(c % 3, 0, 512), O.mult)
+        if not last:
+            cp(ind(A("cab"), A("pl")), A("fa"))
+        tt(A("fg"), A("ti"), A("sgc"), O.subtract)
+        tt(A("ft"), A("fg"), A("fs"), O.mult)
+        cp(ind(A("tab"), A("pl")), A("ft"))
+        if not last:
+            iota(A("tab", 2048, DUMP), [[0, DUMP - 2048]], 128 - K, 0)
+        ts(A("ai"), A(ar), 8, O.arith_shift_right, extra=[(arr, got)])
+        ts(A("a16"), A("ai"), 2048.0, O.subtract)
+        whash("a16")
+        ts(A("aa"), A("ai"), 256.0, O.mult, 128.0 - K, O.add)
+        ts(A("aam"), A("aa"), 256.0, O.subtract)
+        ts(A("ac"), A(ar), 255, O.bitwise_and)
+        mix(True)
+        ts(A("z", 0, 16), A("pi"), 7, O.arith_shift_right, 2047, O.bitwise_and)
+        tt(A("z", 16, 32), A("z", 0, 16), A("st1"), O.add)
+        ts(A("zi2", 0, 32), A("z", 0, 32), 2047, O.bitwise_and)
+        cp(A("zu", 0, 32), A("zi2", 0, 32))
+        late = []
+        for m in range(8):
+            s = 256 * m
+            tt(A("df", s, s + 256), ind(A("tab"), A("zu", 16 * m, 16 * m + 16)), A("aa"), O.subtract)
+            if m == 0:
+                tt(A("z", 32, 64), A("z", 0, 32), A("st2"), O.add)
+                tt(A("z", 64, 128), A("z", 0, 64), A("st4"), O.add)
+                ts(A("zi2", 32, 128), A("z", 32, 128), 2047, O.bitwise_and)
+                cp(A("zu", 32, 128), A("zi2", 32, 128))
+            act(A("ab", s, s + 256), A("df", s, s + 256), F.Abs)
+            while late:
+                z = late.pop()
+                ts(A("rl", z, z + 256), A("ab", z, z + 256), 127.0, O.subtract, 0.0, O.max)
+            if m % 2 == 0:
+                late.append(s)
+            else:
+                act(A("rl", s, s + 256), A("ab", s, s + 256), F.Relu, bias=-127.0)
+            if m % 4 == 3:
+                wsum(P(m // 4, 0, 64), "em", "rl", 256 * m - 768, 256 * m + 256)
+        tt(A("mz"), A("mc"), A("zi2"), O.add)
+        if t == 0:
+            ts(A("tm"), A("xio"), col(0), O.is_le, 0.5, O.mult)
+        if not last:
+            round_v(t + 1)
+        for h in range(2):
+            a, b = 64 * h, 64 * h + 64
+            ts(A("k1", a, b), P(h, 0, 64), 0.5, O.is_gt, 32768.0, O.mult)
+            ts(A("k2", a, b), P(h, 0, 64), 8.4e7, O.is_gt, -16384.0, O.mult)
+            tt(A("k1", a, b), A("k1", a, b), A("mz", a, b), O.add)
+            tt(A("k3", a, b), A("k1", a, b), A("k2", a, b), O.add)
+        tt(A("k4"), A("k3", 0, 64), A("k3", 64, 128), O.min)
+        tt(A("k5"), A("k4", 0, 32), A("k4", 32, 64), O.min)
+        tt(A("kmi"), A("k5", 0, 16), A("k5", 16, 32), O.min)
+        ts(A("inv"), A("kmi"), 32768.0, O.is_ge, -4096.0, O.mult)
+        ts(A("plc"), A("kmi"), 2047, O.bitwise_and)
+        tt(A("key16"), A("plc"), A("inv"), O.add)
+        tt(A("keyw"), A("plc"), A("inv"), O.add)
+        cp(A("plu"), A("plc"))
+        mm(P(3, 0, 256), A("blk"), A("zb"), True, False)
+        for r in range(16):
+            mm(P(2, r, 256, 16), A("bc", 128 * r, 128 * r + 128), A("key16"))
+        cp(A("oi"), ind(A("tab"), A("plu")))
+        ts(A("oc"), A("oi"), 255, O.bitwise_and)
+        for x in range(16):
+            act(A("kr", x, 256, 16), A("keyw"), F.Identity, bias=A("tm", x, x + 1))
+        cp(A("kb16"), P(2, 0, 256))
+        for c in range(15):
+            e = A("eq", 256 * c + 16 * c + 16, 256 * c + 256)
+            ts(e, A("kb16", 16 * c + 16, 256), A("keyw", c, c + 1), O.is_equal)
+            mm(P(3, 16 * c + 16, 256), A("blk"), e, False, False)
+            if c == 13:
+                tt(A("dm"), P(2, 0, 256), A("kr"), O.is_equal)
+        mm(P(3, 0, 256), A("blk"), A("dm"), False, True)
+        act(A("lsb"), P(3, 0, 256), F.Copy)
+        tt(A("cs"), A("oc"), A("ac"), O.add)
+        ts(A("cn"), A("cs"), 129.0, O.max, 383.0, O.min)
+        act(A("ent"), A("cn"), F.Abs, bias=-256.0)
+        wsum(P(4, 0, 16), "em", "lsb", 0, 256)
+        tt(A("tg"), A("aam"), A("cn"), O.add)
+        mm(P(5, 0, 256), A("blk"), A("ent"))
+        act(A("es"), P(5, 0, 256), F.Sign, bias=-0.5)
+        tt(A("ls"), A("inv"), P(4, 0, 16), O.subtract)
+        ts(A("ls2"), A("ls"), -0.5, O.is_lt)
+        tt(A("ls"), A("ls2"), A("dumpc"), O.mult)
+        tt(A("fo"), A("ls"), A("plc"), O.max)
+        cp(A("fou"), A("fo"))
+        if not last:
+            cp(ind(A("cab"), A("fou")), A("ent"))
+            cp(A("cab", 2048, 2064), A("cab", 0, 16))
+        tt(A("tn"), A("tg"), A("es"), O.mult)
+        cp(ind(A("tab"), A("fou")), A("tn"))
+
+    for c in range(4):
+        s = 512 * c
+        act(A("ab", s, s + 512), A("tab", s, s + 512), F.Abs)
+        ts(A("df", s, s + 512), A("ab", s, s + 512), -1.0, O.mult, float(K), O.add)
+        store("y", "out%d" % c, T.y[:, s:s + 512], A("df", s, s + 512))
+    for c in range(4):
+        g.wait_ge(T.sem["out%d" % c], 16)
+    g.wait_ge(T.sem.ldh, 16)
+    g.wait_ge(T.sem.sent, 8 * RO)
+    for q in ("v", "s", "t", "g"):
+        g.wait_ge(T.sem[SEMOF[q]], count[q])

@@ -3,30 +3,33 @@ from concourse.mybir import AluOpType as O, ActivationFunctionType as F
 
 RO, STEP, N, CAP = 3, 650, 4, 64
 CH = ((0, 64), (64, 128), (128, 192), (192, 224))
-TW = 2576
-DUMMY, DUMP = 2064, 2320
-K = 1 << 22
+DUMMY, DUMP = 2064, 2832
+TW = DUMP + 256
+W = 32768.0
+BIG = 12582912.0
+NONE = 14336
+NP = 4
 F32, B16, H16, I32, U16 = "float32", "bfloat16", "float16", "int32", "uint16"
 
 WIDE = {
-    "detb": (2048, I32), "big": (2048, I32), "tab": (TW, F32), "cab": (TW, B16), "hamb": (4096, B16), "ones": (2048, B16),
-    "em": (2048, B16), "ep": (2048, B16), "e1": (2048, B16), "e2": (2048, B16), "bc": (2048, B16), "rexp": (2048, B16),
-    "lb0": (1024, B16), "lb1": (1024, B16), "lb2": (1024, B16), "rvk": (512, B16), "cmp": (2048, B16), "lg": (4096, B16),
-    "mn": (4096, B16), "sb0": (1280, I32), "sb1": (1280, I32), "sb2": (1280, I32), "ar0": (256, I32), "ar1": (256, I32),
-    "ar2": (256, I32), "df": (2048, F32), "ab": (2048, F32), "rl": (2048, B16), "eq": (4096, B16),
+    "detb": (DUMMY + 256, I32), "big": (2048, I32), "dt": (TW, F32), "et": (TW, B16), "yb": (TW, F32), "cab": (DUMMY, B16),
+    "hamb": (4096, B16), "ones": (2048, B16), "frb": (2048, B16),
+    "em": (2048, B16), "es": (2048, B16), "e1": (2048, B16), "e2": (2048, B16), "bc": (2048, B16), "rexp": (2048, B16),
+    "lb": (1024, B16), "rvk": (512, B16), "cmp": (2048, B16), "lg": (4096, B16),
+    "mn": (4096, B16), "sb0": (1280, F32), "sb1": (1280, F32), "sb2": (1280, F32), "ar0": (256, F32), "ar1": (256, F32),
+    "ar2": (256, F32), "ne": (2048, B16), "sg": (2048, B16), "eq": (4096, B16),
 }
 SMALL = {
-    F32: "pcol 1 cols 16 rr0 128 rr1 128 rr2 128 cw0 8 cw1 8 cw2 8 kscan 256 m64 64 sel15 128 iow 16 iow1 16 iow4 16 xio 16 tm 16 "
-         "kr 256 mc 128 dumpc 16 cneg 8 totu 1 bad4 16 cc 256 sgc 256 ff 256 km 256 ma 256 mb 256 lo 256 t1 256 tt 256 own2 16 "
-         "inc 64 rk 64 chp 256 pk 256 fs 256 fg 256 ft 256 aa 256 aam 256 st1 16 st2 32 st4 64 mz 128 k1 128 k2 128 k3 128 k4 64 "
-         "k5 32 inv 16 keyw 16 cs 256 cn 256 tg 256 tn 256 es 256 ls 16 ls2 16 fo 16",
-    B16: "blk 128 blk592 8 idb 128 shu 128 shd 128 cor 128 tmpb 128 mid 128 gum 128 gdm 128 ns0 128 ns1 128 ns2 128 ni0 128 "
-         "ni1 128 ni2 128 t10 128 t11 128 t12 128 t20 128 t21 128 t22 128 r00 256 r01 256 r02 256 negb 256 io0 256 io1 256 "
-         "a1 128 m128 128 trb 128 orow 64 zb 256 w12 16 live 128 w 128 wz 128 val 256 abc 256 ct 256 sd 256 st_ 256 oh 64 fa 256 "
-         "ent 256 dm 256 lsb 256",
-    H16: "nx 16 nt 16 d16 256 vk16 32 t32 128 ch16 256 mk 64 bo 16 a16 256 key16 16 kb16 256",
-    I32: "icol 1 icol2 1 ti 256 ci 256 fi 256 ui 32 ui2 32 pi 16 h16 16 h16t 16 si 16 vk 32 vo 16 vo2 16 own 16 npi 256 "
-         "npa 256 ai 256 ac 256 z 128 zi2 128 kmi 16 plc 16 oi 256 oc 256",
+    F32: "pcol 1 cols 32 rr0 128 rr1 128 rr2 128 cw0 8 cw1 8 cw2 8 kscan 272 m64 64 sel15 128 iow 16 iow1 16 xio 16 tm 16 "
+         "kr 256 cs32 64 dumpc 16 cneg 8 totu 1 gds 256 t1 256 t2 256 t3 256 t4 256 tv 16 cmpo 64 base 256 term 256 d256 256 "
+         "fr 256 aa 256 st1 16 st2 32 st4 64 ka 64 k4 64 k5 32 inv 16 keyw 16 iv2 16 plc2 16 dd 16 fo1 16 fo 16 en32 256",
+    B16: "blk 128 blka 128 blk592 8 idb 128 idw 128 id128 128 id256 128 shu 128 shd 128 cor 128 tmpb 128 mid 128 gum 128 gdm 128 "
+         "ns0 128 ns1 128 ns2 128 ni0 128 ni1 128 ni2 128 t10 128 t11 128 t12 128 t20 128 t21 128 t22 128 r00 256 r01 256 r02 256 "
+         "negb 256 io0 256 io1 256 a1 128 m128 128 trb 128 mrow 128 zb 256 w12 16 live 128 w 128 wz 128 val 256 abc 256 ct 256 "
+         "eg 256 f1 256 ffq 256 sgc 256 fa 256 ef 256 lv 256 ra 256 sd 256 nq 256 oh 64 ohc 64 cq 256 eo 256 so 256 cn 256 "
+         "ent 256 en 256 dm 256 lsb 256",
+    H16: "nx 16 nt 16 d16 256 vk16 32 t32 128 ch16 256 mk 64 cs64 64 dmp16 16 a16 256 z16 128 invw 16 key16 16 kb16 256",
+    I32: "icol 1 icol2 1 icol3 1 ui 32 ui2 32 pi 16 h16 16 km 272 vk 32 own 16 z 128 zi2 128 kmi 16 plc 16",
     U16: "pl 16 du 256 sl 16 zu 128 plu 16 fou 16",
 }
 
@@ -51,7 +54,7 @@ def _layout():
 
 
 SCRATCH, PLACE = _layout()
-SEMAPHORES = ["sv", "ss", "st", "sg", "sent", "ldh"] + ["ld%d" % i for i in range(4)] + ["out%d" % i for i in range(4)] + ["arr%d" % i for i in range(RO)]
+SEMAPHORES = ["sv", "ss", "st", "sg", "sent", "ldh"] + ["ld%d" % i for i in range(NP)] + ["out%d" % i for i in range(4)] + ["arr%d" % i for i in range(RO)]
 SEMOF = {"v": "sv", "s": "ss", "t": "st", "g": "sg"}
 
 
@@ -84,7 +87,8 @@ def rank_program(g, core, T, topo):
         lo, hi = base + c0, base + (w if c1 is None else c1)
         t = T[buf]
         ap = t[p0:p1, lo:hi] if step == 1 else t[p0:p1, lo:hi:step]
-        return (ap, buf, lo, hi)
+        cols = ((1 << (hi - lo + step - 1) // step * step) - 1) // ((1 << step) - 1) << lo
+        return (ap, buf, cols, step)
 
     def P(b, c0, c1, step=1, p0=0, p1=128):
         return A("p%d" % b, c0, c1, step, p0, p1)
@@ -100,13 +104,13 @@ def rank_program(g, core, T, topo):
 
     def need(q, outs, ins, extra=()):
         want = dict(extra)
-        acc = [(a, "w") for o in outs for a in flat(o)] + [(a, "r") for i in ins for a in flat(i)]
-        for (_, buf, lo, hi), kind in acc:
+        acc = [(flat(o)[0], "w") for o in outs] + [(a, "r") for o in outs for a in flat(o)[1:]] + [(a, "r") for i in ins for a in flat(i)]
+        for (_, buf, cols, _), kind in acc:
             ps = ispsum(buf)
-            for (sq, idx, k2, l2, h2) in hist.get(buf, ()):
+            for (sq, idx, k2, c2) in hist.get(buf, ()):
                 if sq == q == "t":
                     continue
-                if (ps and sq != q) or ((kind == "w" or k2 == "w") and lo < h2 and l2 < hi):
+                if (ps and sq != q) or ((kind == "w" or k2 == "w") and cols & c2):
                     want[sq] = max(want.get(sq, 0), idx)
         for s in sorted(want):
             if known[q].get(s, 0) < want[s]:
@@ -118,13 +122,13 @@ def rank_program(g, core, T, topo):
 
     def note(q, idx, acc):
         clock[(q, idx)] = dict(known[srcq.get(q, q)])
-        for (_, buf, lo, hi), kind in acc:
+        for (_, buf, cols, _), kind in acc:
             old = hist.get(buf, [])
             if ispsum(buf):
-                keep = [e for e in old if e[0] == q and q != "t" and not (kind == "w" and lo <= e[3] and e[4] <= hi)]
+                keep = [e for e in old if e[0] == q and q != "t" and not (kind == "w" and e[3] & ~cols == 0)]
             else:
-                keep = [e for e in old if not (lo <= e[3] and e[4] <= hi and (kind == "w" or (e[2] == "r" and e[0] == q)))]
-            hist[buf] = keep + [(q, idx, kind, lo, hi)]
+                keep = [e for e in old if not (e[3] & ~cols == 0 and (kind == "w" or (e[2] == "r" and e[0] == q)))]
+            hist[buf] = keep + [(q, idx, kind, cols)]
 
     def emit(q, outs, ins, call, extra=()):
         acc = need(q, outs, ins, extra)
@@ -186,52 +190,49 @@ def rank_program(g, core, T, topo):
 
     one = lambda w: A("ones", 0, w)
     col = lambda j: A("cols", j, j + 1)
+    ROW, R15, LO, HI, W1, W2, W1S, W2S, BMB, BRA, UP, DOWN, ALT, TMP, TMP2 = range(15)
 
-    for c in range(4):
-        load("y", "ld%d" % c, A("detb", 512 * c, 512 * c + 512), T.det[:, 512 * c:512 * c + 512])
-    load("s", "ldh", A("hamb"), T.ham[:, :])
+    pw = 2048 // NP
+    for c in range(NP):
+        load("y", "ld%d" % c, A("detb", pw * c, pw * c + pw), T.det[:, pw * c:pw * c + pw])
+    load("y", "ldh", A("hamb"), T.ham[:, :])
 
-    fill(A("ones", 0, 256), 1.0)
-    fill(A("em"), 0.0)
+    fill(A("ones", 0, 272), 1.0)
     iota(A("icol"), [[0, 1]], 0, 1)
     sel(A("tmpb"), one(128), [[-16, 8], [0, 16]], O.is_ge, 0.0, 0, 1)
     sel(A("blk"), A("tmpb"), [[16, 8], [0, 16]], O.is_ge, 0.0, 15, -1)
-    ts(A("icol2"), A("icol"), 15, O.bitwise_and)
-    cp(A("pcol"), A("icol"))
-    cp(col(0), A("icol2"))
-    ts(col(1), col(0), 15.0, O.is_equal)
-    ts(col(2), col(1), 15.0, O.mult, 1.0, O.add)
-    ts(col(3), col(1), -1000.0, O.mult)
-    ts(col(4), col(1), 999.0, O.mult, 1.0, O.add)
-    ts(col(5), col(0), 13.0, O.mult, 5.0, O.add)
-    ts(col(6), col(0), -14.0, O.mult, 255.0, O.add)
-    fill(A("negb"), -1.0)
-    ts(col(7), col(0), -1.0, O.mult, -2033.0, O.add)
-    ts(col(8), col(7), 8192.0, O.mult, 8192.0, O.add)
-    ts(col(9), col(1), -8192.0, O.mult)
-    ts(col(10), col(0), 0.0, O.is_equal, 8192.0, O.mult)
-    for r in range(16):
-        act(A("em", 128 * r + r, 128 * r + 128, 16), A("blk", 0, 128, 16), F.Copy)
-    act(A("ep"), A("em"), F.Identity, scale=col(2))
     sel(A("idb"), one(128), [[-1, 128]], O.is_equal, 0.0, 0, 1)
     sel(A("shu"), one(128), [[-1, 128]], O.is_equal, 0.0, -1, 1)
     sel(A("cor"), one(128), [[-1, 128]], O.is_equal, 0.0, 127, 1)
     sel(A("m128"), one(128), [[0, 8], [1, 16]], O.not_equal, 0.0, 0, 0)
-    sel(A("a1"), one(128), [[0, 8], [1, 16]], O.not_equal, 0.0, -15, 0)
-    iota(A("io0"), [[1, 256]], 0, 0)
-    iota(A("io1"), [[1, 256]], 1, 0)
-    for c in range(4):
-        s = 512 * c
-        ts(A("big", s, s + 512), A("detb", s, s + 512), 255, O.bitwise_and)
-        ts(A("df", s, s + 512), A("big", s, s + 512), 128.0, O.subtract)
-        act(A("cab", s, s + 512), A("df", s, s + 512), F.Abs)
-        if c == 0:
-            tt(A("tmpb"), A("idb"), A("shu"), O.subtract)
-            tt(A("tmpb"), A("tmpb"), A("cor"), O.subtract)
-            ts(A("mid"), A("idb"), -1.0, O.mult)
-    act(A("cab", 2048, 2064), A("cab", 0, 16), F.Copy)
-    act(A("e1"), A("em"), F.Identity, scale=col(5))
-    act(A("e2"), A("em"), F.Identity, scale=col(6))
+    fill(A("em"), 0.0)
+    fill(A("negb"), -1.0)
+    ts(A("icol2"), A("icol"), 15, O.bitwise_and)
+    ts(A("icol3"), A("icol"), 1, O.bitwise_and)
+    cp(A("pcol"), A("icol"))
+    fill(A("lb"), 0.0)
+    cp(col(ROW), A("icol2"))
+    ts(col(ALT), A("icol3"), -2.0, O.mult, 1.0, O.add)
+    fill(A("et", 2048, TW), 128.0)
+    ts(col(R15), col(ROW), 15.0, O.is_equal)
+    ts(col(W1), col(ROW), 13.0, O.mult, 5.0, O.add)
+    ts(col(W2), col(ROW), -14.0, O.mult, 255.0, O.add)
+    ts(col(BMB), col(ROW), -8192.0, O.mult, -8192.0 * 2032, O.add)
+    ts(col(BRA), col(ROW), 8192.0, O.mult, 8192.0 * 2034, O.add)
+    ts(col(DOWN), col(ROW), 0.0, O.is_equal, 8192.0, O.mult)
+    ts(col(LO), col(R15), -4000.0, O.mult)
+    ts(col(HI), col(R15), 3999.0, O.mult, 1.0, O.add)
+    ts(col(UP), col(R15), -8192.0, O.mult)
+    ts(col(W1S), col(W1), 1.0 / W, O.mult)
+    ts(col(W2S), col(W2), 1.0 / W, O.mult)
+    fill(A("detb", 2048, DUMMY + 256), 128)
+    tt(A("tmpb"), A("idb"), A("shu"), O.subtract)
+    ts(A("mid"), A("idb"), -1.0, O.mult)
+    tt(A("tmpb"), A("tmpb"), A("cor"), O.subtract)
+    for r in range(16):
+        act(A("em", 128 * r + r, 128 * r + 128, 16), A("blk", 0, 128, 16), F.Identity, scale=W)
+    act(A("idw"), A("idb"), F.Identity, scale=W)
+    act(A("e1"), A("em"), F.Identity, scale=col(W1S))
 
     def chunk(t):
         m0 = STEP * (t + 1) // 16
@@ -243,44 +244,61 @@ def rank_program(g, core, T, topo):
         iota(A(rr, 0, ml), [[1, ml]], 128, 0)
         iota(A(rr, m0, 128), [[1, 128 - m0]], m0, 0)
         iota(A(rr, ml, m0), [[0, 1]], 126, 0)
-        sel(A("cw%d" % t), one(8), [[0, 8]], O.not_equal, -128.0, -ml, 1)
         sel(A("t2%d" % t), one(128), [[200, 128]], O.is_equal, 0.0, -127 - 200 * ml, 1)
         sel(A("ns%d" % t), A("tmpb"), [[1, 128]], O.not_equal, 0.0, -ml, 0)
         sel(A("ni%d" % t), A("mid"), [[1, 128]], O.not_equal, 0.0, -ml, 0)
+        sel(A("cw%d" % t), one(8), [[0, 8]], O.not_equal, -128.0, -ml, 1)
         sel(A("r0%d" % t), A("negb"), [[0, 256]], O.is_equal, 0.0, -m0, 1)
-        if t:
-            iota(A("lb%d" % t), [[0, 1024]], 0, 0)
 
     def round_v(t):
         m0, ml = chunk(t)
-        ts(col(11), A("pcol"), float(m0), O.is_lt, 128.0, O.mult)
-        tt(col(12), col(11), A("pcol"), O.add)
-        ts(A("t1%d" % t), A("rr%d" % t), col(12), O.is_ge)
-        if t == 0:
-            fill(A("lb%d" % t), 0.0)
-        cp(A("lb%d" % t, 15, 1024, 144), A("cw%d" % t))
+        ts(col(TMP), A("pcol"), float(m0), O.is_lt, 128.0, O.mult)
+        tt(col(TMP2), col(TMP), A("pcol"), O.add)
+        ts(A("t1%d" % t), A("rr%d" % t), col(TMP2), O.is_ge)
+        ts(A("lb", 15, 1024, 144), A("cw%d" % t), 16.0, O.mult)
 
+    iota(A("io0"), [[1, 256]], 0, 0)
     round_g(0)
+    sel(A("a1"), one(128), [[0, 8], [1, 16]], O.not_equal, 0.0, -15, 0)
+    iota(A("io1"), [[1, 256]], 1, 0)
     iota(A("iow"), [[16, 16]], 0, 0)
-    round_v(0)
-    fill(A("ones", 256, 2048), 1.0)
+
+    for c in range(NP):
+        s = pw * c
+        ts(A("big", s, s + pw), A("detb", s, s + pw), 255, O.bitwise_and)
+        if c == NP - 1:
+            round_v(0)
+        cp(A("et", s, s + pw), A("big", s, s + pw))
+        act(A("cab", s, s + pw), A("et", s, s + pw), F.Abs, bias=-128.0)
+        if c == 0:
+            act(A("cab", 2048, DUMMY), A("cab", 0, 16), F.Copy)
+            fill(A("ones", 272, 2048), 1.0)
+
+    def free_mark(c):
+        s = 512 * c
+        mm(P(6 + c % 2, 0, 512), A("blk"), A("cab", s, s + 512))
+        act(A("frb", s, s + 512), P(6 + c % 2, 0, 512), F.Relu, bias=1.0, scale=-1.0)
 
     def rest_g():
         sel(A("rexp"), one(2048), [[-1, 128], [0, 16]], O.is_equal, 0.0, 0, 1)
+        sel(A("kscan"), one(272), [[0, 16], [1, 17]], O.not_equal, -3.0e7, 0, 0)
         sel(A("shd"), one(128), [[-1, 128]], O.is_equal, 0.0, 1, 1)
-        sel(A("trb"), A("blk"), [[-1, 128]], O.is_ge, 0.0, 0, 1)
-        sel(A("kscan"), one(256), [[0, 16], [1, 16]], O.not_equal, -4.0e6, 0, 0)
         sel(A("rvk"), one(512), [[-8, 4], [-1, 8], [0, 16]], O.is_equal, 0.0, 0, 1)
-        iota(A("orow"), [[256, 4], [0, 16]], 0, 0)
+        sel(A("trb"), A("blk"), [[-1, 128]], O.is_ge, 0.0, 0, 1)
         sel(A("m64"), one(64), [[0, 4], [1, 16]], O.not_equal, 0.0, 0, 0)
+        iota(A("cs32"), [[256, 4], [-16, 16]], -1024, 0)
+        iota(A("mrow"), [[2048, 8], [0, 16]], -31 * 16384, 0)
+        iota(A("xio"), [[1, 16]], 0, 0)
+        iota(A("sb0"), [[0, 1280]], NONE, 0)
+        iota(A("dt", 2048, TW), [[0, TW - 2048]], 0, 0)
 
     def rest_v():
         ts(A("blk592"), A("blk", 0, 128, 16), 592.0, O.mult)
-        ts(A("w12", 0, 8), A("blk", 0, 128, 16), col(5), O.mult)
-        ts(A("w12", 8, 16), A("blk", 0, 128, 16), col(6), O.mult)
+        ts(A("w12", 0, 8), A("blk", 0, 128, 16), col(W1), O.mult)
+        ts(A("w12", 8, 16), A("blk", 0, 128, 16), col(W2), O.mult)
         fill(A("zb"), 0.0)
-        ts(A("iow4"), A("iow"), 0.25, O.mult, 256.0, O.add)
         ts(A("dumpc"), A("iow"), float(DUMP), O.add)
+        ts(A("dmp16"), A("iow"), 1024.0, O.add)
 
     def rest_v2():
         tt(A("gum"), A("idb"), A("shu"), O.subtract)
@@ -288,74 +306,68 @@ def rank_program(g, core, T, topo):
         tt(A("gum"), A("gum"), A("a1"), O.mult)
         tt(A("gdm"), A("gdm"), A("m128"), O.mult)
 
-    def whash(src):
+    def whash(src, between=None):
         for e in range(2):
             for r in range(16):
                 mm(P(6, 16 * e, 16 * e + 16), A("e%d" % (e + 1), 128 * r, 128 * r + 128), A(src, r, 256, 16), r == 0, r == 15)
+            if between and e == 0:
+                between()
 
-    def mix(steps=False):
-        cp(A("ui"), P(6, 0, 32))
-        ts(A("ui2"), A("ui"), 4095, O.bitwise_and)
-        if steps:
-            ts(A("st1"), A("ui2", 0, 16), 2.0, O.mult, 1.0, O.add)
-            for j in range(2):
-                act(A("st2", 16 * j, 16 * j + 16), A("st1"), F.Identity, scale=2.0)
-            for j in range(2):
-                act(A("st4", 32 * j, 32 * j + 32), A("st2"), F.Identity, scale=2.0)
-        tt(A("pi"), A("ui2", 0, 16), A("ui2", 16, 32), O.mult)
-
-    def wsum(out, weights, src, c0, c1, start=True):
+    def wsum(out, weights, src, c0, c1, start=True, stop=True):
         for r in range(16):
-            mm(out, A(weights, 128 * r, 128 * r + 128), A(src, c0 + r, c1, 16), start and r == 0, r == 15)
+            mm(out, A(weights, 128 * r, 128 * r + 128), A(src, c0 + r, c1, 16), start and r == 0, stop and r == 15)
 
     for t in range(RO):
         start = STEP * (t + 1)
         m0, off = start // 16, start % 16
         last = t == RO - 1
+        dummy = DUMMY + 256 * t
         for u in range(16):
-            mm(P(0, u, 128, 16), A("cab", off + u, off + u + 2033, 16), A("blk", 0, 128, 16))
+            mm(P(0, u, 128, 16), A("et" if t else "cab", off + u, off + u + 2033, 16), A("blk", 0, 128, 16))
         mm(P(3, 0, 256), A("a1", 0, 128, 1, 0, 1), A("io1", 0, 256, 1, 0, 1), True, False)
+        if t == 0:
+            free_mark(0)
         ts(A("live"), P(0, 0, 128), 0.5, O.is_gt)
         scan(A("w"), A("m128"), A("live"), O.mult, O.add)
         if t == 0:
-            ts(A("sel15"), A("blk"), col(1), O.mult)
-            ts(A("iow"), A("iow"), col(0), O.add)
+            ts(A("sel15"), A("blk"), col(R15), O.mult)
+            ts(A("iow"), A("iow"), col(ROW), O.add)
             ts(A("iow1"), A("iow"), 1.0, O.add)
-            for c in range(4):
-                ts(A("tab", 512 * c, 512 * c + 512), A("detb", 512 * c, 512 * c + 512), float(K), O.subtract)
         mm(P(1, 0, 8), A("t1%d" % t), A("w", 15, 128, 16), True, False)
         mm(P(1, 0, 8), A("t2%d" % t), A("w", 15 - off, 128, 16), False, True)
-        mm(P(5, 0, 1), A("w"), A("ones", 0, 1))
         mm(P(2, 128, 136), A("ni%d" % t), A("w", 15, 128, 16))
         mm(P(2, 0, 128), A("ns%d" % t), A("w"))
+        mm(P(5, 0, 1), A("w"), A("ones", 0, 1))
         sel(A("wz"), A("w"), [[0, 8], [1, 16]], O.not_equal, 0.0, -15, 0)
         if t == 0:
             rest_g()
-        iota(A("sb%d" % t, 0, 1024), [[0, 1024]], K + 128, 0)
         act(A("cneg"), P(2, 128, 136), F.Copy)
-        lb = "lb%d" % t
         for h in range(8):
             ts(A("cmp", 256 * h, 256 * h + 256), A("io0"), P(1, h, h + 1), O.is_ge)
-            act(A(lb, 144 * h, 144 * h + 15), P(2, 16 * h, 16 * h + 15), F.Identity, bias=A("cneg", h, h + 1))
+            act(A("lb", 144 * h, 144 * h + 15), P(2, 16 * h, 16 * h + 15), F.Identity, bias=A("cneg", h, h + 1))
             if h == 3:
                 mm(P(3, 0, 256), A("wz"), A("r0%d" % t), False, False)
             if h == 4:
                 act(A("totu"), P(5, 0, 1), F.Copy)
                 mm(P(5, 1, 2), A("sel15"), A("totu"))
-            mm(P(3, 0, 256), A(lb, 128 * h, 128 * h + 128), A("cmp", 256 * h, 256 * h + 256), False, h == 7)
+            mm(P(3, 0, 256), A("lb", 128 * h, 128 * h + 128), A("cmp", 256 * h, 256 * h + 256), False, h == 7)
         ts(A("nx"), A("iow1"), P(5, 1, 2), O.subtract, 0.0, O.max)
-        ts(A("nt"), A("iow"), P(5, 1, 2), O.is_ge, float(DUMMY - start), O.mult)
-        mm(P(4, 0, 16), A("idb"), A("nx"), True, False)
-        mm(P(4, 0, 16), A("idb"), A("nt"), False, False)
-        ts(A("val"), P(3, 0, 256), col(3), O.max, col(4), O.min)
-        wsum(P(4, 0, 16), "ep", "val", 0, 256, False)
+        ts(A("nt"), A("iow"), P(5, 1, 2), O.is_ge, float(dummy - start), O.mult)
+        mm(P(4, 0, 16), A("idw"), A("nx"), True, False)
+        mm(P(4, 0, 16), A("idw"), A("nt"), False, False)
+        ts(A("val"), P(3, 0, 256), col(LO), O.max, col(HI), O.min)
+        wsum(P(4, 0, 16), "em", "val", 0, 256, False)
         if t == 0:
+            free_mark(1)
             rest_v()
-            act(A("tab", 2048, TW), A("ones", 0, TW - 2048), F.Identity, bias=128.0 - K, scale=0.0)
-            act(A("cab", 2064, TW), A("ones", 0, TW - 2064), F.Identity, scale=0.0)
-        ts(A("pl"), P(4, 0, 16), float(16 * m0 + off), O.add)
-        ts(A("du"), ind(A("tab"), A("pl")), 1.0 / 256, O.mult, K / 256 - 0.5, O.add)
-        act(A("abc"), ind(A("cab"), A("pl")), F.Copy)
+        else:
+            tt(ind(A("dt"), A("fou")), A("aa"), A("fr"), O.add)
+        ts(A("pl"), P(4, 0, 16), 1.0 / W, O.mult, float(16 * m0 + off), O.add)
+        if t == 0:
+            ts(A("du"), ind(A("detb"), A("pl")), 1.0 / 256, O.mult, -0.5, O.add)
+        else:
+            ts(A("du"), ind(A("dt"), A("pl")), 1.0 / 256, O.mult)
+        act(A("abc"), ind(A("et"), A("pl")), F.Abs, bias=-128.0)
         for h in range(2):
             mm(P(7, 128 * h, 128 * h + 128), A("abc", 128 * h, 128 * h + 128), A("idb"))
         for a, b in CH:
@@ -375,87 +387,104 @@ def rank_program(g, core, T, topo):
             rep(b)
         mm(P(7, 0, 256), A("gum"), A("d16"))
         mm(P(7, 256, 512), A("gdm"), A("d16"))
+        mm(P(5, 0, 256), A("idb"), A("d16"))
+        mm(P(6, 16, 272, 17), A("zb", 0, 128), A("blk", 0, 16))
         cp(A("ui"), P(4, 0, 32))
         ts(A("ui2"), A("ui"), 4095, O.bitwise_and)
-        tt(A("pi"), A("ui2", 0, 16), A("ui2", 16, 32), O.mult)
-        ts(A("h16"), A("pi"), 1, O.arith_shift_right, 0x7FFFFFF0, O.bitwise_and)
-        ts(A("h16t"), A("h16"), float(16 * t), O.add)
         cp(A("lg", 3584, 4096), ind(A("hamb"), A("du", 224, 256)))
+        tt(A("pi"), A("ui2", 0, 16), A("ui2", 16, 32), O.mult)
+
+        def kmax(h):
+            scan(A("km", 136 * h, 136 * h + 136), A("kscan", 136 * h, 136 * h + 136), P(6, 136 * h, 136 * h + 136), O.add, O.max)
+
         for b in range(8):
             s = 512 * b
             tt(A("mn", s, s + 512), A("lg", s, s + 512), P(b % 4, 0, 512), O.min)
+            if b == 0:
+                ts(A("h16"), A("pi"), 1, O.arith_shift_right, 0x7FFFFFF0, O.bitwise_and)
+            if b == 1:
+                ts(A("kscan", 16, 272, 17), A("h16"), float(16 * t), O.add)
             if b < 4:
                 rep(b + 4)
+            if b == 5:
+                kmax(0)
             if b % 4 == 3:
                 h = b // 4
                 for k in range(16):
-                    mm(P(6, 128 * h + k, 128 * h + 128, 16), A("mn", 2048 * h + k, 2048 * h + 2048, 16), A("blk592"))
+                    mm(P(6, 136 * h + k, 136 * h + 136, 17), A("mn", 2048 * h + k, 2048 * h + 2048, 16), A("blk592"))
+        act(P(7, 0, 256), P(7, 0, 256), F.Identity, bias=col(UP))
+        act(A("gds"), P(7, 256, 512), F.Identity, bias=col(DOWN))
+        act(A("eg"), ind(A("et"), A("pl")), F.Copy)
+        act(A("fa"), A("abc"), F.Relu, bias=-1.0)
+        act(A("sgc"), A("eg"), F.Sign, bias=-128.0)
+        act(A("d256"), P(5, 0, 256), F.Identity, bias=2048.0 * 256, scale=256.0)
+        act(A("f1"), A("eg"), F.Identity, bias=159.625, scale=0.25)
+        act(A("ffq"), A("f1"), F.Identity, bias=-0.75, scale=1.0 / 256)
         if t == 0:
             ts(A("rvk", 0, 256), A("rvk", 0, 256), -1.0, O.mult)
             ts(A("trb"), A("trb"), -1.0, O.mult)
-        cp(A("ti"), ind(A("tab"), A("pl")))
-        ts(A("fi"), A("ti"), 255, O.bitwise_and, 2, O.arith_shift_right)
-        ts(A("ff"), A("fi"), 32.0, O.subtract)
-        act(P(7, 0, 256), P(7, 0, 256), F.Identity, bias=col(9))
-        act(P(7, 256, 512), P(7, 256, 512), F.Identity, bias=col(10))
-        mm(P(5, 0, 256), A("idb"), A("d16"))
-        scan(A("km"), A("kscan"), P(6, 0, 256), O.add, O.max)
-        tt(A("si"), A("km", 15, 256, 16), A("h16t"), O.add)
-        ts(A("vk", 0, 16), A("si"), 4, O.arith_shift_right, 4095, O.bitwise_and)
-        ts(A("vk", 16, 32), A("si"), 15, O.bitwise_and)
+            ts(A("blka"), A("blk"), col(ALT), O.mult)
+            ts(A("cs64"), A("cs32"), col(ROW), O.subtract)
+        kmax(1)
+        ts(A("vk", 0, 16), A("km", 16, 272, 17), 4, O.arith_shift_right, 4095, O.bitwise_and)
+        ts(A("vk", 16, 32), A("km", 16, 272, 17), 15, O.bitwise_and)
         ts(A("vk16"), A("vk"), 2048.0, O.subtract)
+        mm(P(2, 256, 512), A("blk"), A("fa"))
         mm(P(4, 0, 128, 1, 0, 32), A("vk16"), A("idb"))
         cp(A("t32", 0, 128, 1, 0, 32), P(4, 0, 128, 1, 0, 32))
         for h in range(2):
             s = 128 * h
-            mm(P(1, s, s + 128), A("rvk", 256 + s, 256 + s + 128, 1, 0, 32), A("t32", 0, 128, 1, 0, 32))
-        for h in range(2):
-            s = 128 * h
             mm(P(0, s, s + 128), A("idb"), A("d16", s, s + 128), True, False)
             mm(P(0, s, s + 128), A("rvk", s, s + 128, 1, 0, 32), A("t32", 0, 128, 1, 0, 32), False, True)
-        ts(A("ma"), P(1, 0, 256), col(7), O.is_ge)
-        act(A("sd"), P(0, 0, 256), F.Sign)
-        act(A("mb"), P(1, 0, 256), F.Relu, bias=col(8), scale=-8192.0)
-        wsum(P(3, 0, 16), "em", "sd", 0, 256)
-        tt(P(2, 0, 256), P(7, 0, 256), A("ma"), O.mult)
-        tt(A("lo"), P(7, 256, 512), A("mb"), O.min)
-        tt(A("t1"), A("lo"), P(0, 0, 256), O.min)
-        tt(A("tt"), A("t1"), P(2, 0, 256), O.max)
-        tt(A("ch16"), P(5, 0, 256), A("tt"), O.subtract)
-        act(A("st_"), A("tt"), F.Sign)
-        mm(P(5, 256, 512), A("blk"), A("st_"))
-        whash("ch16")
-        act(A("fa"), A("abc"), F.Relu, bias=-1.0)
-        mm(P(2, 0, 256), A("blk"), A("fa"))
-        act(A("fs"), P(2, 0, 256), F.Sign, bias=-0.5)
-        cp(A("vo"), P(3, 0, 16))
-        ts(A("vo2"), A("vo"), 1, O.bitwise_and)
-        tt(A("bad4"), A("vo2"), A("nt"), O.max)
-        ts(A("bad4"), A("bad4"), 0.0, O.is_gt, 4.0, O.mult)
-        tt(A("bo"), A("bad4"), A("iow4"), O.mult)
-        ts(A("chp"), A("ch16"), 256.0, O.mult, 2048.0 * 256 + 128, O.add)
-        cp(A("npi"), P(5, 256, 512))
-        ts(A("npa"), A("npi"), 1, O.bitwise_and)
-        ts(P(1, 0, 256), A("npa"), 2.0, O.mult, -1.0, O.add)
-        tt(P(1, 0, 256), P(1, 0, 256), A("ff"), O.mult)
-        tt(A("pk"), P(1, 0, 256), A("chp"), O.add)
-        mix()
-        ts(A("own"), A("pi"), 5, O.arith_shift_right, 3, O.bitwise_and)
-        tt(A("own2"), A("own"), A("bad4"), O.max)
+        for h in range(2):
+            s = 128 * h
+            mm(P(1, s, s + 128), A("rvk", 256 + s, 256 + s + 128, 1, 0, 32), A("t32", 0, 128, 1, 0, 32))
+        act(A("lv"), P(2, 256, 512), F.Sign)
+        act(A("fr"), P(2, 256, 512), F.Relu, bias=128.0, scale=-128.0)
+        tt(A("t1"), A("gds"), P(0, 0, 256), O.min)
+        act(P(2, 0, 256), P(1, 0, 256), F.Relu, bias=col(BMB), scale=-8192.0)
+        act(A("ra"), P(1, 0, 256), F.Relu, bias=col(BRA), scale=8192.0)
+        act(A("sd"), P(0, 0, 256), F.Sign, scale=col(ALT))
+        tt(A("t2"), A("t1"), P(7, 0, 256), O.max)
+        mm(P(4, 0, 256), A("idb"), A("d16"), True, False)
+        mm(P(4, 0, 256), A("idb"), A("ra"), False, True)
+        mm(P(3, 0, 16), A("idw"), A("nt"), True, False)
+        wsum(P(3, 0, 16), "em", "sd", 0, 256, False)
+        mm(P(7, 0, 256), A("idb"), A("eg"), True, False)
+        mm(P(7, 0, 256), A("mid"), A("sgc"), False, True)
+        tt(A("t3"), A("t2"), P(2, 0, 256), O.min)
+        tt(A("t4"), P(5, 0, 256), A("t3"), O.subtract)
+        tt(A("ch16"), A("t4"), P(4, 0, 256), O.min)
+        act(A("tv"), P(3, 0, 16), F.Abs, bias=1.0, scale=1.0 / W)
         for o in range(4):
-            ts(A("oh", 16 * o, 16 * o + 16), A("own2"), float(o), O.is_equal)
-        mm(P(7, 64, 128), A("blk"), A("oh"))
-        mm(P(4, 0, 64), A("ones", 0, 128, 1, 0, 1), A("orow", 0, 64, 1, 0, 1), True, False)
-        mm(P(4, 0, 64), A("trb"), A("oh"), False, True)
-        scan(A("inc"), A("m64"), P(7, 64, 128), O.mult, O.add)
-        tt(A("rk"), A("inc"), P(4, 0, 64), O.add)
-        tt(A("mk"), A("rk"), A("oh"), O.mult)
-        mm(P(3, 0, 16), A("idb"), A("bo"), True, False)
+            act(A("cmpo", 16 * o, 16 * o + 16), A("tv"), F.Identity, bias=-1.0, scale=o + 1.0)
+        act(A("ef"), P(7, 0, 256), F.Copy)
+        if t == 0:
+            act(A("e2"), A("em"), F.Identity, scale=col(W2S))
+        tt(A("nq"), A("ch16"), P(5, 0, 256), O.not_equal)
+        whash("ch16", lambda: mm(P(1, 0, 256), A("blka"), A("nq")))
+        act(P(1, 0, 256), P(1, 0, 256), F.Abs, scale=2.0)
+        mm(P(0, 0, 256), A("idb"), A("ch16"), True, False)
+        mm(P(0, 0, 256), A("mid"), A("ffq"), False, True)
+        mm(P(4, 0, 64), A("idb"), A("cs64"), True, False)
+        mm(P(3, 0, 16), A("idb"), A("dmp16"), True, False)
+        act(A("base"), P(0, 0, 256), F.Copy)
+        tt(A("term"), A("ffq"), P(1, 0, 256), O.mult)
+        cp(A("ui"), P(6, 0, 32))
+        ts(A("ui2"), A("ui"), 4095, O.bitwise_and)
+        tt(A("pi"), A("ui2", 0, 16), A("ui2", 16, 32), O.mult)
+        ts(A("own"), A("pi"), 5, O.arith_shift_right, 3, O.bitwise_and)
+        for o in range(4):
+            tt(A("oh", 16 * o, 16 * o + 16), A("own"), A("cmpo", 16 * o, 16 * o + 16), O.is_equal)
+        scan(A("ohc"), A("m64"), A("oh"), O.mult, O.add)
+        mm(P(4, 0, 64), A("trb"), A("oh"), False, False)
+        mm(P(4, 0, 64), A("blk"), A("ohc"), False, True)
+        tt(A("mk"), A("oh"), P(4, 0, 64), O.mult)
         for o in range(4):
             mm(P(3, 0, 16), A("idb"), A("mk", 16 * o, 16 * o + 16), False, o == 3)
         cp(A("sl"), P(3, 0, 16))
         sb, ar, arr = "sb%d" % t, "ar%d" % t, "arr%d" % t
-        cp(ind(A(sb), A("sl")), A("pk"))
+        tt(ind(A(sb), A("sl")), A("base"), A("term"), O.add)
         trs = []
         for o, es in plan(topo, T.cores, rank):
             rid, pid = topo.addr(T.cores[o])[:2]
@@ -466,83 +495,104 @@ def rank_program(g, core, T, topo):
         got = sum(len(es) for q in range(N) if q != rank for o, es in plan(topo, T.cores, q) if o == rank)
         if t == 0:
             sel(A("bc"), one(2048), [[-1, 16], [-16, 8], [0, 16]], O.is_equal, 0.0, 0, 1)
-            iota(A("mc"), [[2048, 8], [0, 16]], 0, 0)
-            iota(A("xio"), [[1, 16]], 0, 0)
         if not last:
             round_g(t + 1)
+            iota(A("sb%d" % (t + 1)), [[0, 1280]], NONE, 0)
+        if t == 1:
+            iota(A("yb", 2048, TW), [[0, TW - 2048]], 0, 0)
         cp(A(ar, 64 * rank, 64 * rank + 64), A(sb, 256 * rank, 256 * rank + 64))
-        ts(A("ci"), A("ti"), 255, O.bitwise_and)
-        ts(A("cc"), A("ci"), 128.0, O.subtract)
-        act(A("sgc"), A("cc"), F.Sign)
         if t == 0:
+            act(A("id128"), A("idb"), F.Identity, scale=-128.0)
+            act(A("id256"), A("idb"), F.Identity, scale=256.0)
+            free_mark(2)
+            free_mark(3)
             for c in range(4):
-                s = 512 * c
-                mm(P(c % 3, 0, 512), A("blk"), A("cab", s, s + 512))
-                act(P(c % 3, 0, 512), P(c % 3, 0, 512), F.Sign, bias=-0.5)
-                tt(A("tab", s, s + 512), A("tab", s, s + 512), P(c % 3, 0, 512), O.mult)
-        if not last:
-            cp(ind(A("cab"), A("pl")), A("fa"))
-        tt(A("fg"), A("ti"), A("sgc"), O.subtract)
-        tt(A("ft"), A("fg"), A("fs"), O.mult)
-        cp(ind(A("tab"), A("pl")), A("ft"))
-        if not last:
-            iota(A("tab", 2048, DUMP), [[0, DUMP - 2048]], 128 - K, 0)
-        ts(A("ai"), A(ar), 8, O.arith_shift_right, extra=[(arr, got)])
-        ts(A("a16"), A("ai"), 2048.0, O.subtract)
+                s, b = 512 * c, (0, 1, 2, 5)[c]
+                mm(P(b, 0, 512), A("idb"), A("et", s, s + 512), True, False)
+                mm(P(b, 0, 512), A("id128"), A("frb", s, s + 512), False, True)
+                tt(A("dt", s, s + 512), A("detb", s, s + 512), P(b, 0, 512), O.subtract)
+                act(A("et", s, s + 512), P(b, 0, 512), F.Copy)
+            tt(ind(A("dt"), A("pl")), A("d256"), A("fr"), O.add)
+            tt(ind(A("et"), A("pl")), A("ef"), A("lv"), O.mult)
+            act(A("es"), A("em"), F.Identity, scale=31.0 / 32)
+        else:
+            tt(ind(A("et"), A("pl")), A("ef"), A("lv"), O.mult)
+            tt(ind(A("dt"), A("pl")), A("d256"), A("fr"), O.add)
+
+        def whole(c):
+            s = 512 * c
+            tt(A("yb", s, s + 512), A("dt", s, s + 512), P(2 + c, 0, 512), O.add)
+
+        if last:
+            for c in range(4):
+                mm(P(2 + c, 0, 512), A("idb"), A("et", 512 * c, 512 * c + 512))
+        ts(A("a16"), A(ar), BIG, O.add, BIG, O.subtract, extra=[(arr, got)])
         whash("a16")
-        ts(A("aa"), A("ai"), 256.0, O.mult, 128.0 - K, O.add)
-        ts(A("aam"), A("aa"), 256.0, O.subtract)
-        ts(A("ac"), A(ar), 255, O.bitwise_and)
-        mix(True)
+        ts(A("aa"), A("a16"), 256.0, O.mult, 2048.0 * 256, O.add)
+        tt(A("cq"), A(ar), A("a16"), O.subtract)
+        if last:
+            whole(0)
+        cp(A("ui"), P(6, 0, 32))
+        ts(A("ui2"), A("ui"), 4095, O.bitwise_and)
+        ts(A("invw"), A("ui", 0, 16), 4.0e6, O.is_gt, W, O.mult)
+        tt(A("pi"), A("ui2", 0, 16), A("ui2", 16, 32), O.mult)
+        ts(A("st1"), A("ui2", 0, 16), 2.0, O.mult, 1.0, O.add)
+        for j in range(2):
+            act(A("st2", 16 * j, 16 * j + 16), A("st1"), F.Identity, scale=2.0)
+        for j in range(2):
+            act(A("st4", 32 * j, 32 * j + 32), A("st2"), F.Identity, scale=2.0)
         ts(A("z", 0, 16), A("pi"), 7, O.arith_shift_right, 2047, O.bitwise_and)
+        cp(A("zu", 0, 16), A("z", 0, 16))
         tt(A("z", 16, 32), A("z", 0, 16), A("st1"), O.add)
-        ts(A("zi2", 0, 32), A("z", 0, 32), 2047, O.bitwise_and)
-        cp(A("zu", 0, 32), A("zi2", 0, 32))
-        late = []
-        for m in range(8):
-            s = 256 * m
-            tt(A("df", s, s + 256), ind(A("tab"), A("zu", 16 * m, 16 * m + 16)), A("aa"), O.subtract)
-            if m == 0:
-                tt(A("z", 32, 64), A("z", 0, 32), A("st2"), O.add)
-                tt(A("z", 64, 128), A("z", 0, 64), A("st4"), O.add)
-                ts(A("zi2", 32, 128), A("z", 32, 128), 2047, O.bitwise_and)
-                cp(A("zu", 32, 128), A("zi2", 32, 128))
-            act(A("ab", s, s + 256), A("df", s, s + 256), F.Abs)
-            while late:
-                z = late.pop()
-                ts(A("rl", z, z + 256), A("ab", z, z + 256), 127.0, O.subtract, 0.0, O.max)
-            if m % 2 == 0:
-                late.append(s)
-            else:
-                act(A("rl", s, s + 256), A("ab", s, s + 256), F.Relu, bias=-127.0)
-            if m % 4 == 3:
-                wsum(P(m // 4, 0, 64), "em", "rl", 256 * m - 768, 256 * m + 256)
-        tt(A("mz"), A("mc"), A("zi2"), O.add)
-        if t == 0:
-            ts(A("tm"), A("xio"), col(0), O.is_le, 0.5, O.mult)
-        if not last:
-            round_v(t + 1)
+
+        def probe(m):
+            tt(A("ne", 256 * m, 256 * m + 256), ind(A("dt"), A("zu", 16 * m, 16 * m + 16)), A("aa"), O.not_equal)
+
+        tt(A("z", 32, 64), A("z", 0, 32), A("st2"), O.add)
+        probe(0)
+        tt(A("z", 64, 128), A("z", 0, 64), A("st4"), O.add)
+        ts(A("zi2"), A("z"), 2047, O.bitwise_and)
+        cp(A("zu", 16, 128), A("zi2", 16, 128))
+        cp(A("z16"), A("zi2"))
         for h in range(2):
-            a, b = 64 * h, 64 * h + 64
-            ts(A("k1", a, b), P(h, 0, 64), 0.5, O.is_gt, 32768.0, O.mult)
-            ts(A("k2", a, b), P(h, 0, 64), 8.4e7, O.is_gt, -16384.0, O.mult)
-            tt(A("k1", a, b), A("k1", a, b), A("mz", a, b), O.add)
-            tt(A("k3", a, b), A("k1", a, b), A("k2", a, b), O.add)
-        tt(A("k4"), A("k3", 0, 64), A("k3", 64, 128), O.min)
+            act(A("sg", 1024 * h, 1024 * h + 1024), ind(A("et"), A("zu", 64 * h, 64 * h + 64)), F.Sign)
+            for m in range(max(4 * h, 1), 4 * h + 4):
+                probe(m)
+            mm(P(h, 0, 64), A("ones", 0, 128, 1, 0, 1), A("mrow", 64 * h, 64 * h + 64, 1, 0, 1), True, False)
+            mm(P(h, 0, 64), A("idb"), A("z16", 64 * h, 64 * h + 64), False, False)
+            for j in range(4):
+                mm(P(h, 16 * j, 16 * j + 16), A("idb"), A("invw"), False, False)
+            wsum(P(h, 0, 64), "es", "sg", 1024 * h, 1024 * h + 1024, False, False)
+            wsum(P(h, 0, 64), "em", "ne", 1024 * h, 1024 * h + 1024, False)
+        act(A("ka"), P(0, 0, 64), F.Copy)
+        if t == 0:
+            ts(A("tm"), A("xio"), col(ROW), O.is_le, 0.5, O.mult)
+        if last:
+            whole(1)
+            whole(2)
+        else:
+            round_v(t + 1)
+        tt(A("k4"), A("ka"), P(1, 0, 64), O.min)
         tt(A("k5"), A("k4", 0, 32), A("k4", 32, 64), O.min)
         tt(A("kmi"), A("k5", 0, 16), A("k5", 16, 32), O.min)
-        ts(A("inv"), A("kmi"), 32768.0, O.is_ge, -4096.0, O.mult)
         ts(A("plc"), A("kmi"), 2047, O.bitwise_and)
-        tt(A("key16"), A("plc"), A("inv"), O.add)
+        ts(A("inv"), A("kmi"), W, O.is_ge, -4096.0, O.mult)
+        cp(A("key16"), A("plc"))
         tt(A("keyw"), A("plc"), A("inv"), O.add)
         cp(A("plu"), A("plc"))
-        mm(P(3, 0, 256), A("blk"), A("zb"), True, False)
+        ts(A("iv2"), A("kmi"), W, O.is_ge)
+        if last:
+            whole(3)
         for r in range(16):
             mm(P(2, r, 256, 16), A("bc", 128 * r, 128 * r + 128), A("key16"))
-        cp(A("oi"), ind(A("tab"), A("plu")))
-        ts(A("oc"), A("oi"), 255, O.bitwise_and)
+        mm(P(3, 0, 256), A("blk"), A("zb"), True, False)
+        tt(A("iv2"), A("iv2"), A("dumpc"), O.mult)
+        tt(A("plc2"), A("iv2"), A("plc"), O.max)
+        tt(A("dd"), A("dumpc"), A("plc2"), O.subtract)
+        act(A("eo"), ind(A("et"), A("plu")), F.Copy)
         for x in range(16):
             act(A("kr", x, 256, 16), A("keyw"), F.Identity, bias=A("tm", x, x + 1))
+        act(A("so"), A("eo"), F.Sign)
         cp(A("kb16"), P(2, 0, 256))
         for c in range(15):
             e = A("eq", 256 * c + 16 * c + 16, 256 * c + 256)
@@ -551,30 +601,32 @@ def rank_program(g, core, T, topo):
             if c == 13:
                 tt(A("dm"), P(2, 0, 256), A("kr"), O.is_equal)
         mm(P(3, 0, 256), A("blk"), A("dm"), False, True)
+        mm(P(5, 0, 256), A("id256"), A("cq"), True, False)
+        mm(P(5, 0, 256), A("idb"), A("eo"), False, False)
+        mm(P(5, 0, 256), A("id128"), A("so"), False, True)
         act(A("lsb"), P(3, 0, 256), F.Copy)
-        tt(A("cs"), A("oc"), A("ac"), O.add)
-        ts(A("cn"), A("cs"), 129.0, O.max, 383.0, O.min)
-        act(A("ent"), A("cn"), F.Abs, bias=-256.0)
+        ts(A("cn"), P(5, 0, 256), -127.0, O.max, 127.0, O.min)
         wsum(P(4, 0, 16), "em", "lsb", 0, 256)
-        tt(A("tg"), A("aam"), A("cn"), O.add)
-        mm(P(5, 0, 256), A("blk"), A("ent"))
-        act(A("es"), P(5, 0, 256), F.Sign, bias=-0.5)
-        tt(A("ls"), A("inv"), P(4, 0, 16), O.subtract)
-        ts(A("ls2"), A("ls"), -0.5, O.is_lt)
-        tt(A("ls"), A("ls2"), A("dumpc"), O.mult)
-        tt(A("fo"), A("ls"), A("plc"), O.max)
+        if last:
+            act(A("en32"), A("cn"), F.Identity, bias=128.0)
+        else:
+            act(A("ent"), A("cn"), F.Abs)
+            act(A("en"), A("cn"), F.Identity, bias=128.0)
+            mm(P(5, 256, 512), A("blk"), A("ent"))
+            act(A("lv"), P(5, 256, 512), F.Sign)
+            act(A("fr"), P(5, 256, 512), F.Relu, bias=128.0, scale=-128.0)
+        tt(A("fo1"), A("dd"), P(4, 0, 16), O.min)
+        tt(A("fo"), A("fo1"), A("plc2"), O.add)
         cp(A("fou"), A("fo"))
-        if not last:
-            cp(ind(A("cab"), A("fou")), A("ent"))
-            cp(A("cab", 2048, 2064), A("cab", 0, 16))
-        tt(A("tn"), A("tg"), A("es"), O.mult)
-        cp(ind(A("tab"), A("fou")), A("tn"))
+        if last:
+            tt(ind(A("yb"), A("fou")), A("aa"), A("en32"), O.add)
+        else:
+            tt(ind(A("et"), A("fou")), A("en"), A("lv"), O.mult)
+            cp(A("et", 2048, DUMMY), A("et", 0, 16))
 
     for c in range(4):
         s = 512 * c
-        act(A("ab", s, s + 512), A("tab", s, s + 512), F.Abs)
-        ts(A("df", s, s + 512), A("ab", s, s + 512), -1.0, O.mult, float(K), O.add)
-        store("y", "out%d" % c, T.y[:, s:s + 512], A("df", s, s + 512))
+        store("ys"[c % 2], "out%d" % c, T.y[:, s:s + 512], A("yb", s, s + 512))
     for c in range(4):
         g.wait_ge(T.sem["out%d" % c], 16)
     g.wait_ge(T.sem.ldh, 16)

@@ -2,7 +2,7 @@ from concourse.bass import DstId, RemoteDMATransfer
 from concourse.mybir import AluOpType as O, ActivationFunctionType as F
 
 RO, STEP, N, CAP = 3, 650, 4, 64
-CH = ((0, 64), (64, 128), (128, 192), (192, 224))
+CUT = 208
 DUMMY, DUMP = 2064, 2832
 TW = DUMP + 256
 W = 32768.0
@@ -13,8 +13,8 @@ F32, B16, H16, I32, U16 = "float32", "bfloat16", "float16", "int32", "uint16"
 
 WIDE = {
     "detb": (DUMMY + 256, I32), "big": (2048, I32), "dt": (TW, F32), "et": (TW, B16), "yb": (TW, F32), "cab": (DUMMY, B16),
-    "hamb": (4096, B16), "ones": (2048, B16), "frb": (2048, B16),
-    "em": (2048, B16), "es": (2048, B16), "e1": (2048, B16), "e2": (2048, B16), "bc": (2048, B16), "rexp": (2048, B16),
+    "hamb": (4096, B16), "ones": (512, B16), "frb": (2048, B16),
+    "em": (2048, B16), "es": (2048, B16), "eb": (2048, B16), "e1": (2048, B16), "e2": (2048, B16), "bc": (2048, B16), "rexp": (2048, B16),
     "lb": (1024, B16), "rvk": (512, B16), "cmp": (2048, B16), "lg": (4096, B16),
     "mn": (4096, B16), "sb0": (1280, F32), "sb1": (1280, F32), "sb2": (1280, F32), "ar0": (256, F32), "ar1": (256, F32),
     "ar2": (256, F32), "ne": (2048, B16), "sg": (2048, B16), "eq": (4096, B16),
@@ -22,13 +22,14 @@ WIDE = {
 SMALL = {
     F32: "pcol 1 cols 32 rr0 128 rr1 128 rr2 128 cw0 8 cw1 8 cw2 8 kscan 272 m64 64 sel15 128 iow 16 iow1 16 xio 16 tm 16 "
          "kr 256 cs32 64 dumpc 16 cneg 8 totu 1 gds 256 t1 256 t2 256 t3 256 t4 256 tv 16 cmpo 64 base 256 term 256 d256 256 "
-         "fr 256 aa 256 st1 16 st2 32 st4 64 ka 64 k4 64 k5 32 inv 16 keyw 16 iv2 16 plc2 16 dd 16 fo1 16 fo 16 en32 256",
+         "fr 256 aa 256 sm 128 ka 64 k4 64 k5 32 inv 16 keyw 16 fo 16 en32 256",
     B16: "blk 128 blka 128 blk592 8 idb 128 idw 128 id128 128 id256 128 shu 128 shd 128 cor 128 tmpb 128 mid 128 gum 128 gdm 128 "
-         "ns0 128 ns1 128 ns2 128 ni0 128 ni1 128 ni2 128 t10 128 t11 128 t12 128 t20 128 t21 128 t22 128 r00 256 r01 256 r02 256 "
+         "nblk 128 dif 128 gq 128 xm 128 code0 128 code 128 "
+         "ns0 128 ns1 128 ns2 128 t10 128 t11 128 t12 128 t20 128 t21 128 t22 128 r00 256 r01 256 r02 256 "
          "negb 256 io0 256 io1 256 a1 128 m128 128 trb 128 mrow 128 zb 256 w12 16 live 128 w 128 wz 128 val 256 abc 256 ct 256 "
          "eg 256 f1 256 ffq 256 sgc 256 fa 256 ef 256 lv 256 ra 256 sd 256 nq 256 oh 64 ohc 64 cq 256 eo 256 so 256 cn 256 "
          "ent 256 en 256 dm 256 lsb 256",
-    H16: "nx 16 nt 16 d16 256 vk16 32 t32 128 ch16 256 mk 64 cs64 64 dmp16 16 a16 256 z16 128 invw 16 key16 16 kb16 256",
+    H16: "nx 16 nt 16 d16 256 vk16 32 t32 128 ch16 256 mk 64 cs64 64 dmp16 16 a16 256 z16 128 invw 16 ivw 16 key16 16 kb16 256",
     I32: "icol 1 icol2 1 icol3 1 ui 32 ui2 32 pi 16 h16 16 km 272 vk 32 own 16 z 128 zi2 128 kmi 16 plc 16",
     U16: "pl 16 du 256 sl 16 zu 128 plu 16 fou 16",
 }
@@ -190,49 +191,12 @@ def rank_program(g, core, T, topo):
 
     one = lambda w: A("ones", 0, w)
     col = lambda j: A("cols", j, j + 1)
-    ROW, R15, LO, HI, W1, W2, W1S, W2S, BMB, BRA, UP, DOWN, ALT, TMP, TMP2 = range(15)
+    ROW, G16, R15, LO, HI, W1, W2, BMB, BRA, UP, DOWN, ALT, TMP, TMP2, NML = range(15)
 
     pw = 2048 // NP
     for c in range(NP):
         load("y", "ld%d" % c, A("detb", pw * c, pw * c + pw), T.det[:, pw * c:pw * c + pw])
     load("y", "ldh", A("hamb"), T.ham[:, :])
-
-    fill(A("ones", 0, 272), 1.0)
-    iota(A("icol"), [[0, 1]], 0, 1)
-    sel(A("tmpb"), one(128), [[-16, 8], [0, 16]], O.is_ge, 0.0, 0, 1)
-    sel(A("blk"), A("tmpb"), [[16, 8], [0, 16]], O.is_ge, 0.0, 15, -1)
-    sel(A("idb"), one(128), [[-1, 128]], O.is_equal, 0.0, 0, 1)
-    sel(A("shu"), one(128), [[-1, 128]], O.is_equal, 0.0, -1, 1)
-    sel(A("cor"), one(128), [[-1, 128]], O.is_equal, 0.0, 127, 1)
-    sel(A("m128"), one(128), [[0, 8], [1, 16]], O.not_equal, 0.0, 0, 0)
-    fill(A("em"), 0.0)
-    fill(A("negb"), -1.0)
-    ts(A("icol2"), A("icol"), 15, O.bitwise_and)
-    ts(A("icol3"), A("icol"), 1, O.bitwise_and)
-    cp(A("pcol"), A("icol"))
-    fill(A("lb"), 0.0)
-    cp(col(ROW), A("icol2"))
-    ts(col(ALT), A("icol3"), -2.0, O.mult, 1.0, O.add)
-    fill(A("et", 2048, TW), 128.0)
-    ts(col(R15), col(ROW), 15.0, O.is_equal)
-    ts(col(W1), col(ROW), 13.0, O.mult, 5.0, O.add)
-    ts(col(W2), col(ROW), -14.0, O.mult, 255.0, O.add)
-    ts(col(BMB), col(ROW), -8192.0, O.mult, -8192.0 * 2032, O.add)
-    ts(col(BRA), col(ROW), 8192.0, O.mult, 8192.0 * 2034, O.add)
-    ts(col(DOWN), col(ROW), 0.0, O.is_equal, 8192.0, O.mult)
-    ts(col(LO), col(R15), -4000.0, O.mult)
-    ts(col(HI), col(R15), 3999.0, O.mult, 1.0, O.add)
-    ts(col(UP), col(R15), -8192.0, O.mult)
-    ts(col(W1S), col(W1), 1.0 / W, O.mult)
-    ts(col(W2S), col(W2), 1.0 / W, O.mult)
-    fill(A("detb", 2048, DUMMY + 256), 128)
-    tt(A("tmpb"), A("idb"), A("shu"), O.subtract)
-    ts(A("mid"), A("idb"), -1.0, O.mult)
-    tt(A("tmpb"), A("tmpb"), A("cor"), O.subtract)
-    for r in range(16):
-        act(A("em", 128 * r + r, 128 * r + 128, 16), A("blk", 0, 128, 16), F.Identity, scale=W)
-    act(A("idw"), A("idb"), F.Identity, scale=W)
-    act(A("e1"), A("em"), F.Identity, scale=col(W1S))
 
     def chunk(t):
         m0 = STEP * (t + 1) // 16
@@ -244,24 +208,77 @@ def rank_program(g, core, T, topo):
         iota(A(rr, 0, ml), [[1, ml]], 128, 0)
         iota(A(rr, m0, 128), [[1, 128 - m0]], m0, 0)
         iota(A(rr, ml, m0), [[0, 1]], 126, 0)
+        sel(A("cw%d" % t), one(8), [[0, 8]], O.not_equal, -128.0, -ml, 1)
         sel(A("t2%d" % t), one(128), [[200, 128]], O.is_equal, 0.0, -127 - 200 * ml, 1)
         sel(A("ns%d" % t), A("tmpb"), [[1, 128]], O.not_equal, 0.0, -ml, 0)
-        sel(A("ni%d" % t), A("mid"), [[1, 128]], O.not_equal, 0.0, -ml, 0)
-        sel(A("cw%d" % t), one(8), [[0, 8]], O.not_equal, -128.0, -ml, 1)
         sel(A("r0%d" % t), A("negb"), [[0, 256]], O.is_equal, 0.0, -m0, 1)
 
     def round_v(t):
         m0, ml = chunk(t)
         ts(col(TMP), A("pcol"), float(m0), O.is_lt, 128.0, O.mult)
+        ts(col(NML), A("pcol"), float(ml), O.not_equal, -1.0, O.mult)
+        ts(A("lb", 15, 1024, 144), A("cw%d" % t), 16.0, O.mult)
         tt(col(TMP2), col(TMP), A("pcol"), O.add)
         ts(A("t1%d" % t), A("rr%d" % t), col(TMP2), O.is_ge)
-        ts(A("lb", 15, 1024, 144), A("cw%d" % t), 16.0, O.mult)
 
-    iota(A("io0"), [[1, 256]], 0, 0)
+    def spread(name, weight, r0, r1):
+        for r in range(r0, r1):
+            ts(A(name, 128 * r, 128 * r + 128), A("code"), float(r), O.is_equal, weight, O.mult)
+
+    iota(A("icol"), [[0, 1]], 0, 1)
+    iota(A("dif"), [[1, 128]], 0, -1)
+    iota(A("gq"), [[16, 8], [0, 16]], 0, 0)
+    iota(A("code0"), [[-16, 8], [1, 16]], 0, 0)
+    iota(A("xm"), [[0, 8], [1, 16]], 0, 0)
+    fill(A("ones"), 1.0)
+    fill(A("negb"), -1.0)
+    ts(A("icol2"), A("icol"), 15, O.bitwise_and)
+    ts(A("icol3"), A("icol"), 1, O.bitwise_and)
+    cp(A("pcol"), A("icol"))
+    cp(col(ROW), A("icol2"))
+    ts(col(ALT), A("icol3"), -2.0, O.mult, 1.0, O.add)
+    ts(A("idb"), A("dif"), 0.0, O.is_equal)
+    ts(A("shu"), A("dif"), -1.0, O.is_equal)
+    ts(A("cor"), A("dif"), 127.0, O.is_equal)
+    tt(col(G16), A("pcol"), col(ROW), O.subtract)
+    ts(col(R15), col(ROW), 15.0, O.is_equal)
+    tt(A("tmpb"), A("idb"), A("shu"), O.subtract)
+    ts(col(W1), col(ROW), 13.0, O.mult, 5.0, O.add)
+    ts(col(W2), col(ROW), -14.0, O.mult, 255.0, O.add)
+    ts(A("blk"), A("gq"), col(G16), O.is_equal)
+    tt(A("tmpb"), A("tmpb"), A("cor"), O.subtract)
+    ts(A("code"), A("code0"), col(G16), O.add)
+    ts(col(LO), col(R15), -4000.0, O.mult)
+    ts(col(HI), col(R15), 3999.0, O.mult, 1.0, O.add)
+    ts(A("m128"), A("xm"), 0.0, O.not_equal)
+    ts(A("a1"), A("xm"), 15.0, O.not_equal)
+    spread("em", W, 0, 16)
+    for j in range(2):
+        act(A("lb", 512 * j, 512 * j + 512), one(512), F.Identity, scale=0.0)
+    for k in range(16):
+        act(A("rexp", k, 2048, 16), A("idb"), F.Copy)
+    act(A("idw"), A("idb"), F.Identity, scale=W)
+    act(A("mid"), A("idb"), F.Identity, scale=-1.0)
+    act(A("id128"), A("idb"), F.Identity, scale=-128.0)
+    act(A("id256"), A("idb"), F.Identity, scale=256.0)
+    act(A("zb"), one(256), F.Identity, scale=0.0)
+    act(A("sel15"), A("blk"), F.Identity, scale=col(R15))
+    act(A("blka"), A("blk"), F.Identity, scale=col(ALT))
+    act(A("nblk"), A("blk"), F.Identity, scale=-1.0)
+    act(A("blk592"), A("blk", 0, 128, 16), F.Identity, scale=592.0)
+    act(A("w12", 0, 8), A("blk", 0, 128, 16), F.Identity, scale=col(W1))
+    act(A("w12", 8, 16), A("blk", 0, 128, 16), F.Identity, scale=col(W2))
     round_g(0)
-    sel(A("a1"), one(128), [[0, 8], [1, 16]], O.not_equal, 0.0, -15, 0)
+    iota(A("io0"), [[1, 256]], 0, 0)
     iota(A("io1"), [[1, 256]], 1, 0)
     iota(A("iow"), [[16, 16]], 0, 0)
+    iota(A("detb", 2048, DUMMY + 256), [[0, DUMMY + 256 - 2048]], 128, 0)
+    iota(A("et", 2048, TW), [[0, TW - 2048]], 128, 0)
+
+    def free_mark(c):
+        s = 512 * c
+        mm(P(6 + c % 2, 0, 512), A("blk"), A("cab", s, s + 512))
+        act(A("frb", s, s + 512), P(6 + c % 2, 0, 512), F.Relu, bias=1.0, scale=-1.0)
 
     for c in range(NP):
         s = pw * c
@@ -272,39 +289,39 @@ def rank_program(g, core, T, topo):
         act(A("cab", s, s + pw), A("et", s, s + pw), F.Abs, bias=-128.0)
         if c == 0:
             act(A("cab", 2048, DUMMY), A("cab", 0, 16), F.Copy)
-            fill(A("ones", 272, 2048), 1.0)
+        if c < 2:
+            free_mark(c)
 
-    def free_mark(c):
+    def mark(c, b, part):
         s = 512 * c
-        mm(P(6 + c % 2, 0, 512), A("blk"), A("cab", s, s + 512))
-        act(A("frb", s, s + 512), P(6 + c % 2, 0, 512), F.Relu, bias=1.0, scale=-1.0)
+        if part == 0:
+            mm(P(b, 0, 512), A("idb"), A("et", s, s + 512), True, False)
+            mm(P(b, 0, 512), A("id128"), A("frb", s, s + 512), False, True)
+        else:
+            tt(A("dt", s, s + 512), A("detb", s, s + 512), P(b, 0, 512), O.subtract)
+            act(A("et", s, s + 512), P(b, 0, 512), F.Copy)
 
     def rest_g():
-        sel(A("rexp"), one(2048), [[-1, 128], [0, 16]], O.is_equal, 0.0, 0, 1)
+        sel(A("gum"), A("tmpb"), [[0, 8], [1, 16]], O.not_equal, 0.0, -15, 0)
+        sel(A("shd"), A("idb"), [[1, 128]], O.not_equal, -1.0, -1, -1)
+        sel(A("gdm"), A("shd"), [[0, 8], [1, 16]], O.not_equal, 0.0, 0, 0)
         sel(A("kscan"), one(272), [[0, 16], [1, 17]], O.not_equal, -3.0e7, 0, 0)
-        sel(A("shd"), one(128), [[-1, 128]], O.is_equal, 0.0, 1, 1)
-        sel(A("rvk"), one(512), [[-8, 4], [-1, 8], [0, 16]], O.is_equal, 0.0, 0, 1)
-        sel(A("trb"), A("blk"), [[-1, 128]], O.is_ge, 0.0, 0, 1)
-        sel(A("m64"), one(64), [[0, 4], [1, 16]], O.not_equal, 0.0, 0, 0)
+        sel(A("rvk", 0, 256), A("negb"), [[-8, 2], [-1, 8], [0, 16]], O.is_equal, 0.0, 0, 1)
+        sel(A("rvk", 256, 512), one(256), [[-8, 2], [-1, 8], [0, 16]], O.is_equal, 0.0, -16, 1)
         iota(A("cs32"), [[256, 4], [-16, 16]], -1024, 0)
-        iota(A("mrow"), [[2048, 8], [0, 16]], -31 * 16384, 0)
-        iota(A("xio"), [[1, 16]], 0, 0)
+        sel(A("m64"), one(64), [[0, 4], [1, 16]], O.not_equal, 0.0, 0, 0)
+        sel(A("trb"), A("nblk"), [[-1, 128]], O.is_ge, 0.0, 0, 1)
         iota(A("sb0"), [[0, 1280]], NONE, 0)
         iota(A("dt", 2048, TW), [[0, TW - 2048]], 0, 0)
+        iota(A("mrow"), [[2048, 8], [0, 16]], -31 * 16384, 0)
+        iota(A("xio"), [[1, 16]], 0, 0)
 
     def rest_v():
-        ts(A("blk592"), A("blk", 0, 128, 16), 592.0, O.mult)
-        ts(A("w12", 0, 8), A("blk", 0, 128, 16), col(W1), O.mult)
-        ts(A("w12", 8, 16), A("blk", 0, 128, 16), col(W2), O.mult)
-        fill(A("zb"), 0.0)
-        ts(A("dumpc"), A("iow"), float(DUMP), O.add)
+        ts(col(DOWN), col(ROW), 0.0, O.is_equal, 8192.0, O.mult)
+        ts(col(UP), col(R15), -8192.0, O.mult)
+        ts(col(BMB), col(ROW), -8192.0, O.mult, -8192.0 * 2032, O.add)
+        ts(col(BRA), col(ROW), 8192.0, O.mult, 8192.0 * 2034, O.add)
         ts(A("dmp16"), A("iow"), 1024.0, O.add)
-
-    def rest_v2():
-        tt(A("gum"), A("idb"), A("shu"), O.subtract)
-        tt(A("gdm"), A("idb"), A("shd"), O.subtract)
-        tt(A("gum"), A("gum"), A("a1"), O.mult)
-        tt(A("gdm"), A("gdm"), A("m128"), O.mult)
 
     def whash(src, between=None):
         for e in range(2):
@@ -317,6 +334,9 @@ def rank_program(g, core, T, topo):
         for r in range(16):
             mm(out, A(weights, 128 * r, 128 * r + 128), A(src, c0 + r, c1, 16), start and r == 0, stop and r == 15)
 
+    def enter_d(h):
+        tt(ind(A("dt"), A("fou", 8 * h, 8 * h + 8)), A("aa", 128 * h, 128 * h + 128), A("fr", 128 * h, 128 * h + 128), O.add)
+
     for t in range(RO):
         start = STEP * (t + 1)
         m0, off = start // 16, start % 16
@@ -326,22 +346,24 @@ def rank_program(g, core, T, topo):
             mm(P(0, u, 128, 16), A("et" if t else "cab", off + u, off + u + 2033, 16), A("blk", 0, 128, 16))
         mm(P(3, 0, 256), A("a1", 0, 128, 1, 0, 1), A("io1", 0, 256, 1, 0, 1), True, False)
         if t == 0:
-            free_mark(0)
+            free_mark(2)
+            ts(A("iow"), A("iow"), col(ROW), O.add)
+            spread("e1", col(W1), 0, 8)
+        else:
+            enter_d(0)
         ts(A("live"), P(0, 0, 128), 0.5, O.is_gt)
         scan(A("w"), A("m128"), A("live"), O.mult, O.add)
+        ts(A("cneg"), A("w", 15, 128, 16), col(NML), O.mult)
         if t == 0:
-            ts(A("sel15"), A("blk"), col(R15), O.mult)
-            ts(A("iow"), A("iow"), col(ROW), O.add)
             ts(A("iow1"), A("iow"), 1.0, O.add)
+            ts(A("dumpc"), A("iow"), float(DUMP), O.add)
         mm(P(1, 0, 8), A("t1%d" % t), A("w", 15, 128, 16), True, False)
         mm(P(1, 0, 8), A("t2%d" % t), A("w", 15 - off, 128, 16), False, True)
-        mm(P(2, 128, 136), A("ni%d" % t), A("w", 15, 128, 16))
         mm(P(2, 0, 128), A("ns%d" % t), A("w"))
         mm(P(5, 0, 1), A("w"), A("ones", 0, 1))
         sel(A("wz"), A("w"), [[0, 8], [1, 16]], O.not_equal, 0.0, -15, 0)
         if t == 0:
             rest_g()
-        act(A("cneg"), P(2, 128, 136), F.Copy)
         for h in range(8):
             ts(A("cmp", 256 * h, 256 * h + 256), A("io0"), P(1, h, h + 1), O.is_ge)
             act(A("lb", 144 * h, 144 * h + 15), P(2, 16 * h, 16 * h + 15), F.Identity, bias=A("cneg", h, h + 1))
@@ -355,13 +377,15 @@ def rank_program(g, core, T, topo):
         ts(A("nt"), A("iow"), P(5, 1, 2), O.is_ge, float(dummy - start), O.mult)
         mm(P(4, 0, 16), A("idw"), A("nx"), True, False)
         mm(P(4, 0, 16), A("idw"), A("nt"), False, False)
+        if t == 0:
+            free_mark(3)
         ts(A("val"), P(3, 0, 256), col(LO), O.max, col(HI), O.min)
         wsum(P(4, 0, 16), "em", "val", 0, 256, False)
         if t == 0:
-            free_mark(1)
             rest_v()
+            spread("e1", col(W1), 8, 13)
         else:
-            tt(ind(A("dt"), A("fou")), A("aa"), A("fr"), O.add)
+            enter_d(1)
         ts(A("pl"), P(4, 0, 16), 1.0 / W, O.mult, float(16 * m0 + off), O.add)
         if t == 0:
             ts(A("du"), ind(A("detb"), A("pl")), 1.0 / 256, O.mult, -0.5, O.add)
@@ -370,67 +394,73 @@ def rank_program(g, core, T, topo):
         act(A("abc"), ind(A("et"), A("pl")), F.Abs, bias=-128.0)
         for h in range(2):
             mm(P(7, 128 * h, 128 * h + 128), A("abc", 128 * h, 128 * h + 128), A("idb"))
-        for a, b in CH:
+        for a in range(0, CUT, 32):
+            b = min(a + 32, CUT)
             act(A("lg", 16 * a, 16 * b), ind(A("hamb"), A("du", a, b)), F.Copy)
         ts(A("d16"), A("du"), 2048.0, O.subtract)
         cp(A("ct"), P(7, 0, 256))
-        if t == 0:
-            rest_v2()
+        cp(A("lg", 16 * CUT, 4096), ind(A("hamb"), A("du", CUT, 256)))
+        order = [7, 0, 1, 2, 3, 4, 5, 6]
+
+        def rep(j):
+            b = order[j]
+            mm(P(j % 4, 0, 512), A("ct", 128 * (b // 4), 128 * (b // 4) + 128), A("rexp", 512 * (b % 4), 512 * (b % 4) + 512))
+
+        rep(0)
+        rep(1)
         for h in range(2):
             for e in range(2):
                 mm(P(4, 16 * e + 8 * h, 16 * e + 8 * h + 8), A("d16", 128 * h, 128 * h + 128), A("w12", 8 * e, 8 * e + 8))
-
-        def rep(b):
-            mm(P(b % 4, 0, 512), A("ct", 128 * (b // 4), 128 * (b // 4) + 128), A("rexp", 512 * (b % 4), 512 * (b % 4) + 512))
-
-        for b in range(4):
-            rep(b)
+        rep(2)
+        rep(3)
         mm(P(7, 0, 256), A("gum"), A("d16"))
         mm(P(7, 256, 512), A("gdm"), A("d16"))
         mm(P(5, 0, 256), A("idb"), A("d16"))
         mm(P(6, 16, 272, 17), A("zb", 0, 128), A("blk", 0, 16))
-        cp(A("ui"), P(4, 0, 32))
-        ts(A("ui2"), A("ui"), 4095, O.bitwise_and)
-        cp(A("lg", 3584, 4096), ind(A("hamb"), A("du", 224, 256)))
-        tt(A("pi"), A("ui2", 0, 16), A("ui2", 16, 32), O.mult)
 
         def kmax(h):
             scan(A("km", 136 * h, 136 * h + 136), A("kscan", 136 * h, 136 * h + 136), P(6, 136 * h, 136 * h + 136), O.add, O.max)
 
-        for b in range(8):
+        for j in range(8):
+            b = order[j]
             s = 512 * b
-            tt(A("mn", s, s + 512), A("lg", s, s + 512), P(b % 4, 0, 512), O.min)
-            if b == 0:
+            tt(A("mn", s, s + 512), A("lg", s, s + 512), P(j % 4, 0, 512), O.min)
+            if j == 0:
+                cp(A("ui"), P(4, 0, 32))
+            if j == 1:
+                ts(A("ui2"), A("ui"), 4095, O.bitwise_and)
+            if j == 2:
+                tt(A("pi"), A("ui2", 0, 16), A("ui2", 16, 32), O.mult)
+            if j == 3:
                 ts(A("h16"), A("pi"), 1, O.arith_shift_right, 0x7FFFFFF0, O.bitwise_and)
-            if b == 1:
+            if j == 4:
                 ts(A("kscan", 16, 272, 17), A("h16"), float(16 * t), O.add)
-            if b < 4:
-                rep(b + 4)
-            if b == 5:
-                kmax(0)
-            if b % 4 == 3:
+            if j < 4:
+                rep(j + 4)
+            if b in (3, 6):
                 h = b // 4
                 for k in range(16):
                     mm(P(6, 136 * h + k, 136 * h + 136, 17), A("mn", 2048 * h + k, 2048 * h + 2048, 16), A("blk592"))
-        act(P(7, 0, 256), P(7, 0, 256), F.Identity, bias=col(UP))
         act(A("gds"), P(7, 256, 512), F.Identity, bias=col(DOWN))
+        act(P(7, 0, 256), P(7, 0, 256), F.Identity, bias=col(UP))
         act(A("eg"), ind(A("et"), A("pl")), F.Copy)
         act(A("fa"), A("abc"), F.Relu, bias=-1.0)
-        act(A("sgc"), A("eg"), F.Sign, bias=-128.0)
         act(A("d256"), P(5, 0, 256), F.Identity, bias=2048.0 * 256, scale=256.0)
+        act(A("sgc"), A("eg"), F.Sign, bias=-128.0)
         act(A("f1"), A("eg"), F.Identity, bias=159.625, scale=0.25)
-        act(A("ffq"), A("f1"), F.Identity, bias=-0.75, scale=1.0 / 256)
+        kmax(0)
         if t == 0:
-            ts(A("rvk", 0, 256), A("rvk", 0, 256), -1.0, O.mult)
-            ts(A("trb"), A("trb"), -1.0, O.mult)
-            ts(A("blka"), A("blk"), col(ALT), O.mult)
             ts(A("cs64"), A("cs32"), col(ROW), O.subtract)
+            spread("e1", col(W1), 13, 16)
+            spread("e2", col(W2), 0, 3)
         kmax(1)
         ts(A("vk", 0, 16), A("km", 16, 272, 17), 4, O.arith_shift_right, 4095, O.bitwise_and)
         ts(A("vk", 16, 32), A("km", 16, 272, 17), 15, O.bitwise_and)
         ts(A("vk16"), A("vk"), 2048.0, O.subtract)
         mm(P(2, 256, 512), A("blk"), A("fa"))
         mm(P(4, 0, 128, 1, 0, 32), A("vk16"), A("idb"))
+        if t == 0:
+            spread("e2", col(W2), 3, 8)
         cp(A("t32", 0, 128, 1, 0, 32), P(4, 0, 128, 1, 0, 32))
         for h in range(2):
             s = 128 * h
@@ -439,37 +469,48 @@ def rank_program(g, core, T, topo):
         for h in range(2):
             s = 128 * h
             mm(P(1, s, s + 128), A("rvk", 256 + s, 256 + s + 128, 1, 0, 32), A("t32", 0, 128, 1, 0, 32))
+        if t == 0:
+            spread("e2", col(W2), 8, 13)
         act(A("lv"), P(2, 256, 512), F.Sign)
         act(A("fr"), P(2, 256, 512), F.Relu, bias=128.0, scale=-128.0)
-        tt(A("t1"), A("gds"), P(0, 0, 256), O.min)
+
+        def halves(out, a, b, op):
+            for s in (0, 128):
+                tt(*[P(x, s, s + 128) if isinstance(x, int) else A(x, s, s + 128) for x in (out, a, b)], op)
+
+        halves("t1", "gds", 0, O.min)
         act(P(2, 0, 256), P(1, 0, 256), F.Relu, bias=col(BMB), scale=-8192.0)
         act(A("ra"), P(1, 0, 256), F.Relu, bias=col(BRA), scale=8192.0)
         act(A("sd"), P(0, 0, 256), F.Sign, scale=col(ALT))
-        tt(A("t2"), A("t1"), P(7, 0, 256), O.max)
+        act(A("ffq"), A("f1"), F.Identity, bias=-0.75, scale=1.0 / 256)
+        halves("t2", "t1", 7, O.max)
         mm(P(4, 0, 256), A("idb"), A("d16"), True, False)
         mm(P(4, 0, 256), A("idb"), A("ra"), False, True)
         mm(P(3, 0, 16), A("idw"), A("nt"), True, False)
         wsum(P(3, 0, 16), "em", "sd", 0, 256, False)
-        mm(P(7, 0, 256), A("idb"), A("eg"), True, False)
-        mm(P(7, 0, 256), A("mid"), A("sgc"), False, True)
-        tt(A("t3"), A("t2"), P(2, 0, 256), O.min)
-        tt(A("t4"), P(5, 0, 256), A("t3"), O.subtract)
-        tt(A("ch16"), A("t4"), P(4, 0, 256), O.min)
+        halves("t3", "t2", 2, O.min)
+        halves("t4", 5, "t3", O.subtract)
+        halves("ch16", "t4", 4, O.min)
         act(A("tv"), P(3, 0, 16), F.Abs, bias=1.0, scale=1.0 / W)
         for o in range(4):
             act(A("cmpo", 16 * o, 16 * o + 16), A("tv"), F.Identity, bias=-1.0, scale=o + 1.0)
-        act(A("ef"), P(7, 0, 256), F.Copy)
         if t == 0:
-            act(A("e2"), A("em"), F.Identity, scale=col(W2S))
+            spread("e2", col(W2), 13, 16)
         tt(A("nq"), A("ch16"), P(5, 0, 256), O.not_equal)
-        whash("ch16", lambda: mm(P(1, 0, 256), A("blka"), A("nq")))
-        act(P(1, 0, 256), P(1, 0, 256), F.Abs, scale=2.0)
-        mm(P(0, 0, 256), A("idb"), A("ch16"), True, False)
-        mm(P(0, 0, 256), A("mid"), A("ffq"), False, True)
+        whash("ch16")
+        mm(P(5, 256, 512), A("blka"), A("nq"))
+        act(P(5, 256, 512), P(5, 256, 512), F.Abs, scale=2.0)
+        mm(P(7, 256, 512), A("idb"), A("ch16"), True, False)
+        mm(P(7, 256, 512), A("mid"), A("ffq"), False, True)
         mm(P(4, 0, 64), A("idb"), A("cs64"), True, False)
         mm(P(3, 0, 16), A("idb"), A("dmp16"), True, False)
-        act(A("base"), P(0, 0, 256), F.Copy)
-        tt(A("term"), A("ffq"), P(1, 0, 256), O.mult)
+        mm(P(2, 0, 256), A("idb"), A("eg"), True, False)
+        mm(P(2, 0, 256), A("mid"), A("sgc"), False, True)
+        act(A("base"), P(7, 256, 512), F.Copy)
+        act(A("ef"), P(2, 0, 256), F.Copy)
+        if t == 0:
+            mark(0, 1, 0)
+            act(A("es"), A("em"), F.Identity, scale=31.0 / 32)
         cp(A("ui"), P(6, 0, 32))
         ts(A("ui2"), A("ui"), 4095, O.bitwise_and)
         tt(A("pi"), A("ui2", 0, 16), A("ui2", 16, 32), O.mult)
@@ -477,11 +518,14 @@ def rank_program(g, core, T, topo):
         for o in range(4):
             tt(A("oh", 16 * o, 16 * o + 16), A("own"), A("cmpo", 16 * o, 16 * o + 16), O.is_equal)
         scan(A("ohc"), A("m64"), A("oh"), O.mult, O.add)
+        tt(A("term"), A("ffq"), P(5, 256, 512), O.mult)
         mm(P(4, 0, 64), A("trb"), A("oh"), False, False)
         mm(P(4, 0, 64), A("blk"), A("ohc"), False, True)
         tt(A("mk"), A("oh"), P(4, 0, 64), O.mult)
         for o in range(4):
             mm(P(3, 0, 16), A("idb"), A("mk", 16 * o, 16 * o + 16), False, o == 3)
+        if t == 0:
+            ts(A("tm"), A("xio"), col(ROW), O.is_gt)
         cp(A("sl"), P(3, 0, 16))
         sb, ar, arr = "sb%d" % t, "ar%d" % t, "arr%d" % t
         tt(ind(A(sb), A("sl")), A("base"), A("term"), O.add)
@@ -494,27 +538,26 @@ def rank_program(g, core, T, topo):
         g.remote_dma_fused(trs, local_sem=T.sem.sent)
         got = sum(len(es) for q in range(N) if q != rank for o, es in plan(topo, T.cores, q) if o == rank)
         if t == 0:
-            sel(A("bc"), one(2048), [[-1, 16], [-16, 8], [0, 16]], O.is_equal, 0.0, 0, 1)
+            for j in range(4):
+                sel(A("bc", 512 * j, 512 * j + 512), one(512), [[-1, 4], [-16, 8], [0, 16]], O.is_equal, 0.0, -4 * j, 1)
         if not last:
             round_g(t + 1)
             iota(A("sb%d" % (t + 1)), [[0, 1280]], NONE, 0)
-        if t == 1:
+        if t == RO - 2:
             iota(A("yb", 2048, TW), [[0, TW - 2048]], 0, 0)
-        cp(A(ar, 64 * rank, 64 * rank + 64), A(sb, 256 * rank, 256 * rank + 64))
+        act(A(ar, 64 * rank, 64 * rank + 64), A(sb, 256 * rank, 256 * rank + 64), F.Copy)
         if t == 0:
-            act(A("id128"), A("idb"), F.Identity, scale=-128.0)
-            act(A("id256"), A("idb"), F.Identity, scale=256.0)
-            free_mark(2)
-            free_mark(3)
-            for c in range(4):
-                s, b = 512 * c, (0, 1, 2, 5)[c]
-                mm(P(b, 0, 512), A("idb"), A("et", s, s + 512), True, False)
-                mm(P(b, 0, 512), A("id128"), A("frb", s, s + 512), False, True)
-                tt(A("dt", s, s + 512), A("detb", s, s + 512), P(b, 0, 512), O.subtract)
-                act(A("et", s, s + 512), P(b, 0, 512), F.Copy)
+            mark(1, 0, 0)
+            mark(2, 2, 0)
+            mark(3, 7, 0)
+            mark(0, 1, 1)
+            mark(1, 0, 1)
+            mark(2, 2, 1)
+            mark(3, 7, 1)
             tt(ind(A("dt"), A("pl")), A("d256"), A("fr"), O.add)
             tt(ind(A("et"), A("pl")), A("ef"), A("lv"), O.mult)
-            act(A("es"), A("em"), F.Identity, scale=31.0 / 32)
+            for x in range(16):
+                act(A("eb", 128 * x, 128 * x + 128), A("em", 128 * x, 128 * x + 128), F.Identity, scale=A("tm", x, x + 1))
         else:
             tt(ind(A("et"), A("pl")), A("ef"), A("lv"), O.mult)
             tt(ind(A("dt"), A("pl")), A("d256"), A("fr"), O.add)
@@ -526,49 +569,62 @@ def rank_program(g, core, T, topo):
         if last:
             for c in range(4):
                 mm(P(2 + c, 0, 512), A("idb"), A("et", 512 * c, 512 * c + 512))
+            whole(0)
+            whole(1)
         ts(A("a16"), A(ar), BIG, O.add, BIG, O.subtract, extra=[(arr, got)])
         whash("a16")
         ts(A("aa"), A("a16"), 256.0, O.mult, 2048.0 * 256, O.add)
         tt(A("cq"), A(ar), A("a16"), O.subtract)
-        if last:
-            whole(0)
         cp(A("ui"), P(6, 0, 32))
         ts(A("ui2"), A("ui"), 4095, O.bitwise_and)
         ts(A("invw"), A("ui", 0, 16), 4.0e6, O.is_gt, W, O.mult)
         tt(A("pi"), A("ui2", 0, 16), A("ui2", 16, 32), O.mult)
-        ts(A("st1"), A("ui2", 0, 16), 2.0, O.mult, 1.0, O.add)
-        for j in range(2):
-            act(A("st2", 16 * j, 16 * j + 16), A("st1"), F.Identity, scale=2.0)
-        for j in range(2):
-            act(A("st4", 32 * j, 32 * j + 32), A("st2"), F.Identity, scale=2.0)
-        ts(A("z", 0, 16), A("pi"), 7, O.arith_shift_right, 2047, O.bitwise_and)
-        cp(A("zu", 0, 16), A("z", 0, 16))
-        tt(A("z", 16, 32), A("z", 0, 16), A("st1"), O.add)
+        ts(A("sm", 16, 32), A("ui2", 0, 16), 2.0, O.mult, 1.0, O.add)
+        ts(A("sm", 32, 48), A("ui2", 0, 16), 4.0, O.mult, 2.0, O.add)
+        ts(A("sm", 48, 64), A("ui2", 0, 16), 6.0, O.mult, 3.0, O.add)
+        for m in range(4, 8):
+            act(A("sm", 16 * m, 16 * m + 16), A("sm", 16, 32), F.Identity, scale=float(m))
+        ts(A("zi2", 0, 16), A("pi"), 7, O.arith_shift_right, 2047, O.bitwise_and)
+        cp(A("zu", 0, 16), A("zi2", 0, 16))
 
         def probe(m):
             tt(A("ne", 256 * m, 256 * m + 256), ind(A("dt"), A("zu", 16 * m, 16 * m + 16)), A("aa"), O.not_equal)
 
-        tt(A("z", 32, 64), A("z", 0, 32), A("st2"), O.add)
-        probe(0)
-        tt(A("z", 64, 128), A("z", 0, 64), A("st4"), O.add)
-        ts(A("zi2"), A("z"), 2047, O.bitwise_and)
-        cp(A("zu", 16, 128), A("zi2", 16, 128))
-        cp(A("z16"), A("zi2"))
-        for h in range(2):
-            act(A("sg", 1024 * h, 1024 * h + 1024), ind(A("et"), A("zu", 64 * h, 64 * h + 64)), F.Sign)
-            for m in range(max(4 * h, 1), 4 * h + 4):
-                probe(m)
+        def steps(m0, m1):
+            for m in range(m0, m1):
+                tt(A("z", 16 * m, 16 * m + 16), A("zi2", 0, 16), A("sm", 16 * m, 16 * m + 16), O.add)
+
+        def free_at(m0, m1):
+            act(A("sg", 256 * m0, 256 * m1), ind(A("et"), A("zu", 16 * m0, 16 * m1)), F.Sign)
+
+        def keys(h):
             mm(P(h, 0, 64), A("ones", 0, 128, 1, 0, 1), A("mrow", 64 * h, 64 * h + 64, 1, 0, 1), True, False)
-            mm(P(h, 0, 64), A("idb"), A("z16", 64 * h, 64 * h + 64), False, False)
             for j in range(4):
                 mm(P(h, 16 * j, 16 * j + 16), A("idb"), A("invw"), False, False)
+            mm(P(h, 0, 64), A("idb"), A("z16", 64 * h, 64 * h + 64), False, False)
             wsum(P(h, 0, 64), "es", "sg", 1024 * h, 1024 * h + 1024, False, False)
             wsum(P(h, 0, 64), "em", "ne", 1024 * h, 1024 * h + 1024, False)
+
+        free_at(0, 1)
+        steps(1, 4)
+        ts(A("zi2", 16, 64), A("z", 16, 64), 2047, O.bitwise_and)
+        probe(0)
+        cp(A("zu", 16, 64), A("zi2", 16, 64))
+        steps(4, 8)
+        free_at(1, 4)
+        ts(A("zi2", 64, 128), A("z", 64, 128), 2047, O.bitwise_and)
+        probe(1)
+        cp(A("zu", 64, 128), A("zi2", 64, 128))
+        cp(A("z16"), A("zi2"))
+        free_at(4, 8)
+        probe(2)
+        probe(3)
+        keys(0)
+        for m in range(4, 8):
+            probe(m)
+        keys(1)
         act(A("ka"), P(0, 0, 64), F.Copy)
-        if t == 0:
-            ts(A("tm"), A("xio"), col(ROW), O.is_le, 0.5, O.mult)
         if last:
-            whole(1)
             whole(2)
         else:
             round_v(t + 1)
@@ -577,52 +633,50 @@ def rank_program(g, core, T, topo):
         tt(A("kmi"), A("k5", 0, 16), A("k5", 16, 32), O.min)
         ts(A("plc"), A("kmi"), 2047, O.bitwise_and)
         ts(A("inv"), A("kmi"), W, O.is_ge, -4096.0, O.mult)
+        ts(A("ivw"), A("kmi"), W, O.is_ge, W, O.mult)
         cp(A("key16"), A("plc"))
-        tt(A("keyw"), A("plc"), A("inv"), O.add)
         cp(A("plu"), A("plc"))
-        ts(A("iv2"), A("kmi"), W, O.is_ge)
+        tt(A("keyw"), A("plc"), A("inv"), O.add)
         if last:
             whole(3)
         for r in range(16):
             mm(P(2, r, 256, 16), A("bc", 128 * r, 128 * r + 128), A("key16"))
         mm(P(3, 0, 256), A("blk"), A("zb"), True, False)
-        tt(A("iv2"), A("iv2"), A("dumpc"), O.mult)
-        tt(A("plc2"), A("iv2"), A("plc"), O.max)
-        tt(A("dd"), A("dumpc"), A("plc2"), O.subtract)
+        mm(P(4, 0, 16), A("idb"), A("key16"), True, False)
+        mm(P(4, 0, 16), A("idb"), A("ivw"), False, False)
+        mm(P(5, 0, 256), A("id256"), A("cq"), True, False)
         act(A("eo"), ind(A("et"), A("plu")), F.Copy)
-        for x in range(16):
-            act(A("kr", x, 256, 16), A("keyw"), F.Identity, bias=A("tm", x, x + 1))
         act(A("so"), A("eo"), F.Sign)
         cp(A("kb16"), P(2, 0, 256))
-        for c in range(15):
-            e = A("eq", 256 * c + 16 * c + 16, 256 * c + 256)
-            ts(e, A("kb16", 16 * c + 16, 256), A("keyw", c, c + 1), O.is_equal)
-            mm(P(3, 16 * c + 16, 256), A("blk"), e, False, False)
-            if c == 13:
-                tt(A("dm"), P(2, 0, 256), A("kr"), O.is_equal)
-        mm(P(3, 0, 256), A("blk"), A("dm"), False, True)
-        mm(P(5, 0, 256), A("id256"), A("cq"), True, False)
         mm(P(5, 0, 256), A("idb"), A("eo"), False, False)
         mm(P(5, 0, 256), A("id128"), A("so"), False, True)
+        for c in range(16):
+            ts(A("eq", 272 * c, 256 * c + 256), A("kb16", 16 * c, 256), A("keyw", c, c + 1), O.is_equal)
+            if c < 15:
+                mm(P(3, 16 * c + 16, 256), A("blk"), A("eq", 272 * c + 16, 256 * c + 256), False, c == 14)
+            if c == 6:
+                ts(A("cn"), P(5, 0, 256), -127.0, O.max, 127.0, O.min)
+                if last:
+                    act(A("en32"), A("cn"), F.Identity, bias=128.0)
+                else:
+                    act(A("ent"), A("cn"), F.Abs)
+                    act(A("en"), A("cn"), F.Identity, bias=128.0)
         act(A("lsb"), P(3, 0, 256), F.Copy)
-        ts(A("cn"), P(5, 0, 256), -127.0, O.max, 127.0, O.min)
-        wsum(P(4, 0, 16), "em", "lsb", 0, 256)
-        if last:
-            act(A("en32"), A("cn"), F.Identity, bias=128.0)
-        else:
-            act(A("ent"), A("cn"), F.Abs)
-            act(A("en"), A("cn"), F.Identity, bias=128.0)
+        if not last:
             mm(P(5, 256, 512), A("blk"), A("ent"))
+        for x in range(16):
+            mm(P(4, 0, 16), A("eb", 128 * x, 128 * x + 128), A("eq", x, 4096, 272), False, False)
+        wsum(P(4, 0, 16), "em", "lsb", 0, 256, False)
+        if not last:
             act(A("lv"), P(5, 256, 512), F.Sign)
             act(A("fr"), P(5, 256, 512), F.Relu, bias=128.0, scale=-128.0)
-        tt(A("fo1"), A("dd"), P(4, 0, 16), O.min)
-        tt(A("fo"), A("fo1"), A("plc2"), O.add)
+        tt(A("fo"), A("dumpc"), P(4, 0, 16), O.min)
         cp(A("fou"), A("fo"))
         if last:
             tt(ind(A("yb"), A("fou")), A("aa"), A("en32"), O.add)
         else:
             tt(ind(A("et"), A("fou")), A("en"), A("lv"), O.mult)
-            cp(A("et", 2048, DUMMY), A("et", 0, 16))
+            act(A("et", 2048, DUMMY), A("et", 0, 16), F.Copy)
 
     for c in range(4):
         s = 512 * c

@@ -2,13 +2,16 @@ from concourse.bass import DstId, RemoteDMATransfer
 from concourse.mybir import AluOpType as O, ActivationFunctionType as F
 
 RO, STEP, N, CAP = 3, 650, 4, 64
-CUT = 208
+HAM_S = ((0, 64), (64, 128), (184, 212), (160, 184), (144, 160), (128, 144))
+HAM_V = ((212, 232), (232, 256))
+EQ_S = 12
 DUMMY, DUMP = 2064, 2832
 TW = DUMP + 256
 W = 32768.0
 BIG = 12582912.0
 NONE = 14336
-NP = 4
+PIECES = (0, 512, 1024, 1536, 1792, 2048)
+NP = len(PIECES) - 1
 F32, B16, H16, I32, U16 = "float32", "bfloat16", "float16", "int32", "uint16"
 
 WIDE = {
@@ -22,12 +25,12 @@ WIDE = {
 SMALL = {
     F32: "pcol 1 cols 32 rr0 128 rr1 128 rr2 128 cw0 8 cw1 8 cw2 8 kscan 272 m64 64 sel15 128 iow 16 iow1 16 xio 16 tm 16 "
          "kr 256 cs32 64 dumpc 16 cneg 8 totu 1 gds 256 t1 256 t2 256 t3 256 t4 256 tv 16 cmpo 64 base 256 term 256 d256 256 "
-         "fr 256 aa 256 sm 128 ka 64 k4 64 k5 32 inv 16 keyw 16 fo 16 en32 256",
+         "id256f 128 fr 256 aa 1024 sm 128 ka 64 k4 64 k5 32 inv 16 keyw 16 nkey 16 fo 16 en32 256",
     B16: "blk 128 blka 128 blk592 8 idb 128 idw 128 id128 128 id256 128 shu 128 shd 128 cor 128 tmpb 128 mid 128 gum 128 gdm 128 "
-         "nblk 128 dif 128 gq 128 xm 128 code0 128 code 128 "
+         "nblk 128 blk2 128 dif 128 gq 128 xm 128 code0 128 code 128 "
          "ns0 128 ns1 128 ns2 128 t10 128 t11 128 t12 128 t20 128 t21 128 t22 128 r00 256 r01 256 r02 256 "
          "negb 256 io0 256 io1 256 a1 128 m128 128 trb 128 mrow 128 zb 256 w12 16 live 128 w 128 wz 128 val 256 abc 256 ct 256 "
-         "eg 256 f1 256 ffq 256 sgc 256 fa 256 ef 256 lv 256 ra 256 sd 256 nq 256 oh 64 ohc 64 cq 256 eo 256 so 256 cn 256 "
+         "eg 256 f1 256 ffq 256 sgc 256 fa 256 ef 256 lv 256 ra 256 rb 256 rvn 256 sd 256 nq 256 oh 64 ohc 64 cq 256 eo 256 so 256 cn 256 "
          "ent 256 en 256 dm 256 lsb 256",
     H16: "nx 16 nt 16 d16 256 vk16 32 t32 128 ch16 256 mk 64 cs64 64 dmp16 16 a16 256 z16 128 invw 16 ivw 16 key16 16 kb16 256",
     I32: "icol 1 icol2 1 icol3 1 ui 32 ui2 32 pi 16 h16 16 km 272 vk 32 own 16 z 128 zi2 128 kmi 16 plc 16",
@@ -55,7 +58,7 @@ def _layout():
 
 
 SCRATCH, PLACE = _layout()
-SEMAPHORES = ["sv", "ss", "st", "sg", "sent", "ldh"] + ["ld%d" % i for i in range(NP)] + ["out%d" % i for i in range(4)] + ["arr%d" % i for i in range(RO)]
+SEMAPHORES = ["sv", "ss", "st", "sg", "sent", "ldh", "out"] + ["ld%d" % i for i in range(NP)] + ["arr%d" % i for i in range(RO)]
 SEMOF = {"v": "sv", "s": "ss", "t": "st", "g": "sg"}
 
 
@@ -68,8 +71,9 @@ def plan(topo, cores, rank):
     out, used = [], 0
     others = sorted([o for o in range(N) if o != rank], key=far)
     for o in others:
-        n = 4 if o == others[-1] else 2
-        out.append((o, topo.engines(cores[rank], cores[o])[used:used + n]))
+        es = topo.engines(cores[rank], cores[o])
+        n = len(es) // (2 if o == others[-1] else 4)
+        out.append((o, es[used:used + n]))
         used += n
     return out
 
@@ -193,9 +197,8 @@ def rank_program(g, core, T, topo):
     col = lambda j: A("cols", j, j + 1)
     ROW, G16, R15, LO, HI, W1, W2, BMB, BRA, UP, DOWN, ALT, TMP, TMP2, NML = range(15)
 
-    pw = 2048 // NP
     for c in range(NP):
-        load("y", "ld%d" % c, A("detb", pw * c, pw * c + pw), T.det[:, pw * c:pw * c + pw])
+        load("y", "ld%d" % c, A("detb", PIECES[c], PIECES[c + 1]), T.det[:, PIECES[c]:PIECES[c + 1]])
     load("y", "ldh", A("hamb"), T.ham[:, :])
 
     def chunk(t):
@@ -255,16 +258,16 @@ def rank_program(g, core, T, topo):
     spread("em", W, 0, 16)
     for j in range(2):
         act(A("lb", 512 * j, 512 * j + 512), one(512), F.Identity, scale=0.0)
-    for k in range(16):
-        act(A("rexp", k, 2048, 16), A("idb"), F.Copy)
     act(A("idw"), A("idb"), F.Identity, scale=W)
     act(A("mid"), A("idb"), F.Identity, scale=-1.0)
     act(A("id128"), A("idb"), F.Identity, scale=-128.0)
-    act(A("id256"), A("idb"), F.Identity, scale=256.0)
+    act(A("id256"), A("idb"), F.Identity, scale=-256.0)
+    act(A("id256f"), A("idb"), F.Identity, scale=256.0)
     act(A("zb"), one(256), F.Identity, scale=0.0)
     act(A("sel15"), A("blk"), F.Identity, scale=col(R15))
     act(A("blka"), A("blk"), F.Identity, scale=col(ALT))
     act(A("nblk"), A("blk"), F.Identity, scale=-1.0)
+    act(A("blk2"), A("blk"), F.Identity, scale=col(W2))
     act(A("blk592"), A("blk", 0, 128, 16), F.Identity, scale=592.0)
     act(A("w12", 0, 8), A("blk", 0, 128, 16), F.Identity, scale=col(W1))
     act(A("w12", 8, 16), A("blk", 0, 128, 16), F.Identity, scale=col(W2))
@@ -275,22 +278,29 @@ def rank_program(g, core, T, topo):
     iota(A("detb", 2048, DUMMY + 256), [[0, DUMMY + 256 - 2048]], 128, 0)
     iota(A("et", 2048, TW), [[0, TW - 2048]], 128, 0)
 
-    def free_mark(c):
+    def free_mark(c, b):
         s = 512 * c
-        mm(P(6 + c % 2, 0, 512), A("blk"), A("cab", s, s + 512))
-        act(A("frb", s, s + 512), P(6 + c % 2, 0, 512), F.Relu, bias=1.0, scale=-1.0)
+        mm(P(b, 0, 512), A("blk"), A("cab", s, s + 512))
+        act(A("frb", s, s + 512), P(b, 0, 512), F.Relu, bias=1.0, scale=-1.0)
+
+    def repeat(k0, k1):
+        for k in range(k0, k1):
+            act(A("rexp", k, 2048, 16), A("idb"), F.Copy)
 
     for c in range(NP):
-        s = pw * c
-        ts(A("big", s, s + pw), A("detb", s, s + pw), 255, O.bitwise_and)
-        if c == NP - 1:
+        s, e = PIECES[c], PIECES[c + 1]
+        ts(A("big", s, e), A("detb", s, e), 255, O.bitwise_and)
+        if c == 2:
             round_v(0)
-        cp(A("et", s, s + pw), A("big", s, s + pw))
-        act(A("cab", s, s + pw), A("et", s, s + pw), F.Abs, bias=-128.0)
+        if c < 2:
+            spread("e1", col(W1), 4 * c, 4 * c + 4)
+        act(A("cab", s, e), A("big", s, e), F.Abs, bias=-128.0)
         if c == 0:
             act(A("cab", 2048, DUMMY), A("cab", 0, 16), F.Copy)
         if c < 2:
-            free_mark(c)
+            repeat(2 * c, 2 * c + 2)
+    cp(A("et", 0, 512), A("big", 0, 512))
+    act(A("et", 1024, 2048), A("big", 1024, 2048), F.Copy)
 
     def mark(c, b, part):
         s = 512 * c
@@ -302,23 +312,25 @@ def rank_program(g, core, T, topo):
             act(A("et", s, s + 512), P(b, 0, 512), F.Copy)
 
     def rest_g():
-        sel(A("gum"), A("tmpb"), [[0, 8], [1, 16]], O.not_equal, 0.0, -15, 0)
-        sel(A("shd"), A("idb"), [[1, 128]], O.not_equal, -1.0, -1, -1)
-        sel(A("gdm"), A("shd"), [[0, 8], [1, 16]], O.not_equal, 0.0, 0, 0)
+        sel(A("gum"), A("shu"), [[0, 8], [1, 16]], O.not_equal, 0.0, -15, 0)
+        sel(A("gdm"), A("m128"), [[1, 128]], O.is_equal, 0.0, -1, -1)
         sel(A("kscan"), one(272), [[0, 16], [1, 17]], O.not_equal, -3.0e7, 0, 0)
-        sel(A("rvk", 0, 256), A("negb"), [[-8, 2], [-1, 8], [0, 16]], O.is_equal, 0.0, 0, 1)
-        sel(A("rvk", 256, 512), one(256), [[-8, 2], [-1, 8], [0, 16]], O.is_equal, 0.0, -16, 1)
+        sel(A("rvk"), one(512), [[-8, 4], [-1, 8], [0, 16]], O.is_equal, 0.0, 0, 1)
+        sel(A("rvn"), A("negb"), [[-8, 2], [-1, 8], [0, 16]], O.is_equal, 0.0, 0, 1)
+        for r in range(8):
+            sel(A("e2", 128 * r, 128 * r + 128), A("blk2"), [[0, 8], [1, 16]], O.is_equal, 0.0, -r, 0)
         iota(A("cs32"), [[256, 4], [-16, 16]], -1024, 0)
         sel(A("m64"), one(64), [[0, 4], [1, 16]], O.not_equal, 0.0, 0, 0)
         sel(A("trb"), A("nblk"), [[-1, 128]], O.is_ge, 0.0, 0, 1)
         iota(A("sb0"), [[0, 1280]], NONE, 0)
         iota(A("dt", 2048, TW), [[0, TW - 2048]], 0, 0)
         iota(A("mrow"), [[2048, 8], [0, 16]], -31 * 16384, 0)
-        iota(A("xio"), [[1, 16]], 0, 0)
+        for j in range(4):
+            sel(A("bc", 512 * j, 512 * j + 512), one(512), [[-1, 4], [-16, 8], [0, 16]], O.is_equal, 0.0, -4 * j, 1)
 
     def rest_v():
-        ts(col(DOWN), col(ROW), 0.0, O.is_equal, 8192.0, O.mult)
-        ts(col(UP), col(R15), -8192.0, O.mult)
+        ts(col(DOWN), col(ROW), 0.0, O.is_equal, -8192.0, O.mult)
+        ts(col(UP), col(R15), 8192.0, O.mult)
         ts(col(BMB), col(ROW), -8192.0, O.mult, -8192.0 * 2032, O.add)
         ts(col(BRA), col(ROW), 8192.0, O.mult, 8192.0 * 2034, O.add)
         ts(A("dmp16"), A("iow"), 1024.0, O.add)
@@ -334,8 +346,8 @@ def rank_program(g, core, T, topo):
         for r in range(16):
             mm(out, A(weights, 128 * r, 128 * r + 128), A(src, c0 + r, c1, 16), start and r == 0, stop and r == 15)
 
-    def enter_d(h):
-        tt(ind(A("dt"), A("fou", 8 * h, 8 * h + 8)), A("aa", 128 * h, 128 * h + 128), A("fr", 128 * h, 128 * h + 128), O.add)
+    def put_d(places, d, a, b):
+        tt(ind(A("dt"), A(places, a, b)), A(d, 16 * a, 16 * b), A("fr", 16 * a, 16 * b), O.add)
 
     for t in range(RO):
         start = STEP * (t + 1)
@@ -346,17 +358,16 @@ def rank_program(g, core, T, topo):
             mm(P(0, u, 128, 16), A("et" if t else "cab", off + u, off + u + 2033, 16), A("blk", 0, 128, 16))
         mm(P(3, 0, 256), A("a1", 0, 128, 1, 0, 1), A("io1", 0, 256, 1, 0, 1), True, False)
         if t == 0:
-            free_mark(2)
             ts(A("iow"), A("iow"), col(ROW), O.add)
-            spread("e1", col(W1), 0, 8)
         else:
-            enter_d(0)
+            put_d("fou", "aa", 0, 6)
         ts(A("live"), P(0, 0, 128), 0.5, O.is_gt)
         scan(A("w"), A("m128"), A("live"), O.mult, O.add)
         ts(A("cneg"), A("w", 15, 128, 16), col(NML), O.mult)
         if t == 0:
             ts(A("iow1"), A("iow"), 1.0, O.add)
             ts(A("dumpc"), A("iow"), float(DUMP), O.add)
+            spread("e1", col(W1), 8, 11)
         mm(P(1, 0, 8), A("t1%d" % t), A("w", 15, 128, 16), True, False)
         mm(P(1, 0, 8), A("t2%d" % t), A("w", 15 - off, 128, 16), False, True)
         mm(P(2, 0, 128), A("ns%d" % t), A("w"))
@@ -378,33 +389,48 @@ def rank_program(g, core, T, topo):
         mm(P(4, 0, 16), A("idw"), A("nx"), True, False)
         mm(P(4, 0, 16), A("idw"), A("nt"), False, False)
         if t == 0:
-            free_mark(3)
+            repeat(4, 16)
+            free_mark(0, 6)
+            rest_v()
+        else:
+            put_d("fou", "aa", 6, 10)
         ts(A("val"), P(3, 0, 256), col(LO), O.max, col(HI), O.min)
         wsum(P(4, 0, 16), "em", "val", 0, 256, False)
         if t == 0:
-            rest_v()
-            spread("e1", col(W1), 8, 13)
+            cp(A("et", 512, 1024), A("big", 512, 1024))
+            spread("e1", col(W1), 11, 13)
         else:
-            enter_d(1)
+            put_d("fou", "aa", 10, 16)
         ts(A("pl"), P(4, 0, 16), 1.0 / W, O.mult, float(16 * m0 + off), O.add)
-        if t == 0:
-            ts(A("du"), ind(A("detb"), A("pl")), 1.0 / 256, O.mult, -0.5, O.add)
-        else:
-            ts(A("du"), ind(A("dt"), A("pl")), 1.0 / 256, O.mult)
+        for a, b in ((0, 64), (64, 256)):
+            if t == 0:
+                ts(A("du", a, b), ind(A("detb"), A("pl", a // 16, b // 16)), 1.0 / 256, O.mult, -0.5, O.add)
+            else:
+                ts(A("du", a, b), ind(A("dt"), A("pl", a // 16, b // 16)), 1.0 / 256, O.mult)
         act(A("abc"), ind(A("et"), A("pl")), F.Abs, bias=-128.0)
         for h in range(2):
             mm(P(7, 128 * h, 128 * h + 128), A("abc", 128 * h, 128 * h + 128), A("idb"))
-        for a in range(0, CUT, 32):
-            b = min(a + 32, CUT)
+        for a, b in HAM_S:
             act(A("lg", 16 * a, 16 * b), ind(A("hamb"), A("du", a, b)), F.Copy)
         ts(A("d16"), A("du"), 2048.0, O.subtract)
-        cp(A("ct"), P(7, 0, 256))
-        cp(A("lg", 16 * CUT, 4096), ind(A("hamb"), A("du", CUT, 256)))
-        order = [7, 0, 1, 2, 3, 4, 5, 6]
+        for j, (a, b) in enumerate(HAM_V):
+            cp(A("lg", 16 * a, 16 * b), ind(A("hamb"), A("du", a, b)))
+            if j == 0:
+                cp(A("ct"), P(7, 0, 256))
+        order = [7, 0, 1, 2, 3, 6, 5, 4]
 
         def rep(j):
             b = order[j]
             mm(P(j % 4, 0, 512), A("ct", 128 * (b // 4), 128 * (b // 4) + 128), A("rexp", 512 * (b % 4), 512 * (b % 4) + 512))
+
+        def least(j, a, b):
+            s = 512 * order[j]
+            tt(A("mn", s + a, s + b), A("lg", s + a, s + b), P(j % 4, a, b), O.min)
+
+        def esum(a, b):
+            h = a // 128
+            for k in range(16):
+                mm(P(6, 136 * h + k, 136 * h + 136, 17, a % 128, a % 128 + b - a), A("mn", 16 * a + k, 16 * b, 16), A("blk592"))
 
         rep(0)
         rep(1)
@@ -422,9 +448,9 @@ def rank_program(g, core, T, topo):
             scan(A("km", 136 * h, 136 * h + 136), A("kscan", 136 * h, 136 * h + 136), P(6, 136 * h, 136 * h + 136), O.add, O.max)
 
         for j in range(8):
-            b = order[j]
-            s = 512 * b
-            tt(A("mn", s, s + 512), A("lg", s, s + 512), P(j % 4, 0, 512), O.min)
+            if j == 7:
+                least(7, 256, 512)
+            least(j, 0, 256 if j == 7 else 512)
             if j == 0:
                 cp(A("ui"), P(4, 0, 32))
             if j == 1:
@@ -437,10 +463,8 @@ def rank_program(g, core, T, topo):
                 ts(A("kscan", 16, 272, 17), A("h16"), float(16 * t), O.add)
             if j < 4:
                 rep(j + 4)
-            if b in (3, 6):
-                h = b // 4
-                for k in range(16):
-                    mm(P(6, 136 * h + k, 136 * h + 136, 17), A("mn", 2048 * h + k, 2048 * h + 2048, 16), A("blk592"))
+            if j >= 4:
+                esum(*((0, 128), (192, 256), (160, 192), (128, 160))[j - 4])
         act(A("gds"), P(7, 256, 512), F.Identity, bias=col(DOWN))
         act(P(7, 0, 256), P(7, 0, 256), F.Identity, bias=col(UP))
         act(A("eg"), ind(A("et"), A("pl")), F.Copy)
@@ -451,51 +475,54 @@ def rank_program(g, core, T, topo):
         kmax(0)
         if t == 0:
             ts(A("cs64"), A("cs32"), col(ROW), O.subtract)
-            spread("e1", col(W1), 13, 16)
-            spread("e2", col(W2), 0, 3)
+            spread("e1", col(W1), 13, 14)
         kmax(1)
         ts(A("vk", 0, 16), A("km", 16, 272, 17), 4, O.arith_shift_right, 4095, O.bitwise_and)
         ts(A("vk", 16, 32), A("km", 16, 272, 17), 15, O.bitwise_and)
         ts(A("vk16"), A("vk"), 2048.0, O.subtract)
         mm(P(2, 256, 512), A("blk"), A("fa"))
-        mm(P(4, 0, 128, 1, 0, 32), A("vk16"), A("idb"))
-        if t == 0:
-            spread("e2", col(W2), 3, 8)
-        cp(A("t32", 0, 128, 1, 0, 32), P(4, 0, 128, 1, 0, 32))
-        for h in range(2):
-            s = 128 * h
-            mm(P(0, s, s + 128), A("idb"), A("d16", s, s + 128), True, False)
-            mm(P(0, s, s + 128), A("rvk", s, s + 128, 1, 0, 32), A("t32", 0, 128, 1, 0, 32), False, True)
-        for h in range(2):
-            s = 128 * h
-            mm(P(1, s, s + 128), A("rvk", 256 + s, 256 + s + 128, 1, 0, 32), A("t32", 0, 128, 1, 0, 32))
-        if t == 0:
-            spread("e2", col(W2), 8, 13)
         act(A("lv"), P(2, 256, 512), F.Sign)
         act(A("fr"), P(2, 256, 512), F.Relu, bias=128.0, scale=-128.0)
-
-        def halves(out, a, b, op):
+        mm(P(4, 0, 128, 1, 0, 32), A("vk16"), A("idb"))
+        if t == 0:
+            spread("e1", col(W1), 14, 16)
+            spread("e2", col(W2), 8, 11)
+        cp(A("t32", 0, 128, 1, 0, 32), P(4, 0, 128, 1, 0, 32))
+        t32 = A("t32", 0, 128, 1, 0, 32)
+        for b in (1, 0):
             for s in (0, 128):
-                tt(*[P(x, s, s + 128) if isinstance(x, int) else A(x, s, s + 128) for x in (out, a, b)], op)
+                mm(P(b, s, s + 128), A("rvk", 256 * b + s, 256 * b + s + 128, 1, 0, 32), t32)
+        for s in (0, 128):
+            mm(P(5, 256 + s, 384 + s), A("idb"), A("d16", s, s + 128), True, False)
+            mm(P(5, 256 + s, 384 + s), A("rvn", s, s + 128, 1, 0, 32), t32, False, True)
+        if t == 0:
+            spread("e2", col(W2), 11, 16)
 
-        halves("t1", "gds", 0, O.min)
-        act(P(2, 0, 256), P(1, 0, 256), F.Relu, bias=col(BMB), scale=-8192.0)
-        act(A("ra"), P(1, 0, 256), F.Relu, bias=col(BRA), scale=8192.0)
-        act(A("sd"), P(0, 0, 256), F.Sign, scale=col(ALT))
+        def halves(out, a, banks, op):
+            for h in range(2):
+                s = 128 * h
+                tt(A(out, s, s + 128), A(a, s, s + 128), P(banks[h], s, s + 128), op)
+
+        def bound(name, banks, sign, bias, scale):
+            for h in range(2):
+                s = 128 * h
+                act(A(name, s, s + 128), P(1, s, s + 128), F.Relu, bias=bias, scale=scale)
+                mm(P(banks[h], s, s + 128), A("idb"), A("d16", s, s + 128), True, False)
+                mm(P(banks[h], s, s + 128), A(sign), A(name, s, s + 128), False, True)
+
+        bound("rb", (2, 6), "mid", col(BMB), -8192.0)
+        bound("ra", (4, 3), "idb", col(BRA), 8192.0)
+        act(A("sd"), P(5, 256, 512), F.Sign, scale=col(ALT))
         act(A("ffq"), A("f1"), F.Identity, bias=-0.75, scale=1.0 / 256)
-        halves("t2", "t1", 7, O.max)
-        mm(P(4, 0, 256), A("idb"), A("d16"), True, False)
-        mm(P(4, 0, 256), A("idb"), A("ra"), False, True)
-        mm(P(3, 0, 16), A("idw"), A("nt"), True, False)
-        wsum(P(3, 0, 16), "em", "sd", 0, 256, False)
-        halves("t3", "t2", 2, O.min)
-        halves("t4", 5, "t3", O.subtract)
-        halves("ch16", "t4", 4, O.min)
-        act(A("tv"), P(3, 0, 16), F.Abs, bias=1.0, scale=1.0 / W)
+        halves("t1", "gds", (0, 0), O.max)
+        halves("t2", "t1", (7, 7), O.min)
+        mm(P(1, 0, 16), A("idw"), A("nt"), True, False)
+        wsum(P(1, 0, 16), "em", "sd", 0, 256, False)
+        halves("t3", "t2", (2, 6), O.max)
+        halves("ch16", "t3", (4, 3), O.min)
+        act(A("tv"), P(1, 0, 16), F.Abs, bias=1.0, scale=1.0 / W)
         for o in range(4):
             act(A("cmpo", 16 * o, 16 * o + 16), A("tv"), F.Identity, bias=-1.0, scale=o + 1.0)
-        if t == 0:
-            spread("e2", col(W2), 13, 16)
         tt(A("nq"), A("ch16"), P(5, 0, 256), O.not_equal)
         whash("ch16")
         mm(P(5, 256, 512), A("blka"), A("nq"))
@@ -509,8 +536,8 @@ def rank_program(g, core, T, topo):
         act(A("base"), P(7, 256, 512), F.Copy)
         act(A("ef"), P(2, 0, 256), F.Copy)
         if t == 0:
-            mark(0, 1, 0)
-            act(A("es"), A("em"), F.Identity, scale=31.0 / 32)
+            free_mark(1, 0)
+            free_mark(2, 1)
         cp(A("ui"), P(6, 0, 32))
         ts(A("ui2"), A("ui"), 4095, O.bitwise_and)
         tt(A("pi"), A("ui2", 0, 16), A("ui2", 16, 32), O.mult)
@@ -525,70 +552,67 @@ def rank_program(g, core, T, topo):
         for o in range(4):
             mm(P(3, 0, 16), A("idb"), A("mk", 16 * o, 16 * o + 16), False, o == 3)
         if t == 0:
-            ts(A("tm"), A("xio"), col(ROW), O.is_gt)
+            free_mark(3, 6)
         cp(A("sl"), P(3, 0, 16))
         sb, ar, arr = "sb%d" % t, "ar%d" % t, "arr%d" % t
         tt(ind(A(sb), A("sl")), A("base"), A("term"), O.add)
+        need("g", [], [A(sb)])
         trs = []
         for o, es in plan(topo, T.cores, rank):
             rid, pid = topo.addr(T.cores[o])[:2]
             trs.append(RemoteDMATransfer(dst_ids=[DstId(rid=rid, pnc=pid)], dma_engine_mask=sum(1 << e for e in es), remote_sem=T.sem[arr],
                                          src=A(sb, 256 * o, 256 * o + 64)[0], dst=A(ar, 64 * rank, 64 * rank + 64)[0]))
-        need("g", [], [A(sb)])
         g.remote_dma_fused(trs, local_sem=T.sem.sent)
         got = sum(len(es) for q in range(N) if q != rank for o, es in plan(topo, T.cores, q) if o == rank)
-        if t == 0:
-            for j in range(4):
-                sel(A("bc", 512 * j, 512 * j + 512), one(512), [[-1, 4], [-16, 8], [0, 16]], O.is_equal, 0.0, -4 * j, 1)
         if not last:
             round_g(t + 1)
+            if t == 0:
+                for j in range(4):
+                    sel(A("eb", 512 * j, 512 * j + 512), A("em", 512 * j, 512 * j + 512), [[1, 4], [16, 8], [0, 16]], O.is_ge, 0.0, 4 * j - 1, -1)
             iota(A("sb%d" % (t + 1)), [[0, 1280]], NONE, 0)
         if t == RO - 2:
             iota(A("yb", 2048, TW), [[0, TW - 2048]], 0, 0)
         act(A(ar, 64 * rank, 64 * rank + 64), A(sb, 256 * rank, 256 * rank + 64), F.Copy)
         if t == 0:
-            mark(1, 0, 0)
-            mark(2, 2, 0)
-            mark(3, 7, 0)
-            mark(0, 1, 1)
-            mark(1, 0, 1)
-            mark(2, 2, 1)
-            mark(3, 7, 1)
-            tt(ind(A("dt"), A("pl")), A("d256"), A("fr"), O.add)
+            for part in range(2):
+                for c in range(4):
+                    mark(c, (0, 1, 2, 7)[c], part)
+            put_d("pl", "d256", 0, 8)
             tt(ind(A("et"), A("pl")), A("ef"), A("lv"), O.mult)
-            for x in range(16):
-                act(A("eb", 128 * x, 128 * x + 128), A("em", 128 * x, 128 * x + 128), F.Identity, scale=A("tm", x, x + 1))
+            act(A("es"), A("em"), F.Identity, scale=31.0 / 32)
         else:
             tt(ind(A("et"), A("pl")), A("ef"), A("lv"), O.mult)
-            tt(ind(A("dt"), A("pl")), A("d256"), A("fr"), O.add)
+            put_d("pl", "d256", 0, 8)
 
-        def whole(c):
+        def whole(c, b, part):
             s = 512 * c
-            tt(A("yb", s, s + 512), A("dt", s, s + 512), P(2 + c, 0, 512), O.add)
+            if part == 0:
+                mm(P(b, 0, 512), A("idb"), A("et", s, s + 512))
+            else:
+                tt(A("yb", s, s + 512), A("dt", s, s + 512), P(b, 0, 512), O.add)
 
-        if last:
-            for c in range(4):
-                mm(P(2 + c, 0, 512), A("idb"), A("et", 512 * c, 512 * c + 512))
-            whole(0)
-            whole(1)
         ts(A("a16"), A(ar), BIG, O.add, BIG, O.subtract, extra=[(arr, got)])
         whash("a16")
-        ts(A("aa"), A("a16"), 256.0, O.mult, 2048.0 * 256, O.add)
-        tt(A("cq"), A(ar), A("a16"), O.subtract)
+        ts(A("aa", 0, 256), A("a16"), 256.0, O.mult, 2048.0 * 256, O.add)
+        put_d("pl", "d256", 8, 16)
+        for j in range(1, 4):
+            act(A("aa", 256 * j, 256 * j + 256), A("aa", 0, 256), F.Copy)
+        mm(P(5, 0, 256), A("id256f"), A(ar), True, False)
+        mm(P(5, 0, 256), A("id256"), A("a16"), False, False)
         cp(A("ui"), P(6, 0, 32))
         ts(A("ui2"), A("ui"), 4095, O.bitwise_and)
         ts(A("invw"), A("ui", 0, 16), 4.0e6, O.is_gt, W, O.mult)
+        if last:
+            whole(0, 7, 0)
+            whole(1, 6, 0)
         tt(A("pi"), A("ui2", 0, 16), A("ui2", 16, 32), O.mult)
-        ts(A("sm", 16, 32), A("ui2", 0, 16), 2.0, O.mult, 1.0, O.add)
-        ts(A("sm", 32, 48), A("ui2", 0, 16), 4.0, O.mult, 2.0, O.add)
-        ts(A("sm", 48, 64), A("ui2", 0, 16), 6.0, O.mult, 3.0, O.add)
-        for m in range(4, 8):
-            act(A("sm", 16 * m, 16 * m + 16), A("sm", 16, 32), F.Identity, scale=float(m))
+        for m in range(1, 8):
+            act(A("sm", 16 * m, 16 * m + 16), A("ui2", 0, 16), F.Identity, bias=float(m), scale=2.0 * m)
         ts(A("zi2", 0, 16), A("pi"), 7, O.arith_shift_right, 2047, O.bitwise_and)
         cp(A("zu", 0, 16), A("zi2", 0, 16))
 
-        def probe(m):
-            tt(A("ne", 256 * m, 256 * m + 256), ind(A("dt"), A("zu", 16 * m, 16 * m + 16)), A("aa"), O.not_equal)
+        def probe(m0, m1):
+            tt(A("ne", 256 * m0, 256 * m1), ind(A("dt"), A("zu", 16 * m0, 16 * m1)), A("aa", 0, 256 * (m1 - m0)), O.not_equal)
 
         def steps(m0, m1):
             for m in range(m0, m1):
@@ -597,37 +621,37 @@ def rank_program(g, core, T, topo):
         def free_at(m0, m1):
             act(A("sg", 256 * m0, 256 * m1), ind(A("et"), A("zu", 16 * m0, 16 * m1)), F.Sign)
 
-        def keys(h):
-            mm(P(h, 0, 64), A("ones", 0, 128, 1, 0, 1), A("mrow", 64 * h, 64 * h + 64, 1, 0, 1), True, False)
-            for j in range(4):
-                mm(P(h, 16 * j, 16 * j + 16), A("idb"), A("invw"), False, False)
-            mm(P(h, 0, 64), A("idb"), A("z16", 64 * h, 64 * h + 64), False, False)
-            wsum(P(h, 0, 64), "es", "sg", 1024 * h, 1024 * h + 1024, False, False)
-            wsum(P(h, 0, 64), "em", "ne", 1024 * h, 1024 * h + 1024, False)
+        def keys(b, m0, m1):
+            out = P(b, 0, 16 * (m1 - m0))
+            mm(out, A("ones", 0, 128, 1, 0, 1), A("mrow", 16 * m0, 16 * m1, 1, 0, 1), True, False)
+            for j in range(m1 - m0):
+                mm(P(b, 16 * j, 16 * j + 16), A("idb"), A("invw"), False, False)
+            mm(out, A("idb"), A("z16", 16 * m0, 16 * m1), False, False)
+            wsum(out, "es", "sg", 256 * m0, 256 * m1, False, False)
+
+        def unequal(b, m0, m1):
+            wsum(P(b, 0, 16 * (m1 - m0)), "em", "ne", 256 * m0, 256 * m1, False)
 
         free_at(0, 1)
         steps(1, 4)
         ts(A("zi2", 16, 64), A("z", 16, 64), 2047, O.bitwise_and)
-        probe(0)
-        cp(A("zu", 16, 64), A("zi2", 16, 64))
         steps(4, 8)
+        cp(A("zu", 16, 64), A("zi2", 16, 64))
         free_at(1, 4)
         ts(A("zi2", 64, 128), A("z", 64, 128), 2047, O.bitwise_and)
-        probe(1)
+        probe(0, 1)
         cp(A("zu", 64, 128), A("zi2", 64, 128))
         cp(A("z16"), A("zi2"))
         free_at(4, 8)
-        probe(2)
-        probe(3)
-        keys(0)
-        for m in range(4, 8):
-            probe(m)
-        keys(1)
+        keys(0, 0, 4)
+        probe(1, 4)
+        unequal(0, 0, 4)
         act(A("ka"), P(0, 0, 64), F.Copy)
+        keys(1, 4, 8)
+        probe(4, 8)
+        unequal(1, 4, 8)
         if last:
-            whole(2)
-        else:
-            round_v(t + 1)
+            whole(0, 7, 1)
         tt(A("k4"), A("ka"), P(1, 0, 64), O.min)
         tt(A("k5"), A("k4", 0, 32), A("k4", 32, 64), O.min)
         tt(A("kmi"), A("k5", 0, 16), A("k5", 16, 32), O.min)
@@ -637,53 +661,58 @@ def rank_program(g, core, T, topo):
         cp(A("key16"), A("plc"))
         cp(A("plu"), A("plc"))
         tt(A("keyw"), A("plc"), A("inv"), O.add)
-        if last:
-            whole(3)
+        ts(A("nkey"), A("keyw"), -1.0, O.mult)
         for r in range(16):
             mm(P(2, r, 256, 16), A("bc", 128 * r, 128 * r + 128), A("key16"))
         mm(P(3, 0, 256), A("blk"), A("zb"), True, False)
         mm(P(4, 0, 16), A("idb"), A("key16"), True, False)
         mm(P(4, 0, 16), A("idb"), A("ivw"), False, False)
-        mm(P(5, 0, 256), A("id256"), A("cq"), True, False)
+        if last:
+            whole(1, 6, 1)
+            whole(2, 0, 0)
+            whole(3, 1, 0)
         act(A("eo"), ind(A("et"), A("plu")), F.Copy)
         act(A("so"), A("eo"), F.Sign)
         cp(A("kb16"), P(2, 0, 256))
         mm(P(5, 0, 256), A("idb"), A("eo"), False, False)
         mm(P(5, 0, 256), A("id128"), A("so"), False, True)
+        for c in range(EQ_S, 16):
+            act(A("dm", 16 * c, 256) if c == EQ_S else A("mn", 64 * c, 64 * c + 256 - 16 * c), P(2, 16 * c, 256), F.Abs, bias=A("nkey", c, c + 1))
+        for c in range(EQ_S, 16):
+            act(A("eq", 272 * c, 256 * c + 256), A("dm", 16 * c, 256) if c == EQ_S else A("mn", 64 * c, 64 * c + 256 - 16 * c), F.Relu, bias=1.0, scale=-1.0)
+        if not last:
+            act(A("ent"), P(5, 0, 256), F.Abs)
         for c in range(16):
-            ts(A("eq", 272 * c, 256 * c + 256), A("kb16", 16 * c, 256), A("keyw", c, c + 1), O.is_equal)
+            if c < EQ_S:
+                ts(A("eq", 272 * c, 256 * c + 256), A("kb16", 16 * c, 256), A("keyw", c, c + 1), O.is_equal)
             if c < 15:
                 mm(P(3, 16 * c + 16, 256), A("blk"), A("eq", 272 * c + 16, 256 * c + 256), False, c == 14)
-            if c == 6:
-                ts(A("cn"), P(5, 0, 256), -127.0, O.max, 127.0, O.min)
-                if last:
-                    act(A("en32"), A("cn"), F.Identity, bias=128.0)
-                else:
-                    act(A("ent"), A("cn"), F.Abs)
-                    act(A("en"), A("cn"), F.Identity, bias=128.0)
         act(A("lsb"), P(3, 0, 256), F.Copy)
+        ts(A("cn"), P(5, 0, 256), -127.0, O.max, 127.0, O.min)
+        act(A("en32" if last else "en"), A("cn"), F.Identity, bias=128.0)
         if not last:
-            mm(P(5, 256, 512), A("blk"), A("ent"))
+            mm(P(6, 0, 256), A("blk"), A("ent"))
+            act(A("lv"), P(6, 0, 256), F.Sign)
+            act(A("fr"), P(6, 0, 256), F.Relu, bias=128.0, scale=-128.0)
         for x in range(16):
             mm(P(4, 0, 16), A("eb", 128 * x, 128 * x + 128), A("eq", x, 4096, 272), False, False)
         wsum(P(4, 0, 16), "em", "lsb", 0, 256, False)
-        if not last:
-            act(A("lv"), P(5, 256, 512), F.Sign)
-            act(A("fr"), P(5, 256, 512), F.Relu, bias=128.0, scale=-128.0)
+        if last:
+            whole(2, 0, 1)
+            whole(3, 1, 1)
+        else:
+            round_v(t + 1)
         tt(A("fo"), A("dumpc"), P(4, 0, 16), O.min)
         cp(A("fou"), A("fo"))
         if last:
-            tt(ind(A("yb"), A("fou")), A("aa"), A("en32"), O.add)
+            tt(ind(A("yb"), A("fou")), A("aa", 0, 256), A("en32"), O.add)
         else:
             tt(ind(A("et"), A("fou")), A("en"), A("lv"), O.mult)
             act(A("et", 2048, DUMMY), A("et", 0, 16), F.Copy)
 
-    for c in range(4):
-        s = 512 * c
-        store("ys"[c % 2], "out%d" % c, T.y[:, s:s + 512], A("yb", s, s + 512))
-    for c in range(4):
-        g.wait_ge(T.sem["out%d" % c], 16)
+    store("y", "out", T.y[:, :], A("yb", 0, 2048))
+    g.wait_ge(T.sem.out, 16)
     g.wait_ge(T.sem.ldh, 16)
-    g.wait_ge(T.sem.sent, 8 * RO)
+    g.wait_ge(T.sem.sent, RO * sum(len(es) for o, es in plan(topo, T.cores, rank)))
     for q in ("v", "s", "t", "g"):
         g.wait_ge(T.sem[SEMOF[q]], count[q])

from concourse.bass import DstId, RemoteDMATransfer
from concourse.mybir import AluOpType as O, ActivationFunctionType as F

RO, STEP, N, CAP = 3, 650, 4, 64
HAM_S = ((0, 64), (64, 128), (184, 212), (160, 184), (144, 160), (128, 144))
HAM_V = ((212, 232), (232, 256))
EQ_S = 12
DUMMY, DUMP = 2064, 2832
TW = DUMP + 256
W = 32768.0
BIG = 12582912.0
NONE = 14336
PIECES = (0, 512, 1024, 1536, 1792, 2048)
NP = len(PIECES) - 1
F32, B16, H16, I32, U16 = "float32", "bfloat16", "float16", "int32", "uint16"

WIDE = {
    "detb": (DUMMY + 256, I32), "big": (2048, I32), "dt": (TW, F32), "et": (TW, B16), "yb": (TW, F32), "cab": (DUMMY, B16),
    "hamb": (4096, B16), "ones": (512, B16), "frb": (2048, B16),
    "em": (2048, B16), "es": (2048, B16), "eb": (2048, B16), "e1": (2048, B16), "e2": (2048, B16), "bc": (2048, B16), "rexp": (2048, B16),
    "lb": (1024, B16), "rvk": (512, B16), "cmp": (2048, B16), "lg": (4096, B16),
    "mn": (4096, B16), "sb0": (1280, F32), "sb1": (1280, F32), "sb2": (1280, F32), "ar0": (256, F32), "ar1": (256, F32),
    "ar2": (256, F32), "ne": (2048, B16), "sg": (2048, B16), "eq": (4096, B16),
}
SMALL = {
    F32: "pcol 1 cols 32 rr0 128 rr1 128 rr2 128 cw0 8 cw1 8 cw2 8 kscan 272 m64 64 sel15 128 iow 16 iow1 16 xio 16 tm 16 "
         "kr 256 cs32 64 dumpc 16 cneg 8 totu 1 gds 256 t1 256 t2 256 t3 256 t4 256 tv 16 cmpo 64 base 256 term 256 d256 256 "
         "id256f 128 fr 256 aa 1024 sm 128 ka 64 k4 64 k5 32 inv 16 keyw 16 nkey 16 fo 16 en32 256",
    B16: "blk 128 blka 128 blk592 8 idb 128 idw 128 id128 128 id256 128 shu 128 shd 128 cor 128 tmpb 128 mid 128 gum 128 gdm 128 "
         "nblk 128 blk2 128 dif 128 gq 128 xm 128 code0 128 code 128 "
         "ns0 128 ns1 128 ns2 128 t10 128 t11 128 t12 128 t20 128 t21 128 t22 128 r00 256 r01 256 r02 256 "
         "negb 256 io0 256 io1 256 a1 128 m128 128 trb 128 mrow 128 zb 256 w12 16 live 128 w 128 wz 128 val 256 abc 256 ct 256 "
         "eg 256 f1 256 ffq 256 sgc 256 fa 256 ef 256 lv 256 ra 256 rb 256 rvn 256 sd 256 nq 256 oh 64 ohc 64 cq 256 eo 256 so 256 cn 256 "
         "ent 256 en 256 dm 256 lsb 256",
    H16: "nx 16 nt 16 d16 256 vk16 32 t32 128 ch16 256 mk 64 cs64 64 dmp16 16 a16 256 z16 128 invw 16 ivw 16 key16 16 kb16 256",
    I32: "icol 1 icol2 1 icol3 1 ui 32 ui2 32 pi 16 h16 16 km 272 vk 32 own 16 z 128 zi2 128 kmi 16 plc 16",
    U16: "pl 16 du 256 sl 16 zu 128 plu 16 fou 16",
}


def _layout():
    scratch, place = {}, {}
    for i in range(8):
        scratch["p%d" % i] = ("psum", [128, 512], F32)
        place["p%d" % i] = ("p%d" % i, 0, 512)
    for name in WIDE:
        scratch[name] = ("sbuf", [128, WIDE[name][0]], WIDE[name][1])
        place[name] = (name, 0, WIDE[name][0])
    for dtype in SMALL:
        words = SMALL[dtype].split()
        at = 0
        for j in range(0, len(words), 2):
            w = int(words[j + 1])
            place[words[j]] = ("w_" + dtype, at, w)
            at += (w + 15) // 16 * 16
        scratch["w_" + dtype] = ("sbuf", [128, at], dtype)
    return scratch, place


SCRATCH, PLACE = _layout()
SEMAPHORES = ["sv", "ss", "st", "sg", "sent", "ldh", "out"] + ["ld%d" % i for i in range(NP)] + ["arr%d" % i for i in range(RO)]
SEMOF = {"v": "sv", "s": "ss", "t": "st", "g": "sg"}


def plan(topo, cores, rank):
    a = topo.chip(cores[rank])

    def far(o):
        b = topo.chip(cores[o])
        return 0 if topo.mates(a, b) or topo.same_plane(a, b) else 1
    out, used = [], 0
    others = sorted([o for o in range(N) if o != rank], key=far)
    for o in others:
        es = topo.engines(cores[rank], cores[o])
        n = len(es) // (2 if o == others[-1] else 4)
        out.append((o, es[used:used + n]))
        used += n
    return out


def rank_program(g, core, T, topo):
    rank = T.rank_of(core)
    if rank is None:
        return
    queues = {"v": g.vector, "s": g.scalar, "t": g.tensor, "g": g, "y": g.sync}
    count = {"v": 0, "s": 0, "t": 0, "g": 0}
    known = {q: {} for q in queues}
    clock, hist, srcq = {}, {}, {}

    def A(name, c0=0, c1=None, step=1, p0=0, p1=128):
        buf, base, w = PLACE[name]
        lo, hi = base + c0, base + (w if c1 is None else c1)
        t = T[buf]
        ap = t[p0:p1, lo:hi] if step == 1 else t[p0:p1, lo:hi:step]
        cols = ((1 << (hi - lo + step - 1) // step * step) - 1) // ((1 << step) - 1) << lo
        return (ap, buf, cols, step)

    def P(b, c0, c1, step=1, p0=0, p1=128):
        return A("p%d" % b, c0, c1, step, p0, p1)

    def ind(win, off):
        return (win[0].indirect(off[0]), win, off)

    def flat(x):
        return [x[1], x[2]] if len(x) == 3 else [x]

    def ispsum(buf):
        return buf[0] == "p" and buf[1:].isdigit()

    def need(q, outs, ins, extra=()):
        want = dict(extra)
        acc = [(flat(o)[0], "w") for o in outs] + [(a, "r") for o in outs for a in flat(o)[1:]] + [(a, "r") for i in ins for a in flat(i)]
        for (_, buf, cols, _), kind in acc:
            ps = ispsum(buf)
            for (sq, idx, k2, c2) in hist.get(buf, ()):
                if sq == q == "t":
                    continue
                if (ps and sq != q) or ((kind == "w" or k2 == "w") and cols & c2):
                    want[sq] = max(want.get(sq, 0), idx)
        for s in sorted(want):
            if known[q].get(s, 0) < want[s]:
                queues[q].wait_ge(T.sem[SEMOF.get(s, s)], want[s])
                known[q][s] = want[s]
                for k, v in clock.get((s, want[s]), {}).items():
                    known[q][k] = max(known[q].get(k, 0), v)
        return acc

    def note(q, idx, acc):
        clock[(q, idx)] = dict(known[srcq.get(q, q)])
        for (_, buf, cols, _), kind in acc:
            old = hist.get(buf, [])
            if ispsum(buf):
                keep = [e for e in old if e[0] == q and q != "t" and not (kind == "w" and e[3] & ~cols == 0)]
            else:
                keep = [e for e in old if not (e[3] & ~cols == 0 and (kind == "w" or (e[2] == "r" and e[0] == q)))]
            hist[buf] = keep + [(q, idx, kind, cols)]

    def emit(q, outs, ins, call, extra=()):
        acc = need(q, outs, ins, extra)
        r = call()
        count[q] += 1
        r.then_inc(T.sem[SEMOF[q]], 1)
        note(q, count[q], acc)

    def load(q, sem, out, src):
        acc = need(q, [out], [])
        queues[q].dma_start(out[0], src).then_inc(T.sem[sem], 16)
        srcq[sem] = q
        note(sem, 16, acc)

    def store(q, sem, dst, i):
        acc = need(q, [], [i])
        queues[q].dma_start(dst, i[0]).then_inc(T.sem[sem], 16)
        srcq[sem] = q
        note(sem, 16, acc)

    def mm(out, l, r, start=True, stop=True):
        emit("t", [out], [l, r], lambda: g.tensor.matmul(out[0], l[0], r[0], start, stop))

    def cp(out, i):
        emit("v", [out], [i], lambda: g.vector.tensor_copy(out[0], i[0]))

    def tt(out, a, b, op):
        emit("v", [out], [a, b], lambda: g.vector.tensor_tensor(out[0], a[0], b[0], op))

    def ts(out, i, s1, op0, s2=None, op1=None, extra=()):
        ins = [i] + [s for s in (s1, s2) if isinstance(s, tuple)]
        x1 = s1[0] if isinstance(s1, tuple) else s1
        x2 = s2[0] if isinstance(s2, tuple) else s2
        if op1 is None:
            emit("v", [out], ins, lambda: g.vector.tensor_scalar(out[0], i[0], x1, None, op0), extra)
        else:
            emit("v", [out], ins, lambda: g.vector.tensor_scalar(out[0], i[0], x1, x2, op0, op1), extra)

    def scan(out, a, b, op0, op1):
        emit("v", [out], [a, b], lambda: g.vector.tensor_tensor_scan(out[0], a[0], b[0], 0.0, op0, op1))

    def fill(out, c):
        emit("v", [out], [], lambda: g.vector.memset(out[0], c))

    def act(out, i, func, bias=0.0, scale=1.0):
        ins = [i] + [s for s in (bias, scale) if isinstance(s, tuple)]
        b = bias[0] if isinstance(bias, tuple) else bias
        c = scale[0] if isinstance(scale, tuple) else scale
        if func == F.Copy:
            emit("s", [out], ins, lambda: g.scalar.activation(out[0], i[0], func))
        else:
            emit("s", [out], ins, lambda: g.scalar.activation(out[0], i[0], func, bias=b, scale=c))

    def iota(out, pat, base, cm):
        emit("g", [out], [], lambda: g.iota(out[0], pat, base, cm, allow_small_or_imprecise_dtypes=True))

    def sel(out, i, pat, op, fillv, base, cm):
        emit("g", [out], [i], lambda: g.affine_select(out[0], i[0], pat, op, fillv, base, cm))

    one = lambda w: A("ones", 0, w)
    col = lambda j: A("cols", j, j + 1)
    ROW, G16, R15, LO, HI, W1, W2, BMB, BRA, UP, DOWN, ALT, TMP, TMP2, NML = range(15)

    for c in range(NP):
        load("y", "ld%d" % c, A("detb", PIECES[c], PIECES[c + 1]), T.det[:, PIECES[c]:PIECES[c + 1]])
    load("y", "ldh", A("hamb"), T.ham[:, :])

    def chunk(t):
        m0 = STEP * (t + 1) // 16
        return m0, m0 - 1

    def round_g(t):
        m0, ml = chunk(t)
        rr = "rr%d" % t
        iota(A(rr, 0, ml), [[1, ml]], 128, 0)
        iota(A(rr, m0, 128), [[1, 128 - m0]], m0, 0)
        iota(A(rr, ml, m0), [[0, 1]], 126, 0)
        sel(A("cw%d" % t), one(8), [[0, 8]], O.not_equal, -128.0, -ml, 1)
        sel(A("t2%d" % t), one(128), [[200, 128]], O.is_equal, 0.0, -127 - 200 * ml, 1)
        sel(A("ns%d" % t), A("tmpb"), [[1, 128]], O.not_equal, 0.0, -ml, 0)
        sel(A("r0%d" % t), A("negb"), [[0, 256]], O.is_equal, 0.0, -m0, 1)

    def round_v(t):
        m0, ml = chunk(t)
        ts(col(TMP), A("pcol"), float(m0), O.is_lt, 128.0, O.mult)
        ts(col(NML), A("pcol"), float(ml), O.not_equal, -1.0, O.mult)
        ts(A("lb", 15, 1024, 144), A("cw%d" % t), 16.0, O.mult)
        tt(col(TMP2), col(TMP), A("pcol"), O.add)
        ts(A("t1%d" % t), A("rr%d" % t), col(TMP2), O.is_ge)

    def spread(name, weight, r0, r1):
        for r in range(r0, r1):
            ts(A(name, 128 * r, 128 * r + 128), A("code"), float(r), O.is_equal, weight, O.mult)

    iota(A("icol"), [[0, 1]], 0, 1)
    iota(A("dif"), [[1, 128]], 0, -1)
    iota(A("gq"), [[16, 8], [0, 16]], 0, 0)
    iota(A("code0"), [[-16, 8], [1, 16]], 0, 0)
    iota(A("xm"), [[0, 8], [1, 16]], 0, 0)
    fill(A("ones"), 1.0)
    fill(A("negb"), -1.0)
    ts(A("icol2"), A("icol"), 15, O.bitwise_and)
    ts(A("icol3"), A("icol"), 1, O.bitwise_and)
    cp(A("pcol"), A("icol"))
    cp(col(ROW), A("icol2"))
    ts(col(ALT), A("icol3"), -2.0, O.mult, 1.0, O.add)
    ts(A("idb"), A("dif"), 0.0, O.is_equal)
    ts(A("shu"), A("dif"), -1.0, O.is_equal)
    ts(A("cor"), A("dif"), 127.0, O.is_equal)
    tt(col(G16), A("pcol"), col(ROW), O.subtract)
    ts(col(R15), col(ROW), 15.0, O.is_equal)
    tt(A("tmpb"), A("idb"), A("shu"), O.subtract)
    ts(col(W1), col(ROW), 13.0, O.mult, 5.0, O.add)
    ts(col(W2), col(ROW), -14.0, O.mult, 255.0, O.add)
    ts(A("blk"), A("gq"), col(G16), O.is_equal)
    tt(A("tmpb"), A("tmpb"), A("cor"), O.subtract)
    ts(A("code"), A("code0"), col(G16), O.add)
    ts(col(LO), col(R15), -4000.0, O.mult)
    ts(col(HI), col(R15), 3999.0, O.mult, 1.0, O.add)
    ts(A("m128"), A("xm"), 0.0, O.not_equal)
    ts(A("a1"), A("xm"), 15.0, O.not_equal)
    spread("em", W, 0, 16)
    for j in range(2):
        act(A("lb", 512 * j, 512 * j + 512), one(512), F.Identity, scale=0.0)
    act(A("idw"), A("idb"), F.Identity, scale=W)
    act(A("mid"), A("idb"), F.Identity, scale=-1.0)
    act(A("id128"), A("idb"), F.Identity, scale=-128.0)
    act(A("id256"), A("idb"), F.Identity, scale=-256.0)
    act(A("id256f"), A("idb"), F.Identity, scale=256.0)
    act(A("zb"), one(256), F.Identity, scale=0.0)
    act(A("sel15"), A("blk"), F.Identity, scale=col(R15))
    act(A("blka"), A("blk"), F.Identity, scale=col(ALT))
    act(A("nblk"), A("blk"), F.Identity, scale=-1.0)
    act(A("blk2"), A("blk"), F.Identity, scale=col(W2))
    act(A("blk592"), A("blk", 0, 128, 16), F.Identity, scale=592.0)
    act(A("w12", 0, 8), A("blk", 0, 128, 16), F.Identity, scale=col(W1))
    act(A("w12", 8, 16), A("blk", 0, 128, 16), F.Identity, scale=col(W2))
    round_g(0)
    iota(A("io0"), [[1, 256]], 0, 0)
    iota(A("io1"), [[1, 256]], 1, 0)
    iota(A("iow"), [[16, 16]], 0, 0)
    iota(A("detb", 2048, DUMMY + 256), [[0, DUMMY + 256 - 2048]], 128, 0)
    iota(A("et", 2048, TW), [[0, TW - 2048]], 128, 0)

    def free_mark(c, b):
        s = 512 * c
        mm(P(b, 0, 512), A("blk"), A("cab", s, s + 512))
        act(A("frb", s, s + 512), P(b, 0, 512), F.Relu, bias=1.0, scale=-1.0)

    def repeat(k0, k1):
        for k in range(k0, k1):
            act(A("rexp", k, 2048, 16), A("idb"), F.Copy)

    for c in range(NP):
        s, e = PIECES[c], PIECES[c + 1]
        ts(A("big", s, e), A("detb", s, e), 255, O.bitwise_and)
        if c == 2:
            round_v(0)
        if c < 2:
            spread("e1", col(W1), 4 * c, 4 * c + 4)
        act(A("cab", s, e), A("big", s, e), F.Abs, bias=-128.0)
        if c == 0:
            act(A("cab", 2048, DUMMY), A("cab", 0, 16), F.Copy)
        if c < 2:
            repeat(2 * c, 2 * c + 2)
    cp(A("et", 0, 512), A("big", 0, 512))
    act(A("et", 1024, 2048), A("big", 1024, 2048), F.Copy)

    def mark(c, b, part):
        s = 512 * c
        if part == 0:
            mm(P(b, 0, 512), A("idb"), A("et", s, s + 512), True, False)
            mm(P(b, 0, 512), A("id128"), A("frb", s, s + 512), False, True)
        else:
            tt(A("dt", s, s + 512), A("detb", s, s + 512), P(b, 0, 512), O.subtract)
            act(A("et", s, s + 512), P(b, 0, 512), F.Copy)

    def rest_g():
        sel(A("gum"), A("shu"), [[0, 8], [1, 16]], O.not_equal, 0.0, -15, 0)
        sel(A("gdm"), A("m128"), [[1, 128]], O.is_equal, 0.0, -1, -1)
        sel(A("kscan"), one(272), [[0, 16], [1, 17]], O.not_equal, -3.0e7, 0, 0)
        sel(A("rvk"), one(512), [[-8, 4], [-1, 8], [0, 16]], O.is_equal, 0.0, 0, 1)
        sel(A("rvn"), A("negb"), [[-8, 2], [-1, 8], [0, 16]], O.is_equal, 0.0, 0, 1)
        for r in range(8):
            sel(A("e2", 128 * r, 128 * r + 128), A("blk2"), [[0, 8], [1, 16]], O.is_equal, 0.0, -r, 0)
        iota(A("cs32"), [[256, 4], [-16, 16]], -1024, 0)
        sel(A("m64"), one(64), [[0, 4], [1, 16]], O.not_equal, 0.0, 0, 0)
        sel(A("trb"), A("nblk"), [[-1, 128]], O.is_ge, 0.0, 0, 1)
        iota(A("sb0"), [[0, 1280]], NONE, 0)
        iota(A("dt", 2048, TW), [[0, TW - 2048]], 0, 0)
        iota(A("mrow"), [[2048, 8], [0, 16]], -31 * 16384, 0)
        for j in range(4):
            sel(A("bc", 512 * j, 512 * j + 512), one(512), [[-1, 4], [-16, 8], [0, 16]], O.is_equal, 0.0, -4 * j, 1)

    def rest_v():
        ts(col(DOWN), col(ROW), 0.0, O.is_equal, -8192.0, O.mult)
        ts(col(UP), col(R15), 8192.0, O.mult)
        ts(col(BMB), col(ROW), -8192.0, O.mult, -8192.0 * 2032, O.add)
        ts(col(BRA), col(ROW), 8192.0, O.mult, 8192.0 * 2034, O.add)
        ts(A("dmp16"), A("iow"), 1024.0, O.add)

    def whash(src, between=None):
        for e in range(2):
            for r in range(16):
                mm(P(6, 16 * e, 16 * e + 16), A("e%d" % (e + 1), 128 * r, 128 * r + 128), A(src, r, 256, 16), r == 0, r == 15)
            if between and e == 0:
                between()

    def wsum(out, weights, src, c0, c1, start=True, stop=True):
        for r in range(16):
            mm(out, A(weights, 128 * r, 128 * r + 128), A(src, c0 + r, c1, 16), start and r == 0, stop and r == 15)

    def put_d(places, d, a, b):
        tt(ind(A("dt"), A(places, a, b)), A(d, 16 * a, 16 * b), A("fr", 16 * a, 16 * b), O.add)

    for t in range(RO):
        start = STEP * (t + 1)
        m0, off = start // 16, start % 16
        last = t == RO - 1
        dummy = DUMMY + 256 * t
        for u in range(16):
            mm(P(0, u, 128, 16), A("et" if t else "cab", off + u, off + u + 2033, 16), A("blk", 0, 128, 16))
        mm(P(3, 0, 256), A("a1", 0, 128, 1, 0, 1), A("io1", 0, 256, 1, 0, 1), True, False)
        if t == 0:
            ts(A("iow"), A("iow"), col(ROW), O.add)
        else:
            put_d("fou", "aa", 0, 6)
        ts(A("live"), P(0, 0, 128), 0.5, O.is_gt)
        scan(A("w"), A("m128"), A("live"), O.mult, O.add)
        ts(A("cneg"), A("w", 15, 128, 16), col(NML), O.mult)
        if t == 0:
            ts(A("iow1"), A("iow"), 1.0, O.add)
            ts(A("dumpc"), A("iow"), float(DUMP), O.add)
            spread("e1", col(W1), 8, 11)
        mm(P(1, 0, 8), A("t1%d" % t), A("w", 15, 128, 16), True, False)
        mm(P(1, 0, 8), A("t2%d" % t), A("w", 15 - off, 128, 16), False, True)
        mm(P(2, 0, 128), A("ns%d" % t), A("w"))
        mm(P(5, 0, 1), A("w"), A("ones", 0, 1))
        sel(A("wz"), A("w"), [[0, 8], [1, 16]], O.not_equal, 0.0, -15, 0)
        if t == 0:
            rest_g()
        for h in range(8):
            ts(A("cmp", 256 * h, 256 * h + 256), A("io0"), P(1, h, h + 1), O.is_ge)
            act(A("lb", 144 * h, 144 * h + 15), P(2, 16 * h, 16 * h + 15), F.Identity, bias=A("cneg", h, h + 1))
            if h == 3:
                mm(P(3, 0, 256), A("wz"), A("r0%d" % t), False, False)
            if h == 4:
                act(A("totu"), P(5, 0, 1), F.Copy)
                mm(P(5, 1, 2), A("sel15"), A("totu"))
            mm(P(3, 0, 256), A("lb", 128 * h, 128 * h + 128), A("cmp", 256 * h, 256 * h + 256), False, h == 7)
        ts(A("nx"), A("iow1"), P(5, 1, 2), O.subtract, 0.0, O.max)
        ts(A("nt"), A("iow"), P(5, 1, 2), O.is_ge, float(dummy - start), O.mult)
        mm(P(4, 0, 16), A("idw"), A("nx"), True, False)
        mm(P(4, 0, 16), A("idw"), A("nt"), False, False)
        if t == 0:
            repeat(4, 16)
            free_mark(0, 6)
            rest_v()
        else:
            put_d("fou", "aa", 6, 10)
        ts(A("val"), P(3, 0, 256), col(LO), O.max, col(HI), O.min)
        wsum(P(4, 0, 16), "em", "val", 0, 256, False)
        if t == 0:
            cp(A("et", 512, 1024), A("big", 512, 1024))
            spread("e1", col(W1), 11, 13)
        else:
            put_d("fou", "aa", 10, 16)
        ts(A("pl"), P(4, 0, 16), 1.0 / W, O.mult, float(16 * m0 + off), O.add)
        for a, b in ((0, 64), (64, 256)):
            if t == 0:
                ts(A("du", a, b), ind(A("detb"), A("pl", a // 16, b // 16)), 1.0 / 256, O.mult, -0.5, O.add)
            else:
                ts(A("du", a, b), ind(A("dt"), A("pl", a // 16, b // 16)), 1.0 / 256, O.mult)
        act(A("abc"), ind(A("et"), A("pl")), F.Abs, bias=-128.0)
        for h in range(2):
            mm(P(7, 128 * h, 128 * h + 128), A("abc", 128 * h, 128 * h + 128), A("idb"))
        for a, b in HAM_S:
            act(A("lg", 16 * a, 16 * b), ind(A("hamb"), A("du", a, b)), F.Copy)
        ts(A("d16"), A("du"), 2048.0, O.subtract)
        for j, (a, b) in enumerate(HAM_V):
            cp(A("lg", 16 * a, 16 * b), ind(A("hamb"), A("du", a, b)))
            if j == 0:
                cp(A("ct"), P(7, 0, 256))
        order = [7, 0, 1, 2, 3, 6, 5, 4]

        def rep(j):
            b = order[j]
            mm(P(j % 4, 0, 512), A("ct", 128 * (b // 4), 128 * (b // 4) + 128), A("rexp", 512 * (b % 4), 512 * (b % 4) + 512))

        def least(j, a, b):
            s = 512 * order[j]
            tt(A("mn", s + a, s + b), A("lg", s + a, s + b), P(j % 4, a, b), O.min)

        def esum(a, b):
            h = a // 128
            for k in range(16):
                mm(P(6, 136 * h + k, 136 * h + 136, 17, a % 128, a % 128 + b - a), A("mn", 16 * a + k, 16 * b, 16), A("blk592"))

        rep(0)
        rep(1)
        for h in range(2):
            for e in range(2):
                mm(P(4, 16 * e + 8 * h, 16 * e + 8 * h + 8), A("d16", 128 * h, 128 * h + 128), A("w12", 8 * e, 8 * e + 8))
        rep(2)
        rep(3)
        mm(P(7, 0, 256), A("gum"), A("d16"))
        mm(P(7, 256, 512), A("gdm"), A("d16"))
        mm(P(5, 0, 256), A("idb"), A("d16"))
        mm(P(6, 16, 272, 17), A("zb", 0, 128), A("blk", 0, 16))

        def kmax(h):
            scan(A("km", 136 * h, 136 * h + 136), A("kscan", 136 * h, 136 * h + 136), P(6, 136 * h, 136 * h + 136), O.add, O.max)

        for j in range(8):
            if j == 7:
                least(7, 256, 512)
            least(j, 0, 256 if j == 7 else 512)
            if j == 0:
                cp(A("ui"), P(4, 0, 32))
            if j == 1:
                ts(A("ui2"), A("ui"), 4095, O.bitwise_and)
            if j == 2:
                tt(A("pi"), A("ui2", 0, 16), A("ui2", 16, 32), O.mult)
            if j == 3:
                ts(A("h16"), A("pi"), 1, O.arith_shift_right, 0x7FFFFFF0, O.bitwise_and)
            if j == 4:
                ts(A("kscan", 16, 272, 17), A("h16"), float(16 * t), O.add)
            if j < 4:
                rep(j + 4)
            if j >= 4:
                esum(*((0, 128), (192, 256), (160, 192), (128, 160))[j - 4])
        act(A("gds"), P(7, 256, 512), F.Identity, bias=col(DOWN))
        act(P(7, 0, 256), P(7, 0, 256), F.Identity, bias=col(UP))
        act(A("eg"), ind(A("et"), A("pl")), F.Copy)
        act(A("fa"), A("abc"), F.Relu, bias=-1.0)
        act(A("d256"), P(5, 0, 256), F.Identity, bias=2048.0 * 256, scale=256.0)
        act(A("sgc"), A("eg"), F.Sign, bias=-128.0)
        act(A("f1"), A("eg"), F.Identity, bias=159.625, scale=0.25)
        kmax(0)
        if t == 0:
            ts(A("cs64"), A("cs32"), col(ROW), O.subtract)
            spread("e1", col(W1), 13, 14)
        kmax(1)
        ts(A("vk", 0, 16), A("km", 16, 272, 17), 4, O.arith_shift_right, 4095, O.bitwise_and)
        ts(A("vk", 16, 32), A("km", 16, 272, 17), 15, O.bitwise_and)
        ts(A("vk16"), A("vk"), 2048.0, O.subtract)
        mm(P(2, 256, 512), A("blk"), A("fa"))
        act(A("lv"), P(2, 256, 512), F.Sign)
        act(A("fr"), P(2, 256, 512), F.Relu, bias=128.0, scale=-128.0)
        mm(P(4, 0, 128, 1, 0, 32), A("vk16"), A("idb"))
        if t == 0:
            spread("e1", col(W1), 14, 16)
            spread("e2", col(W2), 8, 11)
        cp(A("t32", 0, 128, 1, 0, 32), P(4, 0, 128, 1, 0, 32))
        t32 = A("t32", 0, 128, 1, 0, 32)
        for b in (1, 0):
            for s in (0, 128):
                mm(P(b, s, s + 128), A("rvk", 256 * b + s, 256 * b + s + 128, 1, 0, 32), t32)
        for s in (0, 128):
            mm(P(5, 256 + s, 384 + s), A("idb"), A("d16", s, s + 128), True, False)
            mm(P(5, 256 + s, 384 + s), A("rvn", s, s + 128, 1, 0, 32), t32, False, True)
        if t == 0:
            spread("e2", col(W2), 11, 16)

        def halves(out, a, banks, op):
            for h in range(2):
                s = 128 * h
                tt(A(out, s, s + 128), A(a, s, s + 128), P(banks[h], s, s + 128), op)

        def bound(name, banks, sign, bias, scale):
            for h in range(2):
                s = 128 * h
                act(A(name, s, s + 128), P(1, s, s + 128), F.Relu, bias=bias, scale=scale)
                mm(P(banks[h], s, s + 128), A("idb"), A("d16", s, s + 128), True, False)
                mm(P(banks[h], s, s + 128), A(sign), A(name, s, s + 128), False, True)

        bound("rb", (2, 6), "mid", col(BMB), -8192.0)
        bound("ra", (4, 3), "idb", col(BRA), 8192.0)
        act(A("sd"), P(5, 256, 512), F.Sign, scale=col(ALT))
        act(A("ffq"), A("f1"), F.Identity, bias=-0.75, scale=1.0 / 256)
        halves("t1", "gds", (0, 0), O.max)
        halves("t2", "t1", (7, 7), O.min)
        mm(P(1, 0, 16), A("idw"), A("nt"), True, False)
        wsum(P(1, 0, 16), "em", "sd", 0, 256, False)
        halves("t3", "t2", (2, 6), O.max)
        halves("ch16", "t3", (4, 3), O.min)
        act(A("tv"), P(1, 0, 16), F.Abs, bias=1.0, scale=1.0 / W)
        for o in range(4):
            act(A("cmpo", 16 * o, 16 * o + 16), A("tv"), F.Identity, bias=-1.0, scale=o + 1.0)
        tt(A("nq"), A("ch16"), P(5, 0, 256), O.not_equal)
        whash("ch16")
        mm(P(5, 256, 512), A("blka"), A("nq"))
        act(P(5, 256, 512), P(5, 256, 512), F.Abs, scale=2.0)
        mm(P(7, 256, 512), A("idb"), A("ch16"), True, False)
        mm(P(7, 256, 512), A("mid"), A("ffq"), False, True)
        mm(P(4, 0, 64), A("idb"), A("cs64"), True, False)
        mm(P(3, 0, 16), A("idb"), A("dmp16"), True, False)
        mm(P(2, 0, 256), A("idb"), A("eg"), True, False)
        mm(P(2, 0, 256), A("mid"), A("sgc"), False, True)
        act(A("base"), P(7, 256, 512), F.Copy)
        act(A("ef"), P(2, 0, 256), F.Copy)
        if t == 0:
            free_mark(1, 0)
            free_mark(2, 1)
        cp(A("ui"), P(6, 0, 32))
        ts(A("ui2"), A("ui"), 4095, O.bitwise_and)
        tt(A("pi"), A("ui2", 0, 16), A("ui2", 16, 32), O.mult)
        ts(A("own"), A("pi"), 5, O.arith_shift_right, 3, O.bitwise_and)
        for o in range(4):
            tt(A("oh", 16 * o, 16 * o + 16), A("own"), A("cmpo", 16 * o, 16 * o + 16), O.is_equal)
        scan(A("ohc"), A("m64"), A("oh"), O.mult, O.add)
        tt(A("term"), A("ffq"), P(5, 256, 512), O.mult)
        mm(P(4, 0, 64), A("trb"), A("oh"), False, False)
        mm(P(4, 0, 64), A("blk"), A("ohc"), False, True)
        tt(A("mk"), A("oh"), P(4, 0, 64), O.mult)
        for o in range(4):
            mm(P(3, 0, 16), A("idb"), A("mk", 16 * o, 16 * o + 16), False, o == 3)
        if t == 0:
            free_mark(3, 6)
        cp(A("sl"), P(3, 0, 16))
        sb, ar, arr = "sb%d" % t, "ar%d" % t, "arr%d" % t
        tt(ind(A(sb), A("sl")), A("base"), A("term"), O.add)
        need("g", [], [A(sb)])
        trs = []
        for o, es in plan(topo, T.cores, rank):
            rid, pid = topo.addr(T.cores[o])[:2]
            trs.append(RemoteDMATransfer(dst_ids=[DstId(rid=rid, pnc=pid)], dma_engine_mask=sum(1 << e for e in es), remote_sem=T.sem[arr],
                                         src=A(sb, 256 * o, 256 * o + 64)[0], dst=A(ar, 64 * rank, 64 * rank + 64)[0]))
        g.remote_dma_fused(trs, local_sem=T.sem.sent)
        got = sum(len(es) for q in range(N) if q != rank for o, es in plan(topo, T.cores, q) if o == rank)
        if not last:
            round_g(t + 1)
            if t == 0:
                for j in range(4):
                    sel(A("eb", 512 * j, 512 * j + 512), A("em", 512 * j, 512 * j + 512), [[1, 4], [16, 8], [0, 16]], O.is_ge, 0.0, 4 * j - 1, -1)
            iota(A("sb%d" % (t + 1)), [[0, 1280]], NONE, 0)
        if t == RO - 2:
            iota(A("yb", 2048, TW), [[0, TW - 2048]], 0, 0)
        act(A(ar, 64 * rank, 64 * rank + 64), A(sb, 256 * rank, 256 * rank + 64), F.Copy)
        if t == 0:
            for part in range(2):
                for c in range(4):
                    mark(c, (0, 1, 2, 7)[c], part)
            put_d("pl", "d256", 0, 8)
            tt(ind(A("et"), A("pl")), A("ef"), A("lv"), O.mult)
            act(A("es"), A("em"), F.Identity, scale=31.0 / 32)
        else:
            tt(ind(A("et"), A("pl")), A("ef"), A("lv"), O.mult)
            put_d("pl", "d256", 0, 8)

        def whole(c, b, part):
            s = 512 * c
            if part == 0:
                mm(P(b, 0, 512), A("idb"), A("et", s, s + 512))
            else:
                tt(A("yb", s, s + 512), A("dt", s, s + 512), P(b, 0, 512), O.add)

        ts(A("a16"), A(ar), BIG, O.add, BIG, O.subtract, extra=[(arr, got)])
        whash("a16")
        ts(A("aa", 0, 256), A("a16"), 256.0, O.mult, 2048.0 * 256, O.add)
        put_d("pl", "d256", 8, 16)
        for j in range(1, 4):
            act(A("aa", 256 * j, 256 * j + 256), A("aa", 0, 256), F.Copy)
        mm(P(5, 0, 256), A("id256f"), A(ar), True, False)
        mm(P(5, 0, 256), A("id256"), A("a16"), False, False)
        cp(A("ui"), P(6, 0, 32))
        ts(A("ui2"), A("ui"), 4095, O.bitwise_and)
        ts(A("invw"), A("ui", 0, 16), 4.0e6, O.is_gt, W, O.mult)
        if last:
            whole(0, 7, 0)
            whole(1, 6, 0)
        tt(A("pi"), A("ui2", 0, 16), A("ui2", 16, 32), O.mult)
        for m in range(1, 8):
            act(A("sm", 16 * m, 16 * m + 16), A("ui2", 0, 16), F.Identity, bias=float(m), scale=2.0 * m)
        ts(A("zi2", 0, 16), A("pi"), 7, O.arith_shift_right, 2047, O.bitwise_and)
        cp(A("zu", 0, 16), A("zi2", 0, 16))

        def probe(m0, m1):
            tt(A("ne", 256 * m0, 256 * m1), ind(A("dt"), A("zu", 16 * m0, 16 * m1)), A("aa", 0, 256 * (m1 - m0)), O.not_equal)

        def steps(m0, m1):
            for m in range(m0, m1):
                tt(A("z", 16 * m, 16 * m + 16), A("zi2", 0, 16), A("sm", 16 * m, 16 * m + 16), O.add)

        def free_at(m0, m1):
            act(A("sg", 256 * m0, 256 * m1), ind(A("et"), A("zu", 16 * m0, 16 * m1)), F.Sign)

        def keys(b, m0, m1):
            out = P(b, 0, 16 * (m1 - m0))
            mm(out, A("ones", 0, 128, 1, 0, 1), A("mrow", 16 * m0, 16 * m1, 1, 0, 1), True, False)
            for j in range(m1 - m0):
                mm(P(b, 16 * j, 16 * j + 16), A("idb"), A("invw"), False, False)
            mm(out, A("idb"), A("z16", 16 * m0, 16 * m1), False, False)
            wsum(out, "es", "sg", 256 * m0, 256 * m1, False, False)

        def unequal(b, m0, m1):
            wsum(P(b, 0, 16 * (m1 - m0)), "em", "ne", 256 * m0, 256 * m1, False)

        free_at(0, 1)
        steps(1, 4)
        ts(A("zi2", 16, 64), A("z", 16, 64), 2047, O.bitwise_and)
        steps(4, 8)
        cp(A("zu", 16, 64), A("zi2", 16, 64))
        free_at(1, 4)
        ts(A("zi2", 64, 128), A("z", 64, 128), 2047, O.bitwise_and)
        probe(0, 1)
        cp(A("zu", 64, 128), A("zi2", 64, 128))
        cp(A("z16"), A("zi2"))
        free_at(4, 8)
        keys(0, 0, 4)
        probe(1, 4)
        unequal(0, 0, 4)
        act(A("ka"), P(0, 0, 64), F.Copy)
        keys(1, 4, 8)
        probe(4, 8)
        unequal(1, 4, 8)
        if last:
            whole(0, 7, 1)
        tt(A("k4"), A("ka"), P(1, 0, 64), O.min)
        tt(A("k5"), A("k4", 0, 32), A("k4", 32, 64), O.min)
        tt(A("kmi"), A("k5", 0, 16), A("k5", 16, 32), O.min)
        ts(A("plc"), A("kmi"), 2047, O.bitwise_and)
        ts(A("inv"), A("kmi"), W, O.is_ge, -4096.0, O.mult)
        ts(A("ivw"), A("kmi"), W, O.is_ge, W, O.mult)
        cp(A("key16"), A("plc"))
        cp(A("plu"), A("plc"))
        tt(A("keyw"), A("plc"), A("inv"), O.add)
        ts(A("nkey"), A("keyw"), -1.0, O.mult)
        for r in range(16):
            mm(P(2, r, 256, 16), A("bc", 128 * r, 128 * r + 128), A("key16"))
        mm(P(3, 0, 256), A("blk"), A("zb"), True, False)
        mm(P(4, 0, 16), A("idb"), A("key16"), True, False)
        mm(P(4, 0, 16), A("idb"), A("ivw"), False, False)
        if last:
            whole(1, 6, 1)
            whole(2, 0, 0)
            whole(3, 1, 0)
        act(A("eo"), ind(A("et"), A("plu")), F.Copy)
        act(A("so"), A("eo"), F.Sign)
        cp(A("kb16"), P(2, 0, 256))
        mm(P(5, 0, 256), A("idb"), A("eo"), False, False)
        mm(P(5, 0, 256), A("id128"), A("so"), False, True)
        for c in range(EQ_S, 16):
            act(A("dm", 16 * c, 256) if c == EQ_S else A("mn", 64 * c, 64 * c + 256 - 16 * c), P(2, 16 * c, 256), F.Abs, bias=A("nkey", c, c + 1))
        for c in range(EQ_S, 16):
            act(A("eq", 272 * c, 256 * c + 256), A("dm", 16 * c, 256) if c == EQ_S else A("mn", 64 * c, 64 * c + 256 - 16 * c), F.Relu, bias=1.0, scale=-1.0)
        if not last:
            act(A("ent"), P(5, 0, 256), F.Abs)
        for c in range(16):
            if c < EQ_S:
                ts(A("eq", 272 * c, 256 * c + 256), A("kb16", 16 * c, 256), A("keyw", c, c + 1), O.is_equal)
            if c < 15:
                mm(P(3, 16 * c + 16, 256), A("blk"), A("eq", 272 * c + 16, 256 * c + 256), False, c == 14)
        act(A("lsb"), P(3, 0, 256), F.Copy)
        ts(A("cn"), P(5, 0, 256), -127.0, O.max, 127.0, O.min)
        act(A("en32" if last else "en"), A("cn"), F.Identity, bias=128.0)
        if not last:
            mm(P(6, 0, 256), A("blk"), A("ent"))
            act(A("lv"), P(6, 0, 256), F.Sign)
            act(A("fr"), P(6, 0, 256), F.Relu, bias=128.0, scale=-128.0)
        for x in range(16):
            mm(P(4, 0, 16), A("eb", 128 * x, 128 * x + 128), A("eq", x, 4096, 272), False, False)
        wsum(P(4, 0, 16), "em", "lsb", 0, 256, False)
        if last:
            whole(2, 0, 1)
            whole(3, 1, 1)
        else:
            round_v(t + 1)
        tt(A("fo"), A("dumpc"), P(4, 0, 16), O.min)
        cp(A("fou"), A("fo"))
        if last:
            tt(ind(A("yb"), A("fou")), A("aa", 0, 256), A("en32"), O.add)
        else:
            tt(ind(A("et"), A("fou")), A("en"), A("lv"), O.mult)
            act(A("et", 2048, DUMMY), A("et", 0, 16), F.Copy)

    store("y", "out", T.y[:, :], A("yb", 0, 2048))
    g.wait_ge(T.sem.out, 16)
    g.wait_ge(T.sem.ldh, 16)
    g.wait_ge(T.sem.sent, RO * sum(len(es) for o, es in plan(topo, T.cores, rank)))
    for q in ("v", "s", "t", "g"):
        g.wait_ge(T.sem[SEMOF[q]], count[q])
